import numpy as np
import ml_dtypes


def mxq(x, axis, fmt="e4m3"):
    dtype, down = {"e4m3": (ml_dtypes.float8_e4m3fn, 7), "e5m2": (ml_dtypes.float8_e5m2, 14)}[fmt]
    v = np.moveaxis(np.asarray(x, np.float32).astype(ml_dtypes.bfloat16).astype(np.float64), axis, -1)
    blocks = v.reshape(v.shape[:-1] + (-1, 32))
    amax = np.abs(blocks).max(-1, keepdims=True)
    byte = np.maximum(np.where(amax > 0, np.frexp(amax)[1] - 1 + 127, 0) - down, 1)
    scale = np.exp2(byte - 127.0)
    codes = (blocks / scale).astype(np.float32).astype(dtype).astype(np.float64)
    return np.moveaxis((codes * scale).reshape(v.shape), -1, axis)


WIDE = False


def mx_kscale(k):
    if not WIDE:
        return np.ones(k)
    levels = np.array([10, -10, 5, -5, 0])
    if k % 512:
        return np.exp2(np.random.permutation(np.resize(levels, k // 32))).repeat(32)
    a = np.empty((k // 512, 16))
    for p in range(k // 512):
        a[p, :8] = np.random.permutation(np.resize(levels, 8))
        for g in range(8):
            far = levels[np.abs(levels - a[p, g]) >= 10]
            a[p, g + 8] = far[np.random.randint(len(far))]
    return np.exp2(a.ravel()).repeat(32)


BF16 = ml_dtypes.bfloat16


def bf(x):
    return np.asarray(x, np.float32).astype(BF16)


def f64(x):
    return np.asarray(x).astype(np.float64)


E2M1 = np.array([0.0, 0.5, 1.0, 1.5, 2.0, 3.0, 4.0, 6.0, -0.0, -0.5, -1.0, -1.5, -2.0, -3.0, -4.0, -6.0])


def pack_weight(w, fmt):
    k, n = w.shape
    w = f64(bf(w)).reshape(k // 32, 32, n)
    amax = np.abs(w).max(1)
    if fmt == "e4m3":
        byte = np.frexp(amax)[1] - 1 + 127 - 7
    else:
        mant, ex = np.frexp(amax / 6.0)
        byte = np.where(mant > 0.5, ex, ex - 1) + 127
    byte = np.clip(np.where(amax > 0, byte, 1), 1, 254)
    scaled = (w * np.exp2(127.0 - byte)[:, None, :]).reshape(k, n).astype(np.float32)
    by_word = np.ascontiguousarray(scaled.reshape(k // 512, 128, 4, n).transpose(0, 1, 3, 2))
    if fmt == "e4m3":
        words = by_word.astype(ml_dtypes.float8_e4m3fn).view(np.uint8)
    else:
        c = by_word.astype(ml_dtypes.float4_e2m1fn).view(np.uint8) & 0xF
        words = c[..., 0::2] | (c[..., 1::2] << 4)
    return np.ascontiguousarray(words), np.ascontiguousarray(byte.astype(np.uint8).reshape(k // 512, 16, n))


def unpack_weight(words, scales, fmt):
    g, p, n, _ = words.shape
    if fmt == "e4m3":
        vals = np.ascontiguousarray(words).view(ml_dtypes.float8_e4m3fn).astype(np.float64)
    else:
        nib = np.empty((g, p, n, 4), np.uint8)
        nib[..., 0::2] = words & 0xF
        nib[..., 1::2] = words >> 4
        vals = E2M1[nib]
    vals = vals * np.repeat(np.exp2(scales.astype(np.float64) - 127.0), 8, axis=1)[..., None]
    return vals.transpose(0, 1, 3, 2).reshape(g * 512, n)
def pack4(w):
    words, scales = pack_weight(w, "e2m1")
    return words.reshape(words.shape[0], 128, -1), scales


def unpack4(words, scales):
    return unpack_weight(words.reshape(words.shape[0], 128, -1, 2), scales, "e2m1")


M, KO, KR, D, V = 512, 512, 1024, 1536, 2048
Z_STD = 0.6
Y_STD = 0.7


def draw0():
    so, sr = mx_kscale(KO), mx_kscale(KR)
    t = mx_kscale(V)
    h_out = 3.0 * np.random.standard_normal((M, KO)) * so
    w_out = np.random.standard_normal((KO, V)) * Z_STD / (3.0 * np.sqrt(KO)) / so[:, None]
    h_rest = np.random.standard_normal((M, KR)) * sr
    w_rest = np.random.standard_normal((KR, V)) * Z_STD / np.sqrt(KR) / sr[:, None]
    w_rest_words, w_rest_scales = pack4(w_rest)
    wt = np.random.standard_normal((V, D)) / np.sqrt(V) / t[:, None]
    wt_words, wt_scales = pack4(wt)
    log_norm = Z_STD ** 2 + 0.2 * np.random.standard_normal(M)
    targets = np.exp(Y_STD * np.random.standard_normal((M, V)) - Y_STD ** 2 / 2)
    vocab_scale = (1 + 0.1 * np.random.standard_normal(V)) * t
    return {"h_out": bf(h_out), "h_rest": bf(h_rest), "w_out": bf(w_out),
            "w_rest_words": w_rest_words, "w_rest_scales": w_rest_scales,
            "log_norm": bf(log_norm), "targets": bf(targets), "vocab_scale": bf(vocab_scale),
            "wt_words": wt_words, "wt_scales": wt_scales}


def core(h_out, h_rest, w_out, w_rest_words, w_rest_scales, log_norm, targets, vocab_scale, wt_words, wt_scales):
    z = ((mxq(f64(h_out), 1, "e4m3") @ mxq(f64(w_out), 0, "e4m3"))
         + (mxq(f64(h_rest), 1, "e4m3") @ unpack4(w_rest_words, w_rest_scales)))
    e = (np.exp(z - f64(log_norm)[:, None]) - f64(targets)) * f64(vocab_scale)
    return mxq(e, 1, "e4m3") @ unpack4(wt_words, wt_scales)


def e4m3fn_bytes(y):
    return np.clip(np.asarray(y, np.float64), -448.0, 448.0).astype(np.float32).astype(ml_dtypes.float8_e4m3fn).view(np.uint8)


def e4m3fn_values(b):
    return np.asarray(b, np.uint8).view(ml_dtypes.float8_e4m3fn).astype(np.float64)


def setup_inputs():
    d = draw0()
    x0 = np.asarray(d['w_out']).astype(np.float64)
    s = (np.max(np.abs(x0), axis=(1,), keepdims=True) / 448.0).astype(np.float32)
    out = {}
    for k, v in d.items():
        if k == 'w_out':
            out['w_out_bytes'] = e4m3fn_bytes(x0 / s.astype(np.float64))
            out['w_out_scale'] = s
        else:
            out[k] = v
    return out


def reference(h_out, h_rest, w_out_bytes, w_out_scale, w_rest_words, w_rest_scales, log_norm, targets, vocab_scale, wt_words, wt_scales):
    return core(h_out, h_rest, e4m3fn_values(w_out_bytes) * w_out_scale.astype(np.float64), w_rest_words, w_rest_scales, log_norm, targets, vocab_scale, wt_words, wt_scales)

@@ -1,0 +1,404 @@
+from contextlib import ExitStack
+
+import concourse.mybir as mybir
+from concourse.masks import make_identity
+
+TOKENS, OUT_CH, REST_CH, HIDDEN, VOCAB = 512, 512, 1024, 1536, 2048
+FLOPS = 2 * TOKENS * (OUT_CH + REST_CH) * VOCAB + 2 * TOKENS * VOCAB * HIDDEN
+
+F32 = mybir.dt.float32
+BF16 = mybir.dt.bfloat16
+I32 = mybir.dt.int32
+U32 = mybir.dt.uint32
+U8 = mybir.dt.uint8
+E4M3FN = mybir.dt.float8_e4m3fn
+E4M3_X4 = mybir.dt.float8_e4m3fn_x4
+E2M1_X4 = mybir.dt.float4_e2m1fn_x4
+MULT = mybir.AluOpType.mult
+SUBTRACT = mybir.AluOpType.subtract
+EXP = mybir.ActivationFunctionType.Exp
+COPY = mybir.ActivationFunctionType.Copy
+
+P = 128
+N = 512
+M_TILES = TOKENS // P
+V_GROUPS = VOCAB // N
+D_GROUPS = HIDDEN // N
+VS_ROWS = VOCAB // P
+BANK_ROWS = VS_ROWS // 2
+
+
+def tile_cross_entropy_hidden_gradient_s3_kernel(
+    tc, h_out, h_rest, w_out_bytes, w_out_scale, w_rest_words, w_rest_scales,
+    log_norm, targets, vocab_scale, wt_words, wt_scales, out
+):
+    nc = tc.nc
+    with ExitStack() as ctx:
+        keep = ctx.enter_context(tc.tile_pool(name="keep", bufs=1))
+        e_pool = ctx.enter_context(tc.tile_pool(name="e_pool", bufs=3))
+        diff_pool = ctx.enter_context(tc.tile_pool(name="diff_pool", bufs=2))
+        store_pool = ctx.enter_context(tc.tile_pool(name="store_pool", bufs=6))
+        z_psum = ctx.enter_context(tc.psum_pool(name="z_psum", bufs=3))
+        t_psum = ctx.enter_context(tc.psum_pool(name="t_psum", bufs=3))
+        o_psum = ctx.enter_context(tc.psum_pool(name="o_psum", bufs=2))
+        ctx.enter_context(tc.manual_schedule())
+
+        def kept(shape, dtype, name):
+            return keep.tile(shape, dtype, name=name, align_bytes=256)
+
+        def rows(m):
+            return slice(m * P, (m + 1) * P)
+
+        def cols(g):
+            return slice(g * N, (g + 1) * N)
+
+        wr_scale = kept([P, 2, VOCAB], U8, "wr_scale")
+        wt_scale = kept([P, V_GROUPS, HIDDEN], U8, "wt_scale")
+        vectors = kept([P, P], BF16, "vectors")
+        table = kept([P, 1], F32, "table")
+        ident = kept([P, P], F32, "ident")
+        ident_bf = kept([P, P], BF16, "ident_bf")
+        make_identity(nc, ident[:])
+        nc.vector.memset(table[:], 0.0)
+        nc.scalar.activation(out=table[:], in_=table[:], func=EXP)
+        nc.vector.memset(vectors[:], 0.0)
+        nc.vector.memset(wr_scale[:].bitcast(I32), 0)
+        nc.vector.memset(wt_scale[:].bitcast(I32), 0)
+        nc.vector.tensor_copy(out=ident_bf[:], in_=ident[:])
+
+        w_scale = kept([P, 4], F32, "w_scale")
+        bytes0 = kept([P, 4, N], U8, "bytes0")
+        bytes1 = kept([P, 4, N], U8, "bytes1")
+        bytes23 = kept([P, 4, 2 * N], U8, "bytes23")
+        w_bytes = [bytes0[:], bytes1[:], bytes23[:, :, 0:N], bytes23[:, :, N:2 * N]]
+        wr = [kept([P, 2, VOCAB], U8, "wr%d" % i) for i in range(2)]
+        rest0 = kept([P, REST_CH], BF16, "rest0")
+        rest1 = kept([P, REST_CH], BF16, "rest1")
+        rest23 = kept([P, 2, REST_CH], BF16, "rest23")
+        rest = [rest0[:], rest1[:], rest23[:, 0, :], rest23[:, 1, :]]
+        outlier = [kept([P, 2, OUT_CH], BF16, "outlier%d" % i) for i in range(2)]
+        target = [kept([P, VOCAB], BF16, "target%d" % m) for m in range(M_TILES)]
+        wt = [kept([P, 2, 2 * HIDDEN], U8, "wt%d" % i) for i in range(2)]
+
+        w_view = w_out_bytes.rearrange("(p t) v -> p t v", t=4)
+        wr_view = w_rest_words.rearrange("g p n -> p g n")
+        wt_view = wt_words.rearrange("g p n -> p g n")
+        outlier_view = h_out.rearrange("(m p) k -> p m k", p=P)
+
+        def load(tile, source):
+            nc.sync.dma_start(out=tile, in_=source)
+
+        def load_scales(plane, source):
+            for q in range(4):
+                load(plane[32 * q:32 * q + 4].bitcast(I32),
+                     source[:, 4 * q:4 * q + 4, :].bitcast(I32).rearrange("g r n -> r g n"))
+
+        load(w_scale[:], w_out_scale.rearrange("(p t) o -> p (t o)", t=4))
+        load(bytes0[:], w_view[:, :, 0:N])
+        load(rest0[:], h_rest[rows(0), :])
+        load(bytes1[:], w_view[:, :, N:2 * N])
+        load(vectors[0:VS_ROWS, :], vocab_scale.rearrange("(r c) -> r c", c=P))
+        load(vectors[VS_ROWS:VS_ROWS + M_TILES, :], log_norm.rearrange("(r c) -> r c", c=P))
+        load(outlier[0][:], outlier_view[:, 0:2, :])
+        load(rest1[:], h_rest[rows(1), :])
+        load_scales(wr_scale, w_rest_scales)
+        load(wr[0][:], wr_view[:, :, 0:VOCAB])
+        load(bytes23[:], w_view[:, :, 2 * N:4 * N])
+        load(rest23[:], h_rest.rearrange("(m p) k -> p m k", p=P)[:, 2:4, :])
+        load(outlier[1][:], outlier_view[:, 2:4, :])
+        load(wr[1][:], wr_view[:, :, VOCAB:2 * VOCAB])
+        load(target[0][:], targets[rows(0), :])
+        load(target[1][:], targets[rows(1), :])
+        for i in range(2):
+            load(wt[i][:], wt_view[:, 2 * i:2 * i + 2, :])
+        load_scales(wt_scale, wt_scales)
+        load(target[2][:], targets[rows(2), :])
+        load(target[3][:], targets[rows(3), :])
+
+        wide = [kept([P, 4, N], BF16, "wide%d" % g) for g in range(V_GROUPS)]
+        w_grouped = [kept([P, N, 4], BF16, "w_grouped%d" % g) for g in range(V_GROUPS)]
+        w_codes = [kept([P, N], U32, "w_codes%d" % g) for g in range(V_GROUPS)]
+        w_codes_scale = [kept([P, N], U8, "w_codes_scale%d" % g) for g in range(V_GROUPS)]
+
+        def widen(g):
+            for t in range(4):
+                source = w_bytes[g][:, t, :].bitcast(E4M3FN)
+                if t % 2 == 0:
+                    nc.vector.tensor_scalar(out=wide[g][:, t, :], in0=source, scalar1=w_scale[:, t:t + 1],
+                                            scalar2=None, op0=MULT)
+                else:
+                    nc.scalar.activation(out=wide[g][:, t, :], in_=source, func=COPY, scale=w_scale[:, t:t + 1])
+
+        def interleave(g):
+            nc.vector.tensor_copy(out=w_grouped[g][:].rearrange("p (c i) t -> p c t i", i=4),
+                                  in_=wide[g][:].rearrange("p t (c i) -> p c t i", i=4))
+
+        def quantise_w(g):
+            nc.vector.quantize_mx(out=w_codes[g][:].bitcast(E4M3_X4), scales=w_codes_scale[g][:],
+                                  in_=w_grouped[g][:].rearrange("p v t -> p (v t)"))
+
+        h_blocks = {}
+        for m in range(M_TILES):
+            h_blocks["rest", m] = [rest[m][:, cols(j)] for j in range(2)]
+        for i in range(2):
+            h_blocks["outlier", i] = [outlier[i][:, j, :] for j in range(2)]
+        h_grouped, h_codes, h_scale, h_bank = {}, {}, {}, {}
+        for kind, i in h_blocks:
+            h_grouped[kind, i] = kept([P, 2, P, 4], BF16, "h_grouped_%s%d" % (kind, i))
+            h_codes[kind, i] = kept([P, 2, P], U32, "h_codes_%s%d" % (kind, i))
+            h_scale[kind, i] = kept([P, 2, P], U8, "h_scale_%s%d" % (kind, i))
+
+        def transpose_h(pair):
+            bank = t_psum.tile([P, 4, P], F32, name="t_bank", tag="t")
+            h_bank[pair] = bank
+            for j in range(2):
+                for u in range(2):
+                    nc.tensor.transpose(bank[:, 2 * j + u, :], h_blocks[pair][j].bitcast(F32)[:, u:N // 2:2], ident[:])
+
+        def copy_h(pair):
+            nc.scalar.copy(out=h_grouped[pair][:].bitcast(F32),
+                           in_=h_bank[pair][:].rearrange("p (j u) r -> p j r u", u=2))
+
+        def quantise_h(pair):
+            nc.vector.quantize_mx(out=h_codes[pair][:].rearrange("p j r -> p (j r)").bitcast(E4M3_X4),
+                                  scales=h_scale[pair][:].rearrange("p j r -> p (j r)"),
+                                  in_=h_grouped[pair][:].rearrange("p j r t -> p (j r t)"))
+
+        minus_log_norm = kept([P, M_TILES], F32, "minus_log_norm")
+        vs = kept([P, VOCAB], BF16, "vs")
+        vs_bank = {}
+
+        def turn_log_norm():
+            bank = t_psum.tile([P, P], BF16, name="log_norm_bank", tag="t")
+            nc.tensor.transpose(bank[:], vectors[:], ident_bf[:])
+            nc.vector.tensor_scalar(out=minus_log_norm[:], in0=bank[:, VS_ROWS:VS_ROWS + M_TILES],
+                                    scalar1=-1.0, scalar2=None, op0=MULT)
+
+        def spread_vs(i):
+            bank = o_psum.tile([P, BANK_ROWS * P], BF16, name="vs_bank", tag="o")
+            vs_bank[i] = bank
+            for r in range(BANK_ROWS):
+                row = i * BANK_ROWS + r
+                nc.tensor.matmul(bank[:, rows(r)], lhsT=ident_bf[:, row:row + 1].to_broadcast([P, P]), rhs=vectors[:],
+                                 start=True, stop=True)
+
+        def copy_vs(g):
+            nc.scalar.copy(out=vs[:, cols(g)].rearrange("q (u w e) -> q u w e", u=2, e=2),
+                           in_=vs_bank[g // 2][:, cols(g % 2)].rearrange("q (w u e) -> q u w e", u=2, e=2))
+
+        z_bank, e_tile, diff_tile, grad_tile = {}, {}, {}, {}
+
+        def logits(m, g):
+            bank = z_psum.tile([P, N], F32, name="z_bank", tag="z")
+            z_bank[m, g] = bank
+            words = slice((g % 2) * 2 * N, (g % 2 + 1) * 2 * N)
+            for j in range(2):
+                nc.tensor.matmul_mx(
+                    out=bank[:],
+                    lhsT=h_codes["rest", m][:, j, :].bitcast(E4M3_X4), lhsT_scale=h_scale["rest", m][:, j, :],
+                    rhs=wr[g // 2][:, j, words].bitcast(E2M1_X4), rhs_scale=wr_scale[:, j, cols(g)],
+                    start=(j == 0), stop=False)
+            pair = ("outlier", m // 2)
+            nc.tensor.matmul_mx(
+                out=bank[:],
+                lhsT=h_codes[pair][:, m % 2, :].bitcast(E4M3_X4), lhsT_scale=h_scale[pair][:, m % 2, :],
+                rhs=w_codes[g][:].bitcast(E4M3_X4), rhs_scale=w_codes_scale[g][:],
+                start=False, stop=True)
+
+        def exponential(m, g):
+            if g == 0:
+                e_m = e_pool.tile([P, VOCAB], F32, name="e_m")
+                e_tile[m] = e_m
+            nc.scalar.activation(out=e_tile[m][:, cols(g)], in_=z_bank[m, g][:], func=EXP, bias=minus_log_norm[:, m:m + 1])
+
+        def subtract(m, half):
+            if half == 0:
+                diff_m = diff_pool.tile([P, VOCAB], F32, name="diff_m")
+                diff_tile[m] = diff_m
+            two_groups = slice(half * 2 * N, (half + 1) * 2 * N)
+            nc.vector.tensor_tensor(out=diff_tile[m][:, two_groups], in0=e_tile[m][:, two_groups],
+                                    in1=target[m][:, two_groups], op=SUBTRACT)
+
+        def multiply(m, g):
+            if g == 0:
+                grad_m = diff_pool.tile([P, VOCAB], BF16, name="grad_m")
+                grad_tile[m] = grad_m
+            nc.vector.tensor_tensor(out=grad_tile[m][:, cols(g)].rearrange("q (u w e) -> q u w e", u=2, e=2),
+                                    in0=diff_tile[m][:, cols(g)].rearrange("q (w u e) -> q u w e", u=2, e=2),
+                                    in1=vs[:, cols(g)].rearrange("q (u w e) -> q u w e", u=2, e=2), op=MULT)
+
+        g_grouped = [kept([P, V_GROUPS, P, 4], BF16, "g_grouped%d" % m) for m in range(M_TILES)]
+        g_codes = [kept([P, V_GROUPS, P], U32, "g_codes%d" % m) for m in range(M_TILES)]
+        g_scale = [kept([P, V_GROUPS, P], U8, "g_scale%d" % m) for m in range(M_TILES)]
+        g_bank = {}
+
+        def transpose_e(m, half):
+            bank = t_psum.tile([P, 4, P], F32, name="t_bank", tag="t")
+            g_bank[m, half] = bank
+            words = grad_tile[m][:].bitcast(F32)
+            for j in range(4):
+                nc.tensor.transpose(bank[:, j, :], words[:, rows(4 * half + j)], ident[:])
+
+        def copy_e(m, half, copy):
+            copy(out=g_grouped[m][:, 2 * half:2 * half + 2].bitcast(F32),
+                 in_=g_bank[m, half][:].rearrange("p (g u) r -> p g r u", u=2))
+
+        def quantise_e(m, half):
+            groups = slice(2 * half, 2 * half + 2)
+            nc.vector.quantize_mx(out=g_codes[m][:, groups].rearrange("p g r -> p (g r)").bitcast(E4M3_X4),
+                                  scales=g_scale[m][:, groups].rearrange("p g r -> p (g r)"),
+                                  in_=g_grouped[m][:, groups].rearrange("p g r t -> p (g r t)"))
+
+        def quantise_e_whole(m):
+            nc.vector.quantize_mx(out=g_codes[m][:].rearrange("p g r -> p (g r)").bitcast(E4M3_X4),
+                                  scales=g_scale[m][:].rearrange("p g r -> p (g r)"),
+                                  in_=g_grouped[m][:].rearrange("p g r t -> p (g r t)"))
+
+        o_bank = {}
+
+        def product(m, first, width, passes_of):
+            bank = o_psum.tile([P, N], F32, name="o_bank", tag="o")
+            o_bank[m, first] = bank
+            for c in range(0, width, passes_of):
+                v0 = first + c
+                for g in range(V_GROUPS):
+                    nc.tensor.matmul_mx(
+                        out=bank[:, c:c + passes_of],
+                        lhsT=g_codes[m][:, g, :].bitcast(E4M3_X4), lhsT_scale=g_scale[m][:, g, :],
+                        rhs=wt[g // 2][:, g % 2, 2 * v0:2 * (v0 + passes_of)].bitcast(E2M1_X4),
+                        rhs_scale=wt_scale[:, g, v0:v0 + passes_of],
+                        start=(g == 0), stop=(g == V_GROUPS - 1))
+
+        def store(m, first, width, copy):
+            result = store_pool.tile([P, N], F32, name="result")
+            copy(out=result[:, 0:width], in_=o_bank[m, first][:, 0:width])
+            nc.sync.dma_start(out=out[rows(m), first:first + width], in_=result[:, 0:width])
+
+        scalar_copy, vector_copy = nc.scalar.copy, nc.vector.tensor_copy
+
+        def out_group(m, d, copy=scalar_copy):
+            product(m, d * N, N, N)
+            store(m, d * N, N, copy)
+
+        widen(0)
+        transpose_h(("rest", 0))
+        widen(1)
+        copy_h(("rest", 0))
+        turn_log_norm()
+        interleave(0)
+        quantise_h(("rest", 0))
+        transpose_h(("outlier", 0))
+        copy_h(("outlier", 0))
+        transpose_h(("rest", 1))
+        spread_vs(0)
+        spread_vs(1)
+        interleave(1)
+        copy_h(("rest", 1))
+        quantise_h(("outlier", 0))
+        quantise_w(0)
+        quantise_h(("rest", 1))
+        quantise_w(1)
+        copy_vs(0)
+        copy_vs(1)
+
+        logits(0, 0)
+        widen(2)
+        logits(1, 0)
+        exponential(0, 0)
+        logits(0, 1)
+        widen(3)
+        exponential(1, 0)
+        exponential(0, 1)
+        logits(1, 1)
+        interleave(2)
+        interleave(3)
+        transpose_h(("rest", 2))
+        copy_h(("rest", 2))
+        exponential(1, 1)
+        transpose_h(("outlier", 1))
+        copy_h(("outlier", 1))
+        transpose_h(("rest", 3))
+        copy_h(("rest", 3))
+        quantise_w(2)
+        subtract(0, 0)
+        quantise_w(3)
+        quantise_h(("rest", 2))
+        multiply(0, 0)
+        multiply(0, 1)
+        quantise_h(("outlier", 1))
+        quantise_h(("rest", 3))
+
+        for g in range(2, 4):
+            for m in range(2):
+                logits(m, g)
+                exponential(m, g)
+        copy_vs(2)
+        copy_vs(3)
+        subtract(0, 1)
+        multiply(0, 2)
+        multiply(0, 3)
+        for g in range(3):
+            logits(2, g)
+            exponential(2, g)
+        for half in range(2):
+            transpose_e(0, half)
+        for half in range(2):
+            copy_e(0, half, scalar_copy)
+        logits(2, 3)
+        exponential(2, 3)
+
+        subtract(1, 0)
+        subtract(1, 1)
+        multiply(1, 0)
+        quantise_e_whole(0)
+        for g in range(1, 4):
+            multiply(1, g)
+        for g in range(3):
+            logits(3, g)
+            exponential(3, g)
+        out_group(0, 0)
+        subtract(2, 0)
+        for half in range(2):
+            transpose_e(1, half)
+        for half in range(2):
+            copy_e(1, half, scalar_copy)
+        out_group(0, 1)
+        subtract(2, 1)
+        logits(3, 3)
+        exponential(3, 3)
+        quantise_e_whole(1)
+        out_group(0, 2)
+
+        for g in range(4):
+            multiply(2, g)
+        subtract(3, 0)
+        out_group(1, 0)
+        for half in range(2):
+            transpose_e(2, half)
+        for half in range(2):
+            copy_e(2, half, scalar_copy)
+        subtract(3, 1)
+        out_group(1, 1)
+        quantise_e_whole(2)
+        out_group(1, 2)
+
+        for g in range(4):
+            multiply(3, g)
+        out_group(2, 0)
+        product(2, N, N, N)
+        for half in range(2):
+            transpose_e(3, half)
+        copy_e(3, 0, vector_copy)
+        copy_e(3, 1, scalar_copy)
+        store(2, N, N, scalar_copy)
+        product(2, 2 * N, N, N)
+        quantise_e(3, 0)
+        quantise_e(3, 1)
+        store(2, 2 * N, N, vector_copy)
+
+        out_group(3, 0)
+        out_group(3, 1)
+        product(3, 2 * N, 3 * P, P)
+        store(3, 2 * N, 3 * P, scalar_copy)
+        product(3, 2 * N + 3 * P, P, P)
+        store(3, 2 * N + 3 * P, P, vector_copy)

@@ -35,12 +35,11 @@ def tile_cross_entropy_hidden_gradient_s3_kernel(
     nc = tc.nc
     with ExitStack() as ctx:
         keep = ctx.enter_context(tc.tile_pool(name="keep", bufs=1))
-        e_pool = ctx.enter_context(tc.tile_pool(name="e_pool", bufs=3))
-        diff_pool = ctx.enter_context(tc.tile_pool(name="diff_pool", bufs=2))
+        wide_pool = ctx.enter_context(tc.tile_pool(name="wide_pool", bufs=2))
+        grad_pool = ctx.enter_context(tc.tile_pool(name="grad_pool", bufs=2))
         store_pool = ctx.enter_context(tc.tile_pool(name="store_pool", bufs=6))
-        z_psum = ctx.enter_context(tc.psum_pool(name="z_psum", bufs=3))
+        sum_psum = ctx.enter_context(tc.psum_pool(name="sum_psum", bufs=5))
         t_psum = ctx.enter_context(tc.psum_pool(name="t_psum", bufs=3))
-        o_psum = ctx.enter_context(tc.psum_pool(name="o_psum", bufs=2))
         ctx.enter_context(tc.manual_schedule())
 
         def kept(shape, dtype, name):
@@ -49,41 +48,38 @@ def tile_cross_entropy_hidden_gradient_s3_kernel(
         def rows(m):
             return slice(m * P, (m + 1) * P)
 
-        def cols(g):
-            return slice(g * N, (g + 1) * N)
+        def cols(g, count=1):
+            return slice(g * N, (g + count) * N)
 
-        wr_scale = kept([P, 2, VOCAB], U8, "wr_scale")
+        wr_scale = [kept([P, 2, 2 * N], U8, "wr_scale%d" % i) for i in range(2)]
         wt_scale = kept([P, V_GROUPS, HIDDEN], U8, "wt_scale")
-        vectors = kept([P, P], BF16, "vectors")
+        vs_rows = kept([P, P], BF16, "vs_rows")
         table = kept([P, 1], F32, "table")
         ident = kept([P, P], F32, "ident")
         ident_bf = kept([P, P], BF16, "ident_bf")
+        nc.gpsimd.memset(vs_rows[:], 0.0)
         make_identity(nc, ident[:])
         nc.vector.memset(table[:], 0.0)
         nc.scalar.activation(out=table[:], in_=table[:], func=EXP)
-        nc.vector.memset(vectors[:], 0.0)
-        nc.vector.memset(wr_scale[:].bitcast(I32), 0)
-        nc.vector.memset(wt_scale[:].bitcast(I32), 0)
+        for plane in wr_scale + [wt_scale]:
+            nc.vector.memset(plane[:].bitcast(I32), 0)
         nc.vector.tensor_copy(out=ident_bf[:], in_=ident[:])
 
+        norm = kept([P, M_TILES], BF16, "norm")
         w_scale = kept([P, 4], F32, "w_scale")
-        bytes0 = kept([P, 4, N], U8, "bytes0")
-        bytes1 = kept([P, 4, N], U8, "bytes1")
-        bytes23 = kept([P, 4, 2 * N], U8, "bytes23")
-        w_bytes = [bytes0[:], bytes1[:], bytes23[:, :, 0:N], bytes23[:, :, N:2 * N]]
-        wr = [kept([P, 2, VOCAB], U8, "wr%d" % i) for i in range(2)]
-        rest0 = kept([P, REST_CH], BF16, "rest0")
-        rest1 = kept([P, REST_CH], BF16, "rest1")
-        rest23 = kept([P, 2, REST_CH], BF16, "rest23")
-        rest = [rest0[:], rest1[:], rest23[:, 0, :], rest23[:, 1, :]]
-        outlier = [kept([P, 2, OUT_CH], BF16, "outlier%d" % i) for i in range(2)]
-        target = [kept([P, VOCAB], BF16, "target%d" % m) for m in range(M_TILES)]
-        wt = [kept([P, 2, 2 * HIDDEN], U8, "wt%d" % i) for i in range(2)]
+        w_bytes = [kept([P, 4, N], U8, "w_bytes%d" % g) for g in range(V_GROUPS)]
+        wr = [kept([P, 2, 2 * N], U8, "wr%d" % g) for g in range(V_GROUPS)]
+        rest = [kept([P, REST_CH], BF16, "rest%d" % m) for m in range(M_TILES)]
+        outlier = [kept([P, 2 * OUT_CH], BF16, "outlier%d" % i) for i in range(2)]
+        target = [[kept([P, 2 * N], BF16, "target%d_%d" % (m, half)) for half in range(2)] for m in range(M_TILES)]
+        wt = [kept([P, 2 * HIDDEN], U8, "wt%d" % g) for g in range(V_GROUPS)]
 
         w_view = w_out_bytes.rearrange("(p t) v -> p t v", t=4)
         wr_view = w_rest_words.rearrange("g p n -> p g n")
-        wt_view = wt_words.rearrange("g p n -> p g n")
-        outlier_view = h_out.rearrange("(m p) k -> p m k", p=P)
+        rest_view = h_rest.rearrange("(p m) k -> p m k", m=M_TILES)
+        outlier_view = h_out.rearrange("(p i m) k -> p i (m k)", i=2, m=2)
+        target_view = targets.rearrange("(p m) v -> p m v", m=M_TILES)
+        out_view = out.rearrange("(p m) d -> p m d", m=M_TILES)
 
         def load(tile, source):
             nc.sync.dma_start(out=tile, in_=source)
@@ -93,43 +89,78 @@ def tile_cross_entropy_hidden_gradient_s3_kernel(
                 load(plane[32 * q:32 * q + 4].bitcast(I32),
                      source[:, 4 * q:4 * q + 4, :].bitcast(I32).rearrange("g r n -> r g n"))
 
-        load(w_scale[:], w_out_scale.rearrange("(p t) o -> p (t o)", t=4))
-        load(bytes0[:], w_view[:, :, 0:N])
-        load(rest0[:], h_rest[rows(0), :])
-        load(bytes1[:], w_view[:, :, N:2 * N])
-        load(vectors[0:VS_ROWS, :], vocab_scale.rearrange("(r c) -> r c", c=P))
-        load(vectors[VS_ROWS:VS_ROWS + M_TILES, :], log_norm.rearrange("(r c) -> r c", c=P))
-        load(outlier[0][:], outlier_view[:, 0:2, :])
-        load(rest1[:], h_rest[rows(1), :])
-        load_scales(wr_scale, w_rest_scales)
-        load(wr[0][:], wr_view[:, :, 0:VOCAB])
-        load(bytes23[:], w_view[:, :, 2 * N:4 * N])
-        load(rest23[:], h_rest.rearrange("(m p) k -> p m k", p=P)[:, 2:4, :])
-        load(outlier[1][:], outlier_view[:, 2:4, :])
-        load(wr[1][:], wr_view[:, :, VOCAB:2 * VOCAB])
-        load(target[0][:], targets[rows(0), :])
-        load(target[1][:], targets[rows(1), :])
-        for i in range(2):
-            load(wt[i][:], wt_view[:, 2 * i:2 * i + 2, :])
-        load_scales(wt_scale, wt_scales)
-        load(target[2][:], targets[rows(2), :])
-        load(target[3][:], targets[rows(3), :])
+        def load_bytes(g):
+            load(w_bytes[g][:], w_view[:, :, cols(g)])
 
-        wide = [kept([P, 4, N], BF16, "wide%d" % g) for g in range(V_GROUPS)]
-        w_grouped = [kept([P, N, 4], BF16, "w_grouped%d" % g) for g in range(V_GROUPS)]
+        def load_wr(g):
+            load(wr[g][:], wr_view[:, :, cols(2 * g, 2)])
+
+        def load_wr_scales(i):
+            load_scales(wr_scale[i], w_rest_scales[:, :, cols(2 * i, 2)])
+
+        def load_rest(m):
+            load(rest[m][:], rest_view[:, m, :])
+
+        def load_outlier(i):
+            load(outlier[i][:], outlier_view[:, i, :])
+
+        def load_target(m, half):
+            load(target[m][half][:], target_view[:, m, cols(2 * half, 2)])
+
+        def load_wt(g):
+            load(wt[g][:], wt_words[g])
+
+        load(vs_rows[0:VS_ROWS, :], vocab_scale.rearrange("(r c) -> r c", c=P))
+        load_bytes(0)
+        load(w_scale[:], w_out_scale.rearrange("(p t) o -> p (t o)", t=4))
+        load_rest(0)
+        load_bytes(1)
+        load_wr_scales(0)
+        load_wr(0)
+        load_outlier(0)
+        load_rest(1)
+        load_wr(1)
+        load(norm[:], log_norm.rearrange("(p m) -> p m", m=M_TILES))
+        load_rest(2)
+        load_outlier(1)
+        load_bytes(2)
+        load_target(0, 0)
+        load_bytes(3)
+        load_wr_scales(1)
+        load_wr(2)
+        load_target(1, 0)
+        load_wr(3)
+        load_target(0, 1)
+        load_rest(3)
+        load_scales(wt_scale, wt_scales)
+        load_wt(0)
+        load_wt(1)
+        load_target(1, 1)
+        load_wt(2)
+        load_wt(3)
+        for m in range(2, M_TILES):
+            for half in range(2):
+                load_target(m, half)
+
+        wide, w_grouped = {}, {}
         w_codes = [kept([P, N], U32, "w_codes%d" % g) for g in range(V_GROUPS)]
         w_codes_scale = [kept([P, N], U8, "w_codes_scale%d" % g) for g in range(V_GROUPS)]
 
-        def widen(g):
-            for t in range(4):
-                source = w_bytes[g][:, t, :].bitcast(E4M3FN)
-                if t % 2 == 0:
-                    nc.vector.tensor_scalar(out=wide[g][:, t, :], in0=source, scalar1=w_scale[:, t:t + 1],
-                                            scalar2=None, op0=MULT)
-                else:
-                    nc.scalar.activation(out=wide[g][:, t, :], in_=source, func=COPY, scale=w_scale[:, t:t + 1])
+        def wide_tile(g):
+            if g not in wide:
+                wide[g] = wide_pool.tile([P, 4, N], BF16, name="wide", align_bytes=256)
+            return wide[g]
+
+        def widen_vector(g, t):
+            nc.vector.tensor_scalar(out=wide_tile(g)[:, t, :], in0=w_bytes[g][:, t, :].bitcast(E4M3FN),
+                                    scalar1=w_scale[:, t:t + 1], scalar2=None, op0=MULT)
+
+        def widen_scalar(g, t):
+            nc.scalar.activation(out=wide_tile(g)[:, t, :], in_=w_bytes[g][:, t, :].bitcast(E4M3FN), func=COPY,
+                                 scale=w_scale[:, t:t + 1])
 
         def interleave(g):
+            w_grouped[g] = wide_pool.tile([P, N, 4], BF16, name="w_grouped", align_bytes=256)
             nc.vector.tensor_copy(out=w_grouped[g][:].rearrange("p (c i) t -> p c t i", i=4),
                                   in_=wide[g][:].rearrange("p t (c i) -> p c t i", i=4))
 
@@ -137,268 +168,288 @@ def tile_cross_entropy_hidden_gradient_s3_kernel(
             nc.vector.quantize_mx(out=w_codes[g][:].bitcast(E4M3_X4), scales=w_codes_scale[g][:],
                                   in_=w_grouped[g][:].rearrange("p v t -> p (v t)"))
 
-        h_blocks = {}
+        h_source = {}
         for m in range(M_TILES):
-            h_blocks["rest", m] = [rest[m][:, cols(j)] for j in range(2)]
+            h_source["rest", m] = rest[m]
         for i in range(2):
-            h_blocks["outlier", i] = [outlier[i][:, j, :] for j in range(2)]
+            h_source["outlier", i] = outlier[i]
         h_grouped, h_codes, h_scale, h_bank = {}, {}, {}, {}
-        for kind, i in h_blocks:
+        for kind, i in h_source:
             h_grouped[kind, i] = kept([P, 2, P, 4], BF16, "h_grouped_%s%d" % (kind, i))
             h_codes[kind, i] = kept([P, 2, P], U32, "h_codes_%s%d" % (kind, i))
             h_scale[kind, i] = kept([P, 2, P], U8, "h_scale_%s%d" % (kind, i))
 
-        def transpose_h(pair):
+        def transpose_h(*pair):
             bank = t_psum.tile([P, 4, P], F32, name="t_bank", tag="t")
             h_bank[pair] = bank
+            words = h_source[pair][:].bitcast(F32)
             for j in range(2):
                 for u in range(2):
-                    nc.tensor.transpose(bank[:, 2 * j + u, :], h_blocks[pair][j].bitcast(F32)[:, u:N // 2:2], ident[:])
+                    nc.tensor.transpose(bank[:, 2 * j + u, :], words[:, 2 * P * j + u:2 * P * (j + 1):2], ident[:])
 
-        def copy_h(pair):
-            nc.scalar.copy(out=h_grouped[pair][:].bitcast(F32),
-                           in_=h_bank[pair][:].rearrange("p (j u) r -> p j r u", u=2))
+        def copy_h(copy, *pair):
+            copy(out=h_grouped[pair][:].bitcast(F32), in_=h_bank[pair][:].rearrange("p (j u) r -> p j r u", u=2))
 
-        def quantise_h(pair):
+        def quantise_h(*pair):
             nc.vector.quantize_mx(out=h_codes[pair][:].rearrange("p j r -> p (j r)").bitcast(E4M3_X4),
                                   scales=h_scale[pair][:].rearrange("p j r -> p (j r)"),
                                   in_=h_grouped[pair][:].rearrange("p j r t -> p (j r t)"))
 
-        minus_log_norm = kept([P, M_TILES], F32, "minus_log_norm")
+        minus_norm = kept([P, M_TILES], F32, "minus_norm")
         vs = kept([P, VOCAB], BF16, "vs")
         vs_bank = {}
 
-        def turn_log_norm():
-            bank = t_psum.tile([P, P], BF16, name="log_norm_bank", tag="t")
-            nc.tensor.transpose(bank[:], vectors[:], ident_bf[:])
-            nc.vector.tensor_scalar(out=minus_log_norm[:], in0=bank[:, VS_ROWS:VS_ROWS + M_TILES],
-                                    scalar1=-1.0, scalar2=None, op0=MULT)
+        def word_order(natural):
+            return natural.rearrange("q (w u e) -> q u w e", u=2, e=2)
 
-        def spread_vs(i):
-            bank = o_psum.tile([P, BANK_ROWS * P], BF16, name="vs_bank", tag="o")
-            vs_bank[i] = bank
+        def stored(tile, g, count):
+            runs = tile[:, cols(g // 2 * 2, 2)].rearrange("q (u w e) -> q u w e", u=2, e=2)
+            return runs[:, :, g % 2 * P:(g % 2 + count) * P, :]
+
+        def negate_norm():
+            nc.vector.tensor_scalar(out=minus_norm[:], in0=norm[:], scalar1=-1.0, scalar2=None, op0=MULT)
+
+        def spread_vs(half):
+            bank = t_psum.tile([P, BANK_ROWS * P], BF16, name="vs_bank", tag="t")
+            vs_bank[half] = bank
             for r in range(BANK_ROWS):
-                row = i * BANK_ROWS + r
-                nc.tensor.matmul(bank[:, rows(r)], lhsT=ident_bf[:, row:row + 1].to_broadcast([P, P]), rhs=vectors[:],
+                row = half * BANK_ROWS + r
+                nc.tensor.matmul(bank[:, rows(r)], lhsT=ident_bf[:, row:row + 1].to_broadcast([P, P]), rhs=vs_rows[:],
                                  start=True, stop=True)
 
-        def copy_vs(g):
-            nc.scalar.copy(out=vs[:, cols(g)].rearrange("q (u w e) -> q u w e", u=2, e=2),
-                           in_=vs_bank[g // 2][:, cols(g % 2)].rearrange("q (w u e) -> q u w e", u=2, e=2))
+        def copy_vs(half):
+            nc.scalar.copy(out=vs[:, cols(2 * half, 2)].bitcast(F32).rearrange("q (u w) -> q u w", u=2),
+                           in_=vs_bank[half][:].bitcast(F32).rearrange("q (w u) -> q u w", u=2))
 
-        z_bank, e_tile, diff_tile, grad_tile = {}, {}, {}, {}
+        z_bank, grad = {}, {}
+        e_tile = [kept([P, VOCAB], F32, "e%d" % m) for m in range(M_TILES)]
 
-        def logits(m, g):
-            bank = z_psum.tile([P, N], F32, name="z_bank", tag="z")
+        def logits_rest(m, g):
+            bank = sum_psum.tile([P, N], F32, name="z_bank", tag="sum")
             z_bank[m, g] = bank
-            words = slice((g % 2) * 2 * N, (g % 2 + 1) * 2 * N)
             for j in range(2):
                 nc.tensor.matmul_mx(
                     out=bank[:],
                     lhsT=h_codes["rest", m][:, j, :].bitcast(E4M3_X4), lhsT_scale=h_scale["rest", m][:, j, :],
-                    rhs=wr[g // 2][:, j, words].bitcast(E2M1_X4), rhs_scale=wr_scale[:, j, cols(g)],
+                    rhs=wr[g][:, j, :].bitcast(E2M1_X4), rhs_scale=wr_scale[g // 2][:, j, cols(g % 2)],
                     start=(j == 0), stop=False)
+
+        def logits_outlier(m, g):
             pair = ("outlier", m // 2)
             nc.tensor.matmul_mx(
-                out=bank[:],
+                out=z_bank[m, g][:],
                 lhsT=h_codes[pair][:, m % 2, :].bitcast(E4M3_X4), lhsT_scale=h_scale[pair][:, m % 2, :],
                 rhs=w_codes[g][:].bitcast(E4M3_X4), rhs_scale=w_codes_scale[g][:],
                 start=False, stop=True)
 
+        def logits(m, g):
+            logits_rest(m, g)
+            logits_outlier(m, g)
+
         def exponential(m, g):
-            if g == 0:
-                e_m = e_pool.tile([P, VOCAB], F32, name="e_m")
-                e_tile[m] = e_m
-            nc.scalar.activation(out=e_tile[m][:, cols(g)], in_=z_bank[m, g][:], func=EXP, bias=minus_log_norm[:, m:m + 1])
+            nc.scalar.activation(out=stored(e_tile[m], g, 1), in_=word_order(z_bank[m, g][:]), func=EXP,
+                                 bias=minus_norm[:, m:m + 1])
 
-        def subtract(m, half):
-            if half == 0:
-                diff_m = diff_pool.tile([P, VOCAB], F32, name="diff_m")
-                diff_tile[m] = diff_m
-            two_groups = slice(half * 2 * N, (half + 1) * 2 * N)
-            nc.vector.tensor_tensor(out=diff_tile[m][:, two_groups], in0=e_tile[m][:, two_groups],
-                                    in1=target[m][:, two_groups], op=SUBTRACT)
+        def subtract(m, g, count=1):
+            e = stored(e_tile[m], g, count)
+            nc.vector.tensor_tensor(out=e, in0=e, in1=word_order(target[m][g // 2][:, cols(g % 2, count)]), op=SUBTRACT)
 
-        def multiply(m, g):
-            if g == 0:
-                grad_m = diff_pool.tile([P, VOCAB], BF16, name="grad_m")
-                grad_tile[m] = grad_m
-            nc.vector.tensor_tensor(out=grad_tile[m][:, cols(g)].rearrange("q (u w e) -> q u w e", u=2, e=2),
-                                    in0=diff_tile[m][:, cols(g)].rearrange("q (w u e) -> q u w e", u=2, e=2),
-                                    in1=vs[:, cols(g)].rearrange("q (u w e) -> q u w e", u=2, e=2), op=MULT)
+        def multiply(m, g, count=1):
+            if m not in grad:
+                grad[m] = grad_pool.tile([P, VOCAB], BF16, name="grad", align_bytes=256)
+            nc.vector.tensor_tensor(out=stored(grad[m], g, count), in0=stored(e_tile[m], g, count),
+                                    in1=stored(vs, g, count), op=MULT)
 
-        g_grouped = [kept([P, V_GROUPS, P, 4], BF16, "g_grouped%d" % m) for m in range(M_TILES)]
+        g_grouped = {}
         g_codes = [kept([P, V_GROUPS, P], U32, "g_codes%d" % m) for m in range(M_TILES)]
         g_scale = [kept([P, V_GROUPS, P], U8, "g_scale%d" % m) for m in range(M_TILES)]
         g_bank = {}
 
-        def transpose_e(m, half):
+        def transpose_e(m, g, count=2):
             bank = t_psum.tile([P, 4, P], F32, name="t_bank", tag="t")
-            g_bank[m, half] = bank
-            words = grad_tile[m][:].bitcast(F32)
-            for j in range(4):
-                nc.tensor.transpose(bank[:, j, :], words[:, rows(4 * half + j)], ident[:])
+            g_bank[m, g] = bank
+            words = grad[m][:].bitcast(F32)
+            for j in range(count):
+                for u in range(2):
+                    run = (g + j) // 2 * 4 + 2 * u + (g + j) % 2
+                    nc.tensor.transpose(bank[:, 2 * j + u, :], words[:, rows(run)], ident[:])
 
-        def copy_e(m, half, copy):
-            copy(out=g_grouped[m][:, 2 * half:2 * half + 2].bitcast(F32),
-                 in_=g_bank[m, half][:].rearrange("p (g u) r -> p g r u", u=2))
+        def copy_e(copy, m, g, count=2):
+            if m not in g_grouped:
+                g_grouped[m] = grad_pool.tile([P, V_GROUPS, P, 4], BF16, name="g_grouped", align_bytes=256)
+            copy(out=g_grouped[m][:, g:g + count].bitcast(F32),
+                 in_=g_bank[m, g][:, 0:2 * count, :].rearrange("p (g u) r -> p g r u", u=2))
 
-        def quantise_e(m, half):
-            groups = slice(2 * half, 2 * half + 2)
+        def quantise_e(m, g, count):
+            groups = slice(g, g + count)
             nc.vector.quantize_mx(out=g_codes[m][:, groups].rearrange("p g r -> p (g r)").bitcast(E4M3_X4),
                                   scales=g_scale[m][:, groups].rearrange("p g r -> p (g r)"),
                                   in_=g_grouped[m][:, groups].rearrange("p g r t -> p (g r t)"))
 
-        def quantise_e_whole(m):
-            nc.vector.quantize_mx(out=g_codes[m][:].rearrange("p g r -> p (g r)").bitcast(E4M3_X4),
-                                  scales=g_scale[m][:].rearrange("p g r -> p (g r)"),
-                                  in_=g_grouped[m][:].rearrange("p g r t -> p (g r t)"))
-
         o_bank = {}
 
-        def product(m, first, width, passes_of):
-            bank = o_psum.tile([P, N], F32, name="o_bank", tag="o")
-            o_bank[m, first] = bank
-            for c in range(0, width, passes_of):
-                v0 = first + c
-                for g in range(V_GROUPS):
+        def product(m, first, width=N, step=N, groups=range(V_GROUPS)):
+            if (m, first) not in o_bank:
+                o_bank[m, first] = sum_psum.tile([P, N], F32, name="o_bank", tag="sum")
+            for c in range(0, width, step):
+                d0 = first + c
+                for g in groups:
                     nc.tensor.matmul_mx(
-                        out=bank[:, c:c + passes_of],
+                        out=o_bank[m, first][:, c:c + step],
                         lhsT=g_codes[m][:, g, :].bitcast(E4M3_X4), lhsT_scale=g_scale[m][:, g, :],
-                        rhs=wt[g // 2][:, g % 2, 2 * v0:2 * (v0 + passes_of)].bitcast(E2M1_X4),
-                        rhs_scale=wt_scale[:, g, v0:v0 + passes_of],
+                        rhs=wt[g][:, 2 * d0:2 * (d0 + step)].bitcast(E2M1_X4), rhs_scale=wt_scale[:, g, d0:d0 + step],
                         start=(g == 0), stop=(g == V_GROUPS - 1))
 
-        def store(m, first, width, copy):
+        def store(copy, m, first, width=N):
             result = store_pool.tile([P, N], F32, name="result")
             copy(out=result[:, 0:width], in_=o_bank[m, first][:, 0:width])
-            nc.sync.dma_start(out=out[rows(m), first:first + width], in_=result[:, 0:width])
+            nc.sync.dma_start(out=out_view[:, m, first:first + width], in_=result[:, 0:width])
 
-        scalar_copy, vector_copy = nc.scalar.copy, nc.vector.tensor_copy
+        scalar, vector = nc.scalar.copy, nc.vector.tensor_copy
 
-        def out_group(m, d, copy=scalar_copy):
-            product(m, d * N, N, N)
-            store(m, d * N, N, copy)
-
-        widen(0)
-        transpose_h(("rest", 0))
-        widen(1)
-        copy_h(("rest", 0))
-        turn_log_norm()
-        interleave(0)
-        quantise_h(("rest", 0))
-        transpose_h(("outlier", 0))
-        copy_h(("outlier", 0))
-        transpose_h(("rest", 1))
+        for t in range(3):
+            widen_vector(0, t)
+        widen_scalar(0, 3)
         spread_vs(0)
+        transpose_h("rest", 0)
         spread_vs(1)
-        interleave(1)
-        copy_h(("rest", 1))
-        quantise_h(("outlier", 0))
-        quantise_w(0)
-        quantise_h(("rest", 1))
-        quantise_w(1)
         copy_vs(0)
+        copy_h(scalar, "rest", 0)
+        interleave(0)
+        widen_scalar(1, 0)
+        widen_scalar(1, 1)
+        quantise_h("rest", 0)
+        quantise_w(0)
+        widen_vector(1, 2)
+        widen_vector(1, 3)
         copy_vs(1)
-
-        logits(0, 0)
-        widen(2)
-        logits(1, 0)
+        interleave(1)
+        logits_rest(0, 0)
+        transpose_h("outlier", 0)
+        copy_h(scalar, "outlier", 0)
+        transpose_h("rest", 1)
+        copy_h(scalar, "rest", 1)
+        negate_norm()
+        quantise_h("outlier", 0)
+        quantise_w(1)
+        quantise_h("rest", 1)
+        logits_rest(0, 1)
+        transpose_h("rest", 2)
+        transpose_h("outlier", 1)
+        copy_h(scalar, "rest", 2)
+        copy_h(scalar, "outlier", 1)
+        logits_outlier(0, 0)
+        logits_outlier(0, 1)
+        for t in range(3):
+            widen_vector(2, t)
+        widen_scalar(2, 3)
+        quantise_h("rest", 2)
+        quantise_h("outlier", 1)
         exponential(0, 0)
-        logits(0, 1)
-        widen(3)
-        exponential(1, 0)
         exponential(0, 1)
-        logits(1, 1)
         interleave(2)
-        interleave(3)
-        transpose_h(("rest", 2))
-        copy_h(("rest", 2))
-        exponential(1, 1)
-        transpose_h(("outlier", 1))
-        copy_h(("outlier", 1))
-        transpose_h(("rest", 3))
-        copy_h(("rest", 3))
+        for m in range(1, 3):
+            for g in range(2):
+                logits(m, g)
+        for t in range(3):
+            widen_scalar(3, t)
+        widen_vector(3, 3)
         quantise_w(2)
         subtract(0, 0)
-        quantise_w(3)
-        quantise_h(("rest", 2))
-        multiply(0, 0)
-        multiply(0, 1)
-        quantise_h(("outlier", 1))
-        quantise_h(("rest", 3))
-
-        for g in range(2, 4):
-            for m in range(2):
-                logits(m, g)
-                exponential(m, g)
-        copy_vs(2)
-        copy_vs(3)
+        interleave(3)
         subtract(0, 1)
+        quantise_w(3)
+        multiply(0, 0)
+        for m in range(3):
+            exponential(1 + m // 2, m % 2)
+            logits(m, 2)
+        exponential(2, 1)
+        exponential(0, 2)
+        exponential(1, 2)
+        subtract(0, 2)
+        multiply(0, 1)
+        logits(0, 3)
+        logits(1, 3)
+        exponential(0, 3)
         multiply(0, 2)
-        multiply(0, 3)
-        for g in range(3):
-            logits(2, g)
-            exponential(2, g)
-        for half in range(2):
-            transpose_e(0, half)
-        for half in range(2):
-            copy_e(0, half, scalar_copy)
-        logits(2, 3)
-        exponential(2, 3)
-
+        subtract(0, 3)
+        transpose_e(0, 0)
+        transpose_h("rest", 3)
+        exponential(2, 2)
+        copy_e(scalar, 0, 0)
+        copy_h(scalar, "rest", 3)
         subtract(1, 0)
+        multiply(0, 3)
+        logits(2, 3)
+        transpose_e(0, 2)
+        quantise_h("rest", 3)
+        quantise_e(0, 0, 2)
+        exponential(1, 3)
+        copy_e(scalar, 0, 2)
         subtract(1, 1)
-        multiply(1, 0)
-        quantise_e_whole(0)
-        for g in range(1, 4):
-            multiply(1, g)
-        for g in range(3):
-            logits(3, g)
-            exponential(3, g)
-        out_group(0, 0)
-        subtract(2, 0)
-        for half in range(2):
-            transpose_e(1, half)
-        for half in range(2):
-            copy_e(1, half, scalar_copy)
-        out_group(0, 1)
-        subtract(2, 1)
+        logits(3, 0)
+        quantise_e(0, 2, 2)
+        subtract(1, 2, 2)
+        exponential(2, 3)
+        product(0, 0)
+        exponential(3, 0)
+        logits(3, 1)
+        multiply(1, 0, 2)
+        multiply(1, 2, 2)
+        store(scalar, 0, 0)
+        product(0, N)
+        exponential(3, 1)
+        product(0, 2 * N)
+        store(scalar, 0, N)
+        transpose_e(1, 0)
+        transpose_e(1, 2)
+        subtract(2, 0, 2)
+        subtract(2, 2, 2)
+        copy_e(scalar, 1, 0)
+        copy_e(scalar, 1, 2)
+        store(scalar, 0, 2 * N)
+        logits(3, 2)
         logits(3, 3)
+        quantise_e(1, 0, 2)
+        multiply(2, 0)
+        quantise_e(1, 2, 2)
+        multiply(2, 1)
+        multiply(2, 2, 2)
+        exponential(3, 2)
         exponential(3, 3)
-        quantise_e_whole(1)
-        out_group(0, 2)
-
-        for g in range(4):
-            multiply(2, g)
-        subtract(3, 0)
-        out_group(1, 0)
-        for half in range(2):
-            transpose_e(2, half)
-        for half in range(2):
-            copy_e(2, half, scalar_copy)
-        subtract(3, 1)
-        out_group(1, 1)
-        quantise_e_whole(2)
-        out_group(1, 2)
-
-        for g in range(4):
-            multiply(3, g)
-        out_group(2, 0)
-        product(2, N, N, N)
-        for half in range(2):
-            transpose_e(3, half)
-        copy_e(3, 0, vector_copy)
-        copy_e(3, 1, scalar_copy)
-        store(2, N, N, scalar_copy)
-        product(2, 2 * N, N, N)
-        quantise_e(3, 0)
-        quantise_e(3, 1)
-        store(2, 2 * N, N, vector_copy)
-
-        out_group(3, 0)
-        out_group(3, 1)
+        product(1, 0)
+        product(1, N)
+        subtract(3, 0, 2)
+        subtract(3, 2, 2)
+        store(scalar, 1, 0)
+        transpose_e(2, 0)
+        transpose_e(2, 2)
+        copy_e(scalar, 2, 0)
+        copy_e(scalar, 2, 2)
+        product(1, 2 * N)
+        quantise_e(2, 0, 2)
+        quantise_e(2, 2, 2)
+        multiply(3, 0, 2)
+        multiply(3, 2, 2)
+        store(scalar, 1, N)
+        product(2, 0)
+        store(scalar, 1, 2 * N)
+        product(2, N)
+        store(scalar, 2, 0)
+        transpose_e(3, 0)
+        transpose_e(3, 2)
+        copy_e(vector, 3, 0)
+        copy_e(scalar, 3, 2)
+        product(2, 2 * N)
+        quantise_e(3, 0, 2)
+        quantise_e(3, 2, 2)
+        store(scalar, 2, N)
+        store(vector, 2, 2 * N)
+        product(3, 0)
+        store(scalar, 3, 0)
+        product(3, N)
+        store(vector, 3, N)
         product(3, 2 * N, 3 * P, P)
-        store(3, 2 * N, 3 * P, scalar_copy)
+        store(scalar, 3, 2 * N, 3 * P)
         product(3, 2 * N + 3 * P, P, P)
-        store(3, 2 * N + 3 * P, P, vector_copy)
+        store(vector, 3, 2 * N + 3 * P, P)

@@ -25,7 +25,6 @@ M_TILES = TOKENS // P
 V_GROUPS = VOCAB // N
 D_GROUPS = HIDDEN // N
 VS_ROWS = VOCAB // P
-BANK_ROWS = VS_ROWS // 2
 
 
 def tile_cross_entropy_hidden_gradient_s3_kernel(
@@ -61,9 +60,10 @@ def tile_cross_entropy_hidden_gradient_s3_kernel(
         make_identity(nc, ident[:])
         nc.vector.memset(table[:], 0.0)
         nc.scalar.activation(out=table[:], in_=table[:], func=EXP)
-        for plane in wr_scale + [wt_scale]:
+        for plane in wr_scale:
             nc.vector.memset(plane[:].bitcast(I32), 0)
         nc.vector.tensor_copy(out=ident_bf[:], in_=ident[:])
+        nc.vector.memset(wt_scale[:].bitcast(I32), 0)
 
         norm = kept([P, M_TILES], BF16, "norm")
         w_scale = kept([P, 4], F32, "w_scale")
@@ -85,9 +85,8 @@ def tile_cross_entropy_hidden_gradient_s3_kernel(
             nc.sync.dma_start(out=tile, in_=source)
 
         def load_scales(plane, source):
-            for q in range(4):
-                load(plane[32 * q:32 * q + 4].bitcast(I32),
-                     source[:, 4 * q:4 * q + 4, :].bitcast(I32).rearrange("g r n -> r g n"))
+            for r in range(4):
+                load(plane[r:P:32].bitcast(I32), source[:, r:16:4, :].bitcast(I32).rearrange("g q n -> q g n"))
 
         def load_bytes(g):
             load(w_bytes[g][:], w_view[:, :, cols(g)])
@@ -110,22 +109,22 @@ def tile_cross_entropy_hidden_gradient_s3_kernel(
         def load_wt(g):
             load(wt[g][:], wt_words[g])
 
-        load(vs_rows[0:VS_ROWS, :], vocab_scale.rearrange("(r c) -> r c", c=P))
         load_bytes(0)
         load(w_scale[:], w_out_scale.rearrange("(p t) o -> p (t o)", t=4))
         load_rest(0)
-        load_bytes(1)
-        load_wr_scales(0)
-        load_wr(0)
+        load(vs_rows[0:VS_ROWS, :], vocab_scale.rearrange("(r c) -> r c", c=P))
         load_outlier(0)
+        load_bytes(1)
         load_rest(1)
-        load_wr(1)
-        load(norm[:], log_norm.rearrange("(p m) -> p m", m=M_TILES))
         load_rest(2)
         load_outlier(1)
+        load_wr_scales(0)
+        load_wr(0)
+        load(norm[:], log_norm.rearrange("(p m) -> p m", m=M_TILES))
         load_bytes(2)
-        load_target(0, 0)
+        load_wr(1)
         load_bytes(3)
+        load_target(0, 0)
         load_wr_scales(1)
         load_wr(2)
         load_target(1, 0)
@@ -209,13 +208,19 @@ def tile_cross_entropy_hidden_gradient_s3_kernel(
         def negate_norm():
             nc.vector.tensor_scalar(out=minus_norm[:], in0=norm[:], scalar1=-1.0, scalar2=None, op0=MULT)
 
-        def spread_vs(half):
-            bank = t_psum.tile([P, BANK_ROWS * P], BF16, name="vs_bank", tag="t")
-            vs_bank[half] = bank
-            for r in range(BANK_ROWS):
-                row = half * BANK_ROWS + r
-                nc.tensor.matmul(bank[:, rows(r)], lhsT=ident_bf[:, row:row + 1].to_broadcast([P, P]), rhs=vs_rows[:],
-                                 start=True, stop=True)
+        def spread_vs(g, pool, tag):
+            if g % 2 == 0:
+                vs_bank[g // 2] = pool.tile([P, 2 * N], BF16, name="vs_bank", tag=tag)
+            for r in range(4):
+                row = 4 * g + r
+                nc.tensor.matmul(vs_bank[g // 2][:, rows(row % 8)], lhsT=ident_bf[:, row:row + 1].to_broadcast([P, P]),
+                                 rhs=vs_rows[:], start=True, stop=True)
+
+        warm_bank = sum_psum.tile([P, N], F32, name="warm_bank", tag="sum")
+
+        def warm_up():
+            nc.tensor.matmul(warm_bank[:].rearrange("p (a c) -> p a c", a=4), lhsT=ident_bf[:],
+                             rhs=ident_bf[:].unsqueeze(1).to_broadcast([P, 4, P]), start=True, stop=True)
 
         def copy_vs(half):
             nc.scalar.copy(out=vs[:, cols(2 * half, 2)].bitcast(F32).rearrange("q (u w) -> q u w", u=2),
@@ -310,11 +315,15 @@ def tile_cross_entropy_hidden_gradient_s3_kernel(
         for t in range(3):
             widen_vector(0, t)
         widen_scalar(0, 3)
-        spread_vs(0)
+        for i in range(3):
+            warm_up()
         transpose_h("rest", 0)
-        spread_vs(1)
-        copy_vs(0)
+        spread_vs(0, sum_psum, "sum")
+        transpose_h("outlier", 0)
+        spread_vs(1, sum_psum, "sum")
+        warm_up()
         copy_h(scalar, "rest", 0)
+        copy_h(scalar, "outlier", 0)
         interleave(0)
         widen_scalar(1, 0)
         widen_scalar(1, 1)
@@ -322,83 +331,83 @@ def tile_cross_entropy_hidden_gradient_s3_kernel(
         quantise_w(0)
         widen_vector(1, 2)
         widen_vector(1, 3)
-        copy_vs(1)
-        interleave(1)
-        logits_rest(0, 0)
-        transpose_h("outlier", 0)
-        copy_h(scalar, "outlier", 0)
-        transpose_h("rest", 1)
-        copy_h(scalar, "rest", 1)
-        negate_norm()
         quantise_h("outlier", 0)
-        quantise_w(1)
-        quantise_h("rest", 1)
-        logits_rest(0, 1)
+        transpose_h("rest", 1)
+        warm_up()
         transpose_h("rest", 2)
+        warm_up()
         transpose_h("outlier", 1)
+        copy_h(scalar, "rest", 1)
+        spread_vs(2, t_psum, "t")
+        spread_vs(3, t_psum, "t")
         copy_h(scalar, "rest", 2)
         copy_h(scalar, "outlier", 1)
-        logits_outlier(0, 0)
-        logits_outlier(0, 1)
-        for t in range(3):
-            widen_vector(2, t)
-        widen_scalar(2, 3)
+        copy_vs(0)
+        interleave(1)
+        quantise_h("rest", 1)
         quantise_h("rest", 2)
         quantise_h("outlier", 1)
+        negate_norm()
+        for t in range(2):
+            widen_vector(2, t)
+        widen_scalar(2, 2)
+        widen_scalar(2, 3)
+        quantise_w(1)
+        for m in range(3):
+            logits(m, 0)
         exponential(0, 0)
-        exponential(0, 1)
         interleave(2)
-        for m in range(1, 3):
-            for g in range(2):
-                logits(m, g)
         for t in range(3):
             widen_scalar(3, t)
+        exponential(1, 0)
+        exponential(2, 0)
         widen_vector(3, 3)
         quantise_w(2)
         subtract(0, 0)
+        for m in range(3):
+            logits(m, 1)
+            exponential(m, 1)
         interleave(3)
         subtract(0, 1)
         quantise_w(3)
-        multiply(0, 0)
+        multiply(0, 0, 2)
         for m in range(3):
-            exponential(1 + m // 2, m % 2)
             logits(m, 2)
-        exponential(2, 1)
         exponential(0, 2)
-        exponential(1, 2)
+        copy_vs(1)
         subtract(0, 2)
-        multiply(0, 1)
+        subtract(1, 0)
         logits(0, 3)
         logits(1, 3)
         exponential(0, 3)
-        multiply(0, 2)
+        exponential(1, 2)
         subtract(0, 3)
+        multiply(0, 2)
+        multiply(0, 3)
         transpose_e(0, 0)
         transpose_h("rest", 3)
-        exponential(2, 2)
         copy_e(scalar, 0, 0)
         copy_h(scalar, "rest", 3)
-        subtract(1, 0)
-        multiply(0, 3)
+        exponential(2, 2)
         logits(2, 3)
         transpose_e(0, 2)
         quantise_h("rest", 3)
         quantise_e(0, 0, 2)
+        subtract(1, 1)
         exponential(1, 3)
         copy_e(scalar, 0, 2)
-        subtract(1, 1)
+        subtract(1, 2, 2)
         logits(3, 0)
         quantise_e(0, 2, 2)
-        subtract(1, 2, 2)
+        multiply(1, 0, 2)
         exponential(2, 3)
+        logits(3, 1)
         product(0, 0)
         exponential(3, 0)
-        logits(3, 1)
-        multiply(1, 0, 2)
+        exponential(3, 1)
         multiply(1, 2, 2)
         store(scalar, 0, 0)
         product(0, N)
-        exponential(3, 1)
         product(0, 2 * N)
         store(scalar, 0, N)
         transpose_e(1, 0)
@@ -411,9 +420,8 @@ def tile_cross_entropy_hidden_gradient_s3_kernel(
         logits(3, 2)
         logits(3, 3)
         quantise_e(1, 0, 2)
-        multiply(2, 0)
         quantise_e(1, 2, 2)
-        multiply(2, 1)
+        multiply(2, 0, 2)
         multiply(2, 2, 2)
         exponential(3, 2)
         exponential(3, 3)

@@ -56,14 +56,15 @@ def tile_cross_entropy_hidden_gradient_s3_kernel(
         table = kept([P, 1], F32, "table")
         ident = kept([P, P], F32, "ident")
         ident_bf = kept([P, P], BF16, "ident_bf")
-        nc.gpsimd.memset(vs_rows[:], 0.0)
         make_identity(nc, ident[:])
+        warm_rows = kept([P, P], BF16, "warm_rows")
         nc.vector.memset(table[:], 0.0)
+        nc.vector.memset(vs_rows[:], 0.0)
+        nc.vector.memset(warm_rows[:], 0.0)
         nc.scalar.activation(out=table[:], in_=table[:], func=EXP)
-        for plane in wr_scale:
+        nc.scalar.copy(out=ident_bf[:], in_=ident[:])
+        for plane in wr_scale + [wt_scale]:
             nc.vector.memset(plane[:].bitcast(I32), 0)
-        nc.vector.tensor_copy(out=ident_bf[:], in_=ident[:])
-        nc.vector.memset(wt_scale[:].bitcast(I32), 0)
 
         norm = kept([P, M_TILES], BF16, "norm")
         w_scale = kept([P, 4], F32, "w_scale")
@@ -71,7 +72,7 @@ def tile_cross_entropy_hidden_gradient_s3_kernel(
         wr = [kept([P, 2, 2 * N], U8, "wr%d" % g) for g in range(V_GROUPS)]
         rest = [kept([P, REST_CH], BF16, "rest%d" % m) for m in range(M_TILES)]
         outlier = [kept([P, 2 * OUT_CH], BF16, "outlier%d" % i) for i in range(2)]
-        target = [[kept([P, 2 * N], BF16, "target%d_%d" % (m, half)) for half in range(2)] for m in range(M_TILES)]
+        target = [kept([P, VOCAB], BF16, "target%d" % m) for m in range(M_TILES)]
         wt = [kept([P, 2 * HIDDEN], U8, "wt%d" % g) for g in range(V_GROUPS)]
 
         w_view = w_out_bytes.rearrange("(p t) v -> p t v", t=4)
@@ -91,8 +92,8 @@ def tile_cross_entropy_hidden_gradient_s3_kernel(
         def load_bytes(g):
             load(w_bytes[g][:], w_view[:, :, cols(g)])
 
-        def load_wr(g):
-            load(wr[g][:], wr_view[:, :, cols(2 * g, 2)])
+        def load_wr(g, first=0, count=2):
+            load(wr[g][:, first:first + count, :], wr_view[:, first:first + count, cols(2 * g, 2)])
 
         def load_wr_scales(i):
             load_scales(wr_scale[i], w_rest_scales[:, :, cols(2 * i, 2)])
@@ -103,8 +104,8 @@ def tile_cross_entropy_hidden_gradient_s3_kernel(
         def load_outlier(i):
             load(outlier[i][:], outlier_view[:, i, :])
 
-        def load_target(m, half):
-            load(target[m][half][:], target_view[:, m, cols(2 * half, 2)])
+        def load_target(m, g=0, count=V_GROUPS):
+            load(target[m][:, cols(g, count)], target_view[:, m, cols(g, count)])
 
         def load_wt(g):
             load(wt[g][:], wt_words[g])
@@ -116,30 +117,29 @@ def tile_cross_entropy_hidden_gradient_s3_kernel(
         load_outlier(0)
         load_bytes(1)
         load_rest(1)
-        load_rest(2)
         load_outlier(1)
-        load_wr_scales(0)
-        load_wr(0)
+        load_rest(2)
         load(norm[:], log_norm.rearrange("(p m) -> p m", m=M_TILES))
         load_bytes(2)
+        load_wr_scales(0)
+        load_wr(0)
         load_wr(1)
         load_bytes(3)
-        load_target(0, 0)
+        load_target(0, 0, 2)
         load_wr_scales(1)
         load_wr(2)
-        load_target(1, 0)
         load_wr(3)
-        load_target(0, 1)
+        load_target(0, 2, 2)
+        load_target(1, 0, 2)
         load_rest(3)
         load_scales(wt_scale, wt_scales)
         load_wt(0)
+        load_target(1, 2, 2)
         load_wt(1)
-        load_target(1, 1)
         load_wt(2)
         load_wt(3)
-        for m in range(2, M_TILES):
-            for half in range(2):
-                load_target(m, half)
+        load_target(2)
+        load_target(3)
 
         wide, w_grouped = {}, {}
         w_codes = [kept([P, N], U32, "w_codes%d" % g) for g in range(V_GROUPS)]
@@ -219,8 +219,8 @@ def tile_cross_entropy_hidden_gradient_s3_kernel(
         warm_bank = sum_psum.tile([P, N], F32, name="warm_bank", tag="sum")
 
         def warm_up():
-            nc.tensor.matmul(warm_bank[:].rearrange("p (a c) -> p a c", a=4), lhsT=ident_bf[:],
-                             rhs=ident_bf[:].unsqueeze(1).to_broadcast([P, 4, P]), start=True, stop=True)
+            nc.tensor.matmul(warm_bank[:].rearrange("p (a c) -> p a c", a=4), lhsT=warm_rows[:],
+                             rhs=warm_rows[:].unsqueeze(1).to_broadcast([P, 4, P]), start=True, stop=True)
 
         def copy_vs(half):
             nc.scalar.copy(out=vs[:, cols(2 * half, 2)].bitcast(F32).rearrange("q (u w) -> q u w", u=2),
@@ -229,27 +229,20 @@ def tile_cross_entropy_hidden_gradient_s3_kernel(
         z_bank, grad = {}, {}
         e_tile = [kept([P, VOCAB], F32, "e%d" % m) for m in range(M_TILES)]
 
-        def logits_rest(m, g):
-            bank = sum_psum.tile([P, N], F32, name="z_bank", tag="sum")
-            z_bank[m, g] = bank
-            for j in range(2):
+        def logits(m, g, passes=("rest0", "rest1", "outlier"), opens=True, closes=True):
+            if opens:
+                z_bank[m, g] = sum_psum.tile([P, N], F32, name="z_bank", tag="sum")
+            for name in passes:
+                if name == "outlier":
+                    pair, j = ("outlier", m // 2), m % 2
+                    moving, moving_scale = w_codes[g][:].bitcast(E4M3_X4), w_codes_scale[g][:]
+                else:
+                    pair, j = ("rest", m), int(name[-1])
+                    moving, moving_scale = wr[g][:, j, :].bitcast(E2M1_X4), wr_scale[g // 2][:, j, cols(g % 2)]
                 nc.tensor.matmul_mx(
-                    out=bank[:],
-                    lhsT=h_codes["rest", m][:, j, :].bitcast(E4M3_X4), lhsT_scale=h_scale["rest", m][:, j, :],
-                    rhs=wr[g][:, j, :].bitcast(E2M1_X4), rhs_scale=wr_scale[g // 2][:, j, cols(g % 2)],
-                    start=(j == 0), stop=False)
-
-        def logits_outlier(m, g):
-            pair = ("outlier", m // 2)
-            nc.tensor.matmul_mx(
-                out=z_bank[m, g][:],
-                lhsT=h_codes[pair][:, m % 2, :].bitcast(E4M3_X4), lhsT_scale=h_scale[pair][:, m % 2, :],
-                rhs=w_codes[g][:].bitcast(E4M3_X4), rhs_scale=w_codes_scale[g][:],
-                start=False, stop=True)
-
-        def logits(m, g):
-            logits_rest(m, g)
-            logits_outlier(m, g)
+                    out=z_bank[m, g][:], lhsT=h_codes[pair][:, j, :].bitcast(E4M3_X4), lhsT_scale=h_scale[pair][:, j, :],
+                    rhs=moving, rhs_scale=moving_scale,
+                    start=(opens and name == passes[0]), stop=(closes and name == passes[-1]))
 
         def exponential(m, g):
             nc.scalar.activation(out=stored(e_tile[m], g, 1), in_=word_order(z_bank[m, g][:]), func=EXP,
@@ -257,7 +250,7 @@ def tile_cross_entropy_hidden_gradient_s3_kernel(
 
         def subtract(m, g, count=1):
             e = stored(e_tile[m], g, count)
-            nc.vector.tensor_tensor(out=e, in0=e, in1=word_order(target[m][g // 2][:, cols(g % 2, count)]), op=SUBTRACT)
+            nc.vector.tensor_tensor(out=e, in0=e, in1=word_order(target[m][:, cols(g, count)]), op=SUBTRACT)
 
         def multiply(m, g, count=1):
             if m not in grad:
@@ -305,17 +298,17 @@ def tile_cross_entropy_hidden_gradient_s3_kernel(
                         rhs=wt[g][:, 2 * d0:2 * (d0 + step)].bitcast(E2M1_X4), rhs_scale=wt_scale[:, g, d0:d0 + step],
                         start=(g == 0), stop=(g == V_GROUPS - 1))
 
-        def store(copy, m, first, width=N):
+        def store(copy, m, first, width=N, skip=0):
             result = store_pool.tile([P, N], F32, name="result")
-            copy(out=result[:, 0:width], in_=o_bank[m, first][:, 0:width])
-            nc.sync.dma_start(out=out_view[:, m, first:first + width], in_=result[:, 0:width])
+            copy(out=result[:, 0:width], in_=o_bank[m, first][:, skip:skip + width])
+            nc.sync.dma_start(out=out_view[:, m, first + skip:first + skip + width], in_=result[:, 0:width])
 
         scalar, vector = nc.scalar.copy, nc.vector.tensor_copy
 
         for t in range(3):
             widen_vector(0, t)
         widen_scalar(0, 3)
-        for i in range(3):
+        for i in range(5):
             warm_up()
         transpose_h("rest", 0)
         spread_vs(0, sum_psum, "sum")
@@ -334,115 +327,126 @@ def tile_cross_entropy_hidden_gradient_s3_kernel(
         quantise_h("outlier", 0)
         transpose_h("rest", 1)
         warm_up()
-        transpose_h("rest", 2)
-        warm_up()
         transpose_h("outlier", 1)
+        warm_up()
+        transpose_h("rest", 2)
         copy_h(scalar, "rest", 1)
         spread_vs(2, t_psum, "t")
         spread_vs(3, t_psum, "t")
-        copy_h(scalar, "rest", 2)
         copy_h(scalar, "outlier", 1)
-        copy_vs(0)
+        copy_h(scalar, "rest", 2)
         interleave(1)
-        quantise_h("rest", 1)
-        quantise_h("rest", 2)
         quantise_h("outlier", 1)
+        quantise_h("rest", 1)
         negate_norm()
         for t in range(2):
             widen_vector(2, t)
         widen_scalar(2, 2)
         widen_scalar(2, 3)
+        copy_vs(0)
         quantise_w(1)
+        quantise_h("rest", 2)
         for m in range(3):
-            logits(m, 0)
-        exponential(0, 0)
+            logits(m, 0, ("outlier",), closes=False)
+        for m in range(3):
+            logits(m, 0, ("rest0", "rest1"), opens=False)
         interleave(2)
-        for t in range(3):
-            widen_scalar(3, t)
-        exponential(1, 0)
-        exponential(2, 0)
+        exponential(0, 0)
+        widen_scalar(3, 0)
+        widen_scalar(3, 1)
+        widen_vector(3, 2)
         widen_vector(3, 3)
         quantise_w(2)
         subtract(0, 0)
-        for m in range(3):
+        logits(0, 1)
+        exponential(0, 1)
+        exponential(1, 0)
+        exponential(2, 0)
+        for m in range(1, 3):
             logits(m, 1)
             exponential(m, 1)
         interleave(3)
         subtract(0, 1)
         quantise_w(3)
         multiply(0, 0, 2)
-        for m in range(3):
-            logits(m, 2)
+        logits(0, 2)
+        logits(1, 2)
+        logits(2, 2)
+        logits(0, 3)
         exponential(0, 2)
         copy_vs(1)
-        subtract(0, 2)
-        subtract(1, 0)
-        logits(0, 3)
-        logits(1, 3)
-        exponential(0, 3)
         exponential(1, 2)
+        exponential(0, 3)
+        subtract(0, 2)
+        subtract(1, 0, 2)
         subtract(0, 3)
+        logits(1, 3)
         multiply(0, 2)
         multiply(0, 3)
-        transpose_e(0, 0)
         transpose_h("rest", 3)
-        copy_e(scalar, 0, 0)
+        transpose_e(0, 0)
         copy_h(scalar, "rest", 3)
+        copy_e(scalar, 0, 0)
+        exponential(1, 3)
         exponential(2, 2)
         logits(2, 3)
         transpose_e(0, 2)
         quantise_h("rest", 3)
+        multiply(1, 0)
         quantise_e(0, 0, 2)
-        subtract(1, 1)
-        exponential(1, 3)
+        multiply(1, 1)
         copy_e(scalar, 0, 2)
         subtract(1, 2, 2)
         logits(3, 0)
         quantise_e(0, 2, 2)
-        multiply(1, 0, 2)
         exponential(2, 3)
         logits(3, 1)
-        product(0, 0)
+        for d in range(D_GROUPS):
+            product(0, d * N, groups=range(2))
         exponential(3, 0)
         exponential(3, 1)
         multiply(1, 2, 2)
+        for d in range(D_GROUPS):
+            product(0, d * N, groups=range(2, 4))
         store(scalar, 0, 0)
-        product(0, N)
-        product(0, 2 * N)
         store(scalar, 0, N)
         transpose_e(1, 0)
         transpose_e(1, 2)
         subtract(2, 0, 2)
         subtract(2, 2, 2)
+        multiply(2, 0)
         copy_e(scalar, 1, 0)
         copy_e(scalar, 1, 2)
         store(scalar, 0, 2 * N)
         logits(3, 2)
         logits(3, 3)
         quantise_e(1, 0, 2)
+        multiply(2, 1)
         quantise_e(1, 2, 2)
-        multiply(2, 0, 2)
         multiply(2, 2, 2)
         exponential(3, 2)
         exponential(3, 3)
-        product(1, 0)
-        product(1, N)
+        for groups in (range(2), range(2, 4)):
+            product(1, 0, groups=groups)
+            product(1, N, groups=groups)
         subtract(3, 0, 2)
-        subtract(3, 2, 2)
+        subtract(3, 2)
         store(scalar, 1, 0)
         transpose_e(2, 0)
         transpose_e(2, 2)
         copy_e(scalar, 2, 0)
         copy_e(scalar, 2, 2)
         product(1, 2 * N)
+        subtract(3, 3)
         quantise_e(2, 0, 2)
         quantise_e(2, 2, 2)
         multiply(3, 0, 2)
         multiply(3, 2, 2)
         store(scalar, 1, N)
-        product(2, 0)
         store(scalar, 1, 2 * N)
-        product(2, N)
+        for groups in (range(2), range(2, 4)):
+            product(2, 0, groups=groups)
+            product(2, N, groups=groups)
         store(scalar, 2, 0)
         transpose_e(3, 0)
         transpose_e(3, 2)
@@ -457,7 +461,6 @@ def tile_cross_entropy_hidden_gradient_s3_kernel(
         store(scalar, 3, 0)
         product(3, N)
         store(vector, 3, N)
-        product(3, 2 * N, 3 * P, P)
-        store(scalar, 3, 2 * N, 3 * P)
-        product(3, 2 * N + 3 * P, P, P)
-        store(vector, 3, 2 * N + 3 * P, P)
+        product(3, 2 * N)
+        store(scalar, 3, 2 * N, 2 * P)
+        store(scalar, 3, 2 * N, 2 * P, 2 * P)

@@ -53,15 +53,10 @@ def tile_cross_entropy_hidden_gradient_s3_kernel(
         wr_scale = [kept([P, 2, 2 * N], U8, "wr_scale%d" % i) for i in range(2)]
         wt_scale = kept([P, V_GROUPS, HIDDEN], U8, "wt_scale")
         vs_rows = kept([P, P], BF16, "vs_rows")
-        table = kept([P, 1], F32, "table")
         ident = kept([P, P], F32, "ident")
         ident_bf = kept([P, P], BF16, "ident_bf")
         make_identity(nc, ident[:])
-        warm_rows = kept([P, P], BF16, "warm_rows")
-        nc.vector.memset(table[:], 0.0)
         nc.vector.memset(vs_rows[:], 0.0)
-        nc.vector.memset(warm_rows[:], 0.0)
-        nc.scalar.activation(out=table[:], in_=table[:], func=EXP)
         nc.scalar.copy(out=ident_bf[:], in_=ident[:])
         for plane in wr_scale + [wt_scale]:
             nc.vector.memset(plane[:].bitcast(I32), 0)
@@ -216,12 +211,6 @@ def tile_cross_entropy_hidden_gradient_s3_kernel(
                 nc.tensor.matmul(vs_bank[g // 2][:, rows(row % 8)], lhsT=ident_bf[:, row:row + 1].to_broadcast([P, P]),
                                  rhs=vs_rows[:], start=True, stop=True)
 
-        warm_bank = sum_psum.tile([P, N], F32, name="warm_bank", tag="sum")
-
-        def warm_up():
-            nc.tensor.matmul(warm_bank[:].rearrange("p (a c) -> p a c", a=4), lhsT=warm_rows[:],
-                             rhs=warm_rows[:].unsqueeze(1).to_broadcast([P, 4, P]), start=True, stop=True)
-
         def copy_vs(half):
             nc.scalar.copy(out=vs[:, cols(2 * half, 2)].bitcast(F32).rearrange("q (u w) -> q u w", u=2),
                            in_=vs_bank[half][:].bitcast(F32).rearrange("q (w u) -> q u w", u=2))
@@ -308,13 +297,10 @@ def tile_cross_entropy_hidden_gradient_s3_kernel(
         for t in range(3):
             widen_vector(0, t)
         widen_scalar(0, 3)
-        for i in range(5):
-            warm_up()
         transpose_h("rest", 0)
         spread_vs(0, sum_psum, "sum")
         transpose_h("outlier", 0)
         spread_vs(1, sum_psum, "sum")
-        warm_up()
         copy_h(scalar, "rest", 0)
         copy_h(scalar, "outlier", 0)
         interleave(0)
@@ -326,9 +312,7 @@ def tile_cross_entropy_hidden_gradient_s3_kernel(
         widen_vector(1, 3)
         quantise_h("outlier", 0)
         transpose_h("rest", 1)
-        warm_up()
         transpose_h("outlier", 1)
-        warm_up()
         transpose_h("rest", 2)
         copy_h(scalar, "rest", 1)
         spread_vs(2, t_psum, "t")

@@ -51,24 +51,25 @@ def tile_cross_entropy_hidden_gradient_s3_kernel(
             return slice(g * N, (g + count) * N)
 
         wr_scale = [kept([P, 2, 2 * N], U8, "wr_scale%d" % i) for i in range(2)]
-        wt_scale = kept([P, V_GROUPS, HIDDEN], U8, "wt_scale")
         vs_rows = kept([P, P], BF16, "vs_rows")
         ident = kept([P, P], F32, "ident")
         ident_bf = kept([P, P], BF16, "ident_bf")
         make_identity(nc, ident[:])
         nc.vector.memset(vs_rows[:], 0.0)
         nc.scalar.copy(out=ident_bf[:], in_=ident[:])
-        for plane in wr_scale + [wt_scale]:
+        for plane in wr_scale:
             nc.vector.memset(plane[:].bitcast(I32), 0)
 
         norm = kept([P, M_TILES], BF16, "norm")
         w_scale = kept([P, 4], F32, "w_scale")
-        w_bytes = [kept([P, 4, N], U8, "w_bytes%d" % g) for g in range(V_GROUPS)]
-        wr = [kept([P, 2, 2 * N], U8, "wr%d" % g) for g in range(V_GROUPS)]
-        rest = [kept([P, REST_CH], BF16, "rest%d" % m) for m in range(M_TILES)]
-        outlier = [kept([P, 2 * OUT_CH], BF16, "outlier%d" % i) for i in range(2)]
+        w_bytes = [kept([P, 2, VOCAB], U8, "w_bytes%d" % i) for i in range(2)]
+        wr = kept([P, 2, 2 * VOCAB], U8, "wr")
+        h_first = keep.tile([P, 3 * REST_CH], BF16, name="h_first", tag="shared", align_bytes=256)
+        rest = [h_first[:, 0:REST_CH], h_first[:, REST_CH:2 * REST_CH]]
+        rest = rest + [kept([P, REST_CH], BF16, "rest%d" % m)[:] for m in range(2, M_TILES)]
+        outlier = [h_first[:, 2 * REST_CH:3 * REST_CH], kept([P, 2 * OUT_CH], BF16, "outlier1")[:]]
         target = [kept([P, VOCAB], BF16, "target%d" % m) for m in range(M_TILES)]
-        wt = [kept([P, 2 * HIDDEN], U8, "wt%d" % g) for g in range(V_GROUPS)]
+        wt = kept([P, V_GROUPS, 2 * HIDDEN], U8, "wt")
 
         w_view = w_out_bytes.rearrange("(p t) v -> p t v", t=4)
         wr_view = w_rest_words.rearrange("g p n -> p g n")
@@ -84,11 +85,11 @@ def tile_cross_entropy_hidden_gradient_s3_kernel(
             for r in range(4):
                 load(plane[r:P:32].bitcast(I32), source[:, r:16:4, :].bitcast(I32).rearrange("g q n -> q g n"))
 
-        def load_bytes(g):
-            load(w_bytes[g][:], w_view[:, :, cols(g)])
+        def load_bytes(i):
+            load(w_bytes[i][:], w_view[:, 2 * i:2 * i + 2, :])
 
-        def load_wr(g, first=0, count=2):
-            load(wr[g][:, first:first + count, :], wr_view[:, first:first + count, cols(2 * g, 2)])
+        def load_wr(g, count=1):
+            load(wr[:, :, cols(2 * g, 2 * count)], wr_view[:, :, cols(2 * g, 2 * count)])
 
         def load_wr_scales(i):
             load_scales(wr_scale[i], w_rest_scales[:, :, cols(2 * i, 2)])
@@ -102,39 +103,29 @@ def tile_cross_entropy_hidden_gradient_s3_kernel(
         def load_target(m, g=0, count=V_GROUPS):
             load(target[m][:, cols(g, count)], target_view[:, m, cols(g, count)])
 
-        def load_wt(g):
-            load(wt[g][:], wt_words[g])
+        def load_wt(g, count):
+            load(wt[:, g:g + count, :], wt_words[g:g + count].rearrange("g p n -> p g n"))
 
         load_bytes(0)
         load(w_scale[:], w_out_scale.rearrange("(p t) o -> p (t o)", t=4))
-        load_rest(0)
         load(vs_rows[0:VS_ROWS, :], vocab_scale.rearrange("(r c) -> r c", c=P))
-        load_outlier(0)
         load_bytes(1)
+        load_rest(0)
+        load_outlier(0)
         load_rest(1)
         load_outlier(1)
         load_rest(2)
-        load(norm[:], log_norm.rearrange("(p m) -> p m", m=M_TILES))
-        load_bytes(2)
         load_wr_scales(0)
         load_wr(0)
+        load(norm[:], log_norm.rearrange("(p m) -> p m", m=M_TILES))
         load_wr(1)
-        load_bytes(3)
         load_target(0, 0, 2)
         load_wr_scales(1)
         load_wr(2)
         load_wr(3)
         load_target(0, 2, 2)
-        load_target(1, 0, 2)
+        load_target(1)
         load_rest(3)
-        load_scales(wt_scale, wt_scales)
-        load_wt(0)
-        load_target(1, 2, 2)
-        load_wt(1)
-        load_wt(2)
-        load_wt(3)
-        load_target(2)
-        load_target(3)
 
         wide, w_grouped = {}, {}
         w_codes = [kept([P, N], U32, "w_codes%d" % g) for g in range(V_GROUPS)]
@@ -142,15 +133,15 @@ def tile_cross_entropy_hidden_gradient_s3_kernel(
 
         def wide_tile(g):
             if g not in wide:
-                wide[g] = wide_pool.tile([P, 4, N], BF16, name="wide", align_bytes=256)
+                wide[g] = wide_pool.tile([P, 4, N], BF16, name="wide", align_bytes=256, bufs=V_GROUPS)
             return wide[g]
 
         def widen_vector(g, t):
-            nc.vector.tensor_scalar(out=wide_tile(g)[:, t, :], in0=w_bytes[g][:, t, :].bitcast(E4M3FN),
+            nc.vector.tensor_scalar(out=wide_tile(g)[:, t, :], in0=w_bytes[t // 2][:, t % 2, cols(g)].bitcast(E4M3FN),
                                     scalar1=w_scale[:, t:t + 1], scalar2=None, op0=MULT)
 
         def widen_scalar(g, t):
-            nc.scalar.activation(out=wide_tile(g)[:, t, :], in_=w_bytes[g][:, t, :].bitcast(E4M3FN), func=COPY,
+            nc.scalar.activation(out=wide_tile(g)[:, t, :], in_=w_bytes[t // 2][:, t % 2, cols(g)].bitcast(E4M3FN), func=COPY,
                                  scale=w_scale[:, t:t + 1])
 
         def interleave(g):
@@ -227,7 +218,7 @@ def tile_cross_entropy_hidden_gradient_s3_kernel(
                     moving, moving_scale = w_codes[g][:].bitcast(E4M3_X4), w_codes_scale[g][:]
                 else:
                     pair, j = ("rest", m), int(name[-1])
-                    moving, moving_scale = wr[g][:, j, :].bitcast(E2M1_X4), wr_scale[g // 2][:, j, cols(g % 2)]
+                    moving, moving_scale = wr[:, j, cols(2 * g, 2)].bitcast(E2M1_X4), wr_scale[g // 2][:, j, cols(g % 2)]
                 nc.tensor.matmul_mx(
                     out=z_bank[m, g][:], lhsT=h_codes[pair][:, j, :].bitcast(E4M3_X4), lhsT_scale=h_scale[pair][:, j, :],
                     rhs=moving, rhs_scale=moving_scale,
@@ -284,7 +275,7 @@ def tile_cross_entropy_hidden_gradient_s3_kernel(
                     nc.tensor.matmul_mx(
                         out=o_bank[m, first][:, c:c + step],
                         lhsT=g_codes[m][:, g, :].bitcast(E4M3_X4), lhsT_scale=g_scale[m][:, g, :],
-                        rhs=wt[g][:, 2 * d0:2 * (d0 + step)].bitcast(E2M1_X4), rhs_scale=wt_scale[:, g, d0:d0 + step],
+                        rhs=wt[:, g, 2 * d0:2 * (d0 + step)].bitcast(E2M1_X4), rhs_scale=wt_scale[:, g, d0:d0 + step],
                         start=(g == 0), stop=(g == V_GROUPS - 1))
 
         def store(copy, m, first, width=N, skip=0):
@@ -294,57 +285,63 @@ def tile_cross_entropy_hidden_gradient_s3_kernel(
 
         scalar, vector = nc.scalar.copy, nc.vector.tensor_copy
 
-        for t in range(3):
-            widen_vector(0, t)
-        widen_scalar(0, 3)
+        for g in range(2):
+            for t in range(2):
+                widen_vector(g, t)
+        widen_scalar(2, 0)
+        widen_scalar(2, 1)
+        widen_vector(0, 2)
+        widen_vector(0, 3)
+        widen_scalar(1, 2)
+        widen_scalar(1, 3)
+        for g in range(V_GROUPS):
+            spread_vs(g, sum_psum, "sum")
+        copy_vs(0)
         transpose_h("rest", 0)
-        spread_vs(0, sum_psum, "sum")
         transpose_h("outlier", 0)
-        spread_vs(1, sum_psum, "sum")
         copy_h(scalar, "rest", 0)
         copy_h(scalar, "outlier", 0)
+        widen_vector(3, 0)
         interleave(0)
-        widen_scalar(1, 0)
-        widen_scalar(1, 1)
-        quantise_h("rest", 0)
+        widen_vector(3, 1)
         quantise_w(0)
-        widen_vector(1, 2)
-        widen_vector(1, 3)
+        quantise_h("rest", 0)
         quantise_h("outlier", 0)
         transpose_h("rest", 1)
         transpose_h("outlier", 1)
-        transpose_h("rest", 2)
         copy_h(scalar, "rest", 1)
-        spread_vs(2, t_psum, "t")
-        spread_vs(3, t_psum, "t")
+        transpose_h("rest", 2)
         copy_h(scalar, "outlier", 1)
         copy_h(scalar, "rest", 2)
+        wt_scale = keep.tile([P, V_GROUPS, HIDDEN], U8, name="wt_scale", tag="shared", align_bytes=256)
+        load_scales(wt_scale, wt_scales)
+        load_wt(0, 2)
+        load_wt(2, 2)
+        load_target(2)
+        load_target(3)
         interleave(1)
-        quantise_h("outlier", 1)
         quantise_h("rest", 1)
+        quantise_h("outlier", 1)
+        quantise_h("rest", 2)
         negate_norm()
-        for t in range(2):
-            widen_vector(2, t)
+        quantise_w(1)
         widen_scalar(2, 2)
         widen_scalar(2, 3)
-        copy_vs(0)
-        quantise_w(1)
-        quantise_h("rest", 2)
-        for m in range(3):
+        copy_vs(1)
+        for m in range(2):
             logits(m, 0, ("outlier",), closes=False)
-        for m in range(3):
+        for m in range(2):
             logits(m, 0, ("rest0", "rest1"), opens=False)
-        interleave(2)
+        logits(2, 0)
         exponential(0, 0)
-        widen_scalar(3, 0)
-        widen_scalar(3, 1)
-        widen_vector(3, 2)
-        widen_vector(3, 3)
-        quantise_w(2)
+        interleave(2)
+        for t in range(2, 4):
+            widen_scalar(3, t)
         subtract(0, 0)
+        quantise_w(2)
         logits(0, 1)
-        exponential(0, 1)
         exponential(1, 0)
+        exponential(0, 1)
         exponential(2, 0)
         for m in range(1, 3):
             logits(m, 1)
@@ -358,7 +355,6 @@ def tile_cross_entropy_hidden_gradient_s3_kernel(
         logits(2, 2)
         logits(0, 3)
         exponential(0, 2)
-        copy_vs(1)
         exponential(1, 2)
         exponential(0, 3)
         subtract(0, 2)

@@ -63,13 +63,13 @@ def tile_cross_entropy_hidden_gradient_s3_kernel(
         norm = kept([P, M_TILES], BF16, "norm")
         w_scale = kept([P, 4], F32, "w_scale")
         w_bytes = [kept([P, 2, VOCAB], U8, "w_bytes%d" % i) for i in range(2)]
-        wr = kept([P, 2, 2 * VOCAB], U8, "wr")
+        wr = [kept([P, 2, 2 * N], U8, "wr%d" % g) for g in range(V_GROUPS)]
         h_first = keep.tile([P, 3 * REST_CH], BF16, name="h_first", tag="shared", align_bytes=256)
         rest = [h_first[:, 0:REST_CH], h_first[:, REST_CH:2 * REST_CH]]
         rest = rest + [kept([P, REST_CH], BF16, "rest%d" % m)[:] for m in range(2, M_TILES)]
         outlier = [h_first[:, 2 * REST_CH:3 * REST_CH], kept([P, 2 * OUT_CH], BF16, "outlier1")[:]]
         target = [kept([P, VOCAB], BF16, "target%d" % m) for m in range(M_TILES)]
-        wt = kept([P, V_GROUPS, 2 * HIDDEN], U8, "wt")
+        wt = [kept([P, 2, 2 * HIDDEN], U8, "wt%d" % i) for i in range(2)]
 
         w_view = w_out_bytes.rearrange("(p t) v -> p t v", t=4)
         wr_view = w_rest_words.rearrange("g p n -> p g n")
@@ -88,8 +88,8 @@ def tile_cross_entropy_hidden_gradient_s3_kernel(
         def load_bytes(i):
             load(w_bytes[i][:], w_view[:, 2 * i:2 * i + 2, :])
 
-        def load_wr(g, count=1):
-            load(wr[:, :, cols(2 * g, 2 * count)], wr_view[:, :, cols(2 * g, 2 * count)])
+        def load_wr(g):
+            load(wr[g][:], wr_view[:, :, cols(2 * g, 2)])
 
         def load_wr_scales(i):
             load_scales(wr_scale[i], w_rest_scales[:, :, cols(2 * i, 2)])
@@ -103,8 +103,8 @@ def tile_cross_entropy_hidden_gradient_s3_kernel(
         def load_target(m, g=0, count=V_GROUPS):
             load(target[m][:, cols(g, count)], target_view[:, m, cols(g, count)])
 
-        def load_wt(g, count):
-            load(wt[:, g:g + count, :], wt_words[g:g + count].rearrange("g p n -> p g n"))
+        def load_wt(i):
+            load(wt[i][:], wt_words[2 * i:2 * i + 2].rearrange("g p n -> p g n"))
 
         load_bytes(0)
         load(w_scale[:], w_out_scale.rearrange("(p t) o -> p (t o)", t=4))
@@ -218,7 +218,7 @@ def tile_cross_entropy_hidden_gradient_s3_kernel(
                     moving, moving_scale = w_codes[g][:].bitcast(E4M3_X4), w_codes_scale[g][:]
                 else:
                     pair, j = ("rest", m), int(name[-1])
-                    moving, moving_scale = wr[:, j, cols(2 * g, 2)].bitcast(E2M1_X4), wr_scale[g // 2][:, j, cols(g % 2)]
+                    moving, moving_scale = wr[g][:, j, :].bitcast(E2M1_X4), wr_scale[g // 2][:, j, cols(g % 2)]
                 nc.tensor.matmul_mx(
                     out=z_bank[m, g][:], lhsT=h_codes[pair][:, j, :].bitcast(E4M3_X4), lhsT_scale=h_scale[pair][:, j, :],
                     rhs=moving, rhs_scale=moving_scale,
@@ -275,7 +275,7 @@ def tile_cross_entropy_hidden_gradient_s3_kernel(
                     nc.tensor.matmul_mx(
                         out=o_bank[m, first][:, c:c + step],
                         lhsT=g_codes[m][:, g, :].bitcast(E4M3_X4), lhsT_scale=g_scale[m][:, g, :],
-                        rhs=wt[:, g, 2 * d0:2 * (d0 + step)].bitcast(E2M1_X4), rhs_scale=wt_scale[:, g, d0:d0 + step],
+                        rhs=wt[g // 2][:, g % 2, 2 * d0:2 * (d0 + step)].bitcast(E2M1_X4), rhs_scale=wt_scale[:, g, d0:d0 + step],
                         start=(g == 0), stop=(g == V_GROUPS - 1))
 
         def store(copy, m, first, width=N, skip=0):
@@ -315,8 +315,8 @@ def tile_cross_entropy_hidden_gradient_s3_kernel(
         copy_h(scalar, "rest", 2)
         wt_scale = keep.tile([P, V_GROUPS, HIDDEN], U8, name="wt_scale", tag="shared", align_bytes=256)
         load_scales(wt_scale, wt_scales)
-        load_wt(0, 2)
-        load_wt(2, 2)
+        load_wt(0)
+        load_wt(1)
         load_target(2)
         load_target(3)
         interleave(1)

@@ -202,6 +202,12 @@ def tile_cross_entropy_hidden_gradient_s3_kernel(
                 nc.tensor.matmul(vs_bank[g // 2][:, rows(row % 8)], lhsT=ident_bf[:, row:row + 1].to_broadcast([P, P]),
                                  rhs=vs_rows[:], start=True, stop=True)
 
+        warm_bank = sum_psum.tile([P, N], F32, name="warm_bank", tag="sum")
+
+        def warm_up():
+            nc.tensor.matmul(warm_bank[:].rearrange("p (a c) -> p a c", a=4), lhsT=ident_bf[:],
+                             rhs=ident_bf[:].unsqueeze(1).to_broadcast([P, 4, P]), start=True, stop=True)
+
         def copy_vs(half):
             nc.scalar.copy(out=vs[:, cols(2 * half, 2)].bitcast(F32).rearrange("q (u w) -> q u w", u=2),
                            in_=vs_bank[half][:].bitcast(F32).rearrange("q (w u) -> q u w", u=2))
@@ -299,6 +305,7 @@ def tile_cross_entropy_hidden_gradient_s3_kernel(
         copy_vs(0)
         transpose_h("rest", 0)
         transpose_h("outlier", 0)
+        warm_up()
         copy_h(scalar, "rest", 0)
         copy_h(scalar, "outlier", 0)
         widen_vector(3, 0)
@@ -308,8 +315,10 @@ def tile_cross_entropy_hidden_gradient_s3_kernel(
         quantise_h("rest", 0)
         quantise_h("outlier", 0)
         transpose_h("rest", 1)
+        warm_up()
         transpose_h("outlier", 1)
         copy_h(scalar, "rest", 1)
+        warm_up()
         transpose_h("rest", 2)
         copy_h(scalar, "outlier", 1)
         copy_h(scalar, "rest", 2)

@@ -264,6 +264,12 @@ def tile_cross_entropy_hidden_gradient_s3_kernel(
             copy(out=g_grouped[m][:, g:g + count].bitcast(F32),
                  in_=g_bank[m, g][:, 0:2 * count, :].rearrange("p (g u) r -> p g r u", u=2))
 
+        def split_copy(copy, m, g):
+            if m not in g_grouped:
+                g_grouped[m] = grad_pool.tile([P, V_GROUPS, P, 4], BF16, name="g_grouped", align_bytes=256)
+            for j in range(2):
+                copy(out=g_grouped[m][:, g + j].bitcast(F32), in_=g_bank[m, g][:, 2 * j:2 * j + 2, :].rearrange("p u r -> p r u"))
+
         def quantise_e(m, g, count):
             groups = slice(g, g + count)
             nc.vector.quantize_mx(out=g_codes[m][:, groups].rearrange("p g r -> p (g r)").bitcast(E4M3_X4),
@@ -369,31 +375,29 @@ def tile_cross_entropy_hidden_gradient_s3_kernel(
         subtract(0, 2)
         subtract(1, 0, 2)
         subtract(0, 3)
-        logits(1, 3)
-        multiply(0, 2)
-        multiply(0, 3)
         transpose_h("rest", 3)
         transpose_e(0, 0)
         copy_h(scalar, "rest", 3)
         copy_e(scalar, 0, 0)
-        exponential(1, 3)
+        logits(1, 3)
         exponential(2, 2)
         logits(2, 3)
-        transpose_e(0, 2)
         quantise_h("rest", 3)
-        multiply(1, 0)
+        multiply(0, 2, 2)
+        exponential(1, 3)
+        exponential(2, 3)
         quantise_e(0, 0, 2)
-        multiply(1, 1)
-        copy_e(scalar, 0, 2)
         subtract(1, 2, 2)
         logits(3, 0)
-        quantise_e(0, 2, 2)
-        exponential(2, 3)
+        transpose_e(0, 2)
         logits(3, 1)
+        exponential(3, 0)
+        copy_e(scalar, 0, 2)
+        exponential(3, 1)
+        multiply(1, 0, 2)
+        quantise_e(0, 2, 2)
         for d in range(D_GROUPS):
             product(0, d * N, groups=range(2))
-        exponential(3, 0)
-        exponential(3, 1)
         multiply(1, 2, 2)
         for d in range(D_GROUPS):
             product(0, d * N, groups=range(2, 4))
@@ -419,36 +423,39 @@ def tile_cross_entropy_hidden_gradient_s3_kernel(
             product(1, 0, groups=groups)
             product(1, N, groups=groups)
         subtract(3, 0, 2)
-        subtract(3, 2)
         store(scalar, 1, 0)
         transpose_e(2, 0)
         transpose_e(2, 2)
-        copy_e(scalar, 2, 0)
+        split_copy(scalar, 2, 0)
         copy_e(scalar, 2, 2)
         product(1, 2 * N)
-        subtract(3, 3)
-        quantise_e(2, 0, 2)
+        subtract(3, 2, 2)
+        quantise_e(2, 0, 1)
+        quantise_e(2, 1, 1)
+        multiply(3, 0)
         quantise_e(2, 2, 2)
-        multiply(3, 0, 2)
+        multiply(3, 1)
         multiply(3, 2, 2)
         store(scalar, 1, N)
         store(scalar, 1, 2 * N)
-        for groups in (range(2), range(2, 4)):
+        for groups in (range(1), range(1, 2), range(2, 4)):
             product(2, 0, groups=groups)
             product(2, N, groups=groups)
         store(scalar, 2, 0)
         transpose_e(3, 0)
         transpose_e(3, 2)
-        copy_e(vector, 3, 0)
+        split_copy(vector, 3, 0)
         copy_e(scalar, 3, 2)
         product(2, 2 * N)
-        quantise_e(3, 0, 2)
+        quantise_e(3, 0, 1)
+        quantise_e(3, 1, 1)
         quantise_e(3, 2, 2)
         store(scalar, 2, N)
         store(vector, 2, 2 * N)
-        product(3, 0)
+        for groups in (range(1), range(1, 2), range(2, 4)):
+            product(3, 0, groups=groups)
+            product(3, N, groups=groups)
         store(scalar, 3, 0)
-        product(3, N)
         store(vector, 3, N)
         product(3, 2 * N)
         store(scalar, 3, 2 * N, 2 * P)

@@ -62,7 +62,9 @@ def tile_cross_entropy_hidden_gradient_s3_kernel(
 
         norm = kept([P, M_TILES], BF16, "norm")
         w_scale = kept([P, 4], F32, "w_scale")
-        w_bytes = [kept([P, 2, VOCAB], U8, "w_bytes%d" % i) for i in range(2)]
+        w_first = [kept([P, VOCAB], U8, "w_first%d" % t) for t in range(2)]
+        w_second = kept([P, 2, VOCAB], U8, "w_second")
+        w_plane = [w_first[0][:], w_first[1][:], w_second[:, 0, :], w_second[:, 1, :]]
         wr = [kept([P, 2, 2 * N], U8, "wr%d" % g) for g in range(V_GROUPS)]
         h_first = keep.tile([P, 3 * REST_CH], BF16, name="h_first", tag="shared", align_bytes=256)
         rest = [h_first[:, 0:REST_CH], h_first[:, REST_CH:2 * REST_CH]]
@@ -85,9 +87,6 @@ def tile_cross_entropy_hidden_gradient_s3_kernel(
             for r in range(4):
                 load(plane[r:P:32].bitcast(I32), source[:, r:16:4, :].bitcast(I32).rearrange("g q n -> q g n"))
 
-        def load_bytes(i):
-            load(w_bytes[i][:], w_view[:, 2 * i:2 * i + 2, :])
-
         def load_wr(g):
             load(wr[g][:], wr_view[:, :, cols(2 * g, 2)])
 
@@ -106,10 +105,11 @@ def tile_cross_entropy_hidden_gradient_s3_kernel(
         def load_wt(i):
             load(wt[i][:], wt_words[2 * i:2 * i + 2].rearrange("g p n -> p g n"))
 
-        load_bytes(0)
+        load(w_first[0][:], w_view[:, 0, :])
         load(w_scale[:], w_out_scale.rearrange("(p t) o -> p (t o)", t=4))
+        load(w_first[1][:], w_view[:, 1, :])
         load(vs_rows[0:VS_ROWS, :], vocab_scale.rearrange("(r c) -> r c", c=P))
-        load_bytes(1)
+        load(w_second[:], w_view[:, 2:4, :])
         load_rest(0)
         load_outlier(0)
         load_rest(1)
@@ -127,27 +127,24 @@ def tile_cross_entropy_hidden_gradient_s3_kernel(
         load_target(1)
         load_rest(3)
 
-        wide, w_grouped = {}, {}
+        w_grouped = {}
+        wide = [kept([P, 2, 4, N], BF16, "wide%d" % half) for half in range(2)]
         w_codes = [kept([P, N], U32, "w_codes%d" % g) for g in range(V_GROUPS)]
         w_codes_scale = [kept([P, N], U8, "w_codes_scale%d" % g) for g in range(V_GROUPS)]
 
-        def wide_tile(g):
-            if g not in wide:
-                wide[g] = wide_pool.tile([P, 4, N], BF16, name="wide", align_bytes=256, bufs=V_GROUPS)
-            return wide[g]
-
-        def widen_vector(g, t):
-            nc.vector.tensor_scalar(out=wide_tile(g)[:, t, :], in0=w_bytes[t // 2][:, t % 2, cols(g)].bitcast(E4M3FN),
+        def widen_vector(g, t, count=1):
+            nc.vector.tensor_scalar(out=wide[g // 2][:, g % 2:g % 2 + count, t, :],
+                                    in0=w_plane[t][:, cols(g, count)].bitcast(E4M3FN).rearrange("p (j v) -> p j v", j=count),
                                     scalar1=w_scale[:, t:t + 1], scalar2=None, op0=MULT)
 
         def widen_scalar(g, t):
-            nc.scalar.activation(out=wide_tile(g)[:, t, :], in_=w_bytes[t // 2][:, t % 2, cols(g)].bitcast(E4M3FN), func=COPY,
+            nc.scalar.activation(out=wide[g // 2][:, g % 2, t, :], in_=w_plane[t][:, cols(g)].bitcast(E4M3FN), func=COPY,
                                  scale=w_scale[:, t:t + 1])
 
         def interleave(g):
             w_grouped[g] = wide_pool.tile([P, N, 4], BF16, name="w_grouped", align_bytes=256)
             nc.vector.tensor_copy(out=w_grouped[g][:].rearrange("p (c i) t -> p c t i", i=4),
-                                  in_=wide[g][:].rearrange("p t (c i) -> p c t i", i=4))
+                                  in_=wide[g // 2][:, g % 2].rearrange("p t (c i) -> p c t i", i=4))
 
         def quantise_w(g):
             nc.vector.quantize_mx(out=w_codes[g][:].bitcast(E4M3_X4), scales=w_codes_scale[g][:],
@@ -297,15 +294,17 @@ def tile_cross_entropy_hidden_gradient_s3_kernel(
 
         scalar, vector = nc.scalar.copy, nc.vector.tensor_copy
 
-        for g in range(2):
-            for t in range(2):
-                widen_vector(g, t)
+        widen_vector(0, 0, 2)
         widen_scalar(2, 0)
-        widen_scalar(2, 1)
+        widen_scalar(3, 0)
+        widen_vector(0, 1, 2)
+        widen_vector(2, 1, 2)
         widen_vector(0, 2)
-        widen_vector(0, 3)
-        widen_scalar(1, 2)
+        widen_scalar(0, 3)
         widen_scalar(1, 3)
+        widen_vector(1, 2)
+        warm_up()
+        warm_up()
         for g in range(V_GROUPS):
             spread_vs(g, sum_psum, "sum")
         copy_vs(0)
@@ -314,12 +313,11 @@ def tile_cross_entropy_hidden_gradient_s3_kernel(
         warm_up()
         copy_h(scalar, "rest", 0)
         copy_h(scalar, "outlier", 0)
-        widen_vector(3, 0)
         interleave(0)
-        widen_vector(3, 1)
+        widen_vector(2, 2)
         quantise_w(0)
-        quantise_h("rest", 0)
         quantise_h("outlier", 0)
+        quantise_h("rest", 0)
         transpose_h("rest", 1)
         warm_up()
         transpose_h("outlier", 1)
@@ -340,7 +338,6 @@ def tile_cross_entropy_hidden_gradient_s3_kernel(
         quantise_h("rest", 2)
         negate_norm()
         quantise_w(1)
-        widen_scalar(2, 2)
         widen_scalar(2, 3)
         copy_vs(1)
         for m in range(2):
@@ -365,6 +362,7 @@ def tile_cross_entropy_hidden_gradient_s3_kernel(
         subtract(0, 1)
         quantise_w(3)
         multiply(0, 0, 2)
+
         logits(0, 2)
         logits(1, 2)
         logits(2, 2)
@@ -429,30 +427,33 @@ def tile_cross_entropy_hidden_gradient_s3_kernel(
         split_copy(scalar, 2, 0)
         copy_e(scalar, 2, 2)
         product(1, 2 * N)
-        subtract(3, 2, 2)
+        subtract(3, 2)
         quantise_e(2, 0, 1)
         quantise_e(2, 1, 1)
-        multiply(3, 0)
+        multiply(3, 0, 2)
         quantise_e(2, 2, 2)
-        multiply(3, 1)
-        multiply(3, 2, 2)
+        subtract(3, 3)
+        multiply(3, 2)
+        multiply(3, 3)
         store(scalar, 1, N)
         store(scalar, 1, 2 * N)
-        for groups in (range(1), range(1, 2), range(2, 4)):
-            product(2, 0, groups=groups)
-            product(2, N, groups=groups)
-        store(scalar, 2, 0)
+        for g in range(2):
+            for d in range(D_GROUPS):
+                product(2, d * N, groups=range(g, g + 1))
         transpose_e(3, 0)
+        copy_e(scalar, 3, 0)
+        quantise_e(3, 0, 2)
+        product(2, 0, groups=range(2, 4))
+        product(2, N, groups=range(2, 4))
+        store(scalar, 2, 0)
         transpose_e(3, 2)
-        split_copy(vector, 3, 0)
-        copy_e(scalar, 3, 2)
-        product(2, 2 * N)
-        quantise_e(3, 0, 1)
-        quantise_e(3, 1, 1)
-        quantise_e(3, 2, 2)
+        split_copy(vector, 3, 2)
+        quantise_e(3, 2, 1)
+        quantise_e(3, 3, 1)
+        product(2, 2 * N, groups=range(2, 4))
         store(scalar, 2, N)
-        store(vector, 2, 2 * N)
-        for groups in (range(1), range(1, 2), range(2, 4)):
+        store(scalar, 2, 2 * N)
+        for groups in (range(2), range(2, 4)):
             product(3, 0, groups=groups)
             product(3, N, groups=groups)
         store(scalar, 3, 0)

@@ -37,8 +37,9 @@ def tile_cross_entropy_hidden_gradient_s3_kernel(
         wide_pool = ctx.enter_context(tc.tile_pool(name="wide_pool", bufs=2))
         grad_pool = ctx.enter_context(tc.tile_pool(name="grad_pool", bufs=2))
         store_pool = ctx.enter_context(tc.tile_pool(name="store_pool", bufs=6))
-        sum_psum = ctx.enter_context(tc.psum_pool(name="sum_psum", bufs=5))
-        t_psum = ctx.enter_context(tc.psum_pool(name="t_psum", bufs=3))
+        sum_psum = ctx.enter_context(tc.psum_pool(name="sum_psum", bufs=4))
+        t_psum = ctx.enter_context(tc.psum_pool(name="t_psum", bufs=2))
+        vs_psum = ctx.enter_context(tc.psum_pool(name="vs_psum", bufs=1))
         ctx.enter_context(tc.manual_schedule())
 
         def kept(shape, dtype, name):
@@ -113,8 +114,8 @@ def tile_cross_entropy_hidden_gradient_s3_kernel(
         load_rest(0)
         load_outlier(0)
         load_rest(1)
-        load_outlier(1)
         load_rest(2)
+        load_outlier(1)
         load_wr_scales(0)
         load_wr(0)
         load(norm[:], log_norm.rearrange("(p m) -> p m", m=M_TILES))
@@ -141,10 +142,11 @@ def tile_cross_entropy_hidden_gradient_s3_kernel(
             nc.scalar.activation(out=wide[g // 2][:, g % 2, t, :], in_=w_plane[t][:, cols(g)].bitcast(E4M3FN), func=COPY,
                                  scale=w_scale[:, t:t + 1])
 
-        def interleave(g):
-            w_grouped[g] = wide_pool.tile([P, N, 4], BF16, name="w_grouped", align_bytes=256)
-            nc.vector.tensor_copy(out=w_grouped[g][:].rearrange("p (c i) t -> p c t i", i=4),
-                                  in_=wide[g // 2][:, g % 2].rearrange("p t (c i) -> p c t i", i=4))
+        def interleave(g, copy=nc.vector.tensor_copy, first=0, width=N):
+            if g not in w_grouped:
+                w_grouped[g] = wide_pool.tile([P, N, 4], BF16, name="w_grouped", align_bytes=256)
+            copy(out=w_grouped[g][:, first:first + width].rearrange("p (c i) t -> p c t i", i=4),
+                 in_=wide[g // 2][:, g % 2, :, first:first + width].rearrange("p t (c i) -> p c t i", i=4))
 
         def quantise_w(g):
             nc.vector.quantize_mx(out=w_codes[g][:].bitcast(E4M3_X4), scales=w_codes_scale[g][:],
@@ -161,8 +163,8 @@ def tile_cross_entropy_hidden_gradient_s3_kernel(
             h_codes[kind, i] = kept([P, 2, P], U32, "h_codes_%s%d" % (kind, i))
             h_scale[kind, i] = kept([P, 2, P], U8, "h_scale_%s%d" % (kind, i))
 
-        def transpose_h(*pair):
-            bank = t_psum.tile([P, 4, P], F32, name="t_bank", tag="t")
+        def transpose_h(*pair, pool=t_psum, tag="t"):
+            bank = pool.tile([P, 4, P], F32, name="t_bank", tag=tag)
             h_bank[pair] = bank
             words = h_source[pair][:].bitcast(F32)
             for j in range(2):
@@ -178,8 +180,7 @@ def tile_cross_entropy_hidden_gradient_s3_kernel(
                                   in_=h_grouped[pair][:].rearrange("p j r t -> p (j r t)"))
 
         minus_norm = kept([P, M_TILES], F32, "minus_norm")
-        vs = kept([P, VOCAB], BF16, "vs")
-        vs_bank = {}
+        vs_bank = [vs_psum.tile([P, 2 * N], BF16, name="vs_bank%d" % half) for half in range(2)]
 
         def word_order(natural):
             return natural.rearrange("q (w u e) -> q u w e", u=2, e=2)
@@ -191,23 +192,18 @@ def tile_cross_entropy_hidden_gradient_s3_kernel(
         def negate_norm():
             nc.vector.tensor_scalar(out=minus_norm[:], in0=norm[:], scalar1=-1.0, scalar2=None, op0=MULT)
 
-        def spread_vs(g, pool, tag):
-            if g % 2 == 0:
-                vs_bank[g // 2] = pool.tile([P, 2 * N], BF16, name="vs_bank", tag=tag)
+        def spread_vs(g):
             for r in range(4):
                 row = 4 * g + r
-                nc.tensor.matmul(vs_bank[g // 2][:, rows(row % 8)], lhsT=ident_bf[:, row:row + 1].to_broadcast([P, P]),
-                                 rhs=vs_rows[:], start=True, stop=True)
+                runs = vs_bank[g // 2][:].rearrange("q (u r c) -> q u r c", u=2, r=8)
+                nc.tensor.matmul(runs[:, :, row % 8, :], lhsT=ident_bf[:, row:row + 1].to_broadcast([P, P]),
+                                 rhs=word_order(vs_rows[:]), start=True, stop=True)
 
         warm_bank = sum_psum.tile([P, N], F32, name="warm_bank", tag="sum")
 
         def warm_up():
             nc.tensor.matmul(warm_bank[:].rearrange("p (a c) -> p a c", a=4), lhsT=ident_bf[:],
                              rhs=ident_bf[:].unsqueeze(1).to_broadcast([P, 4, P]), start=True, stop=True)
-
-        def copy_vs(half):
-            nc.scalar.copy(out=vs[:, cols(2 * half, 2)].bitcast(F32).rearrange("q (u w) -> q u w", u=2),
-                           in_=vs_bank[half][:].bitcast(F32).rearrange("q (w u) -> q u w", u=2))
 
         z_bank, grad = {}, {}
         e_tile = [kept([P, VOCAB], F32, "e%d" % m) for m in range(M_TILES)]
@@ -239,7 +235,7 @@ def tile_cross_entropy_hidden_gradient_s3_kernel(
             if m not in grad:
                 grad[m] = grad_pool.tile([P, VOCAB], BF16, name="grad", align_bytes=256)
             nc.vector.tensor_tensor(out=stored(grad[m], g, count), in0=stored(e_tile[m], g, count),
-                                    in1=stored(vs, g, count), op=MULT)
+                                    in1=stored(vs_bank[g // 2], g % 2, count), op=MULT)
 
         g_grouped = {}
         g_codes = [kept([P, V_GROUPS, P], U32, "g_codes%d" % m) for m in range(M_TILES)]
@@ -302,12 +298,12 @@ def tile_cross_entropy_hidden_gradient_s3_kernel(
         widen_vector(0, 2)
         widen_scalar(0, 3)
         widen_scalar(1, 3)
+        widen_scalar(3, 3)
         widen_vector(1, 2)
         warm_up()
         warm_up()
         for g in range(V_GROUPS):
-            spread_vs(g, sum_psum, "sum")
-        copy_vs(0)
+            spread_vs(g)
         transpose_h("rest", 0)
         transpose_h("outlier", 0)
         warm_up()
@@ -318,28 +314,28 @@ def tile_cross_entropy_hidden_gradient_s3_kernel(
         quantise_w(0)
         quantise_h("outlier", 0)
         quantise_h("rest", 0)
-        transpose_h("rest", 1)
-        warm_up()
-        transpose_h("outlier", 1)
-        copy_h(scalar, "rest", 1)
+        transpose_h("rest", 1, pool=sum_psum, tag="sum")
         warm_up()
         transpose_h("rest", 2)
-        copy_h(scalar, "outlier", 1)
+        copy_h(scalar, "rest", 1)
+        warm_up()
+        transpose_h("outlier", 1)
         copy_h(scalar, "rest", 2)
+        copy_h(scalar, "outlier", 1)
         wt_scale = keep.tile([P, V_GROUPS, HIDDEN], U8, name="wt_scale", tag="shared", align_bytes=256)
         load_scales(wt_scale, wt_scales)
         load_wt(0)
         load_wt(1)
         load_target(2)
         load_target(3)
-        interleave(1)
         quantise_h("rest", 1)
-        quantise_h("outlier", 1)
+        interleave(1)
         quantise_h("rest", 2)
+        quantise_h("outlier", 1)
         negate_norm()
         quantise_w(1)
         widen_scalar(2, 3)
-        copy_vs(1)
+        widen_scalar(3, 2)
         for m in range(2):
             logits(m, 0, ("outlier",), closes=False)
         for m in range(2):
@@ -347,28 +343,29 @@ def tile_cross_entropy_hidden_gradient_s3_kernel(
         logits(2, 0)
         exponential(0, 0)
         interleave(2)
-        for t in range(2, 4):
-            widen_scalar(3, t)
+        exponential(1, 0)
         subtract(0, 0)
         quantise_w(2)
         logits(0, 1)
-        exponential(1, 0)
-        exponential(0, 1)
+        interleave(3, scalar, 0 * P, P)
         exponential(2, 0)
-        for m in range(1, 3):
-            logits(m, 1)
-            exponential(m, 1)
-        interleave(3)
+        exponential(0, 1)
+        logits(1, 1)
+        exponential(1, 1)
+        logits(2, 1)
+        exponential(2, 1)
+        interleave(3, vector, 1 * P, 3 * P)
         subtract(0, 1)
         quantise_w(3)
         multiply(0, 0, 2)
 
         logits(0, 2)
+        exponential(0, 2)
         logits(1, 2)
+        exponential(1, 2)
         logits(2, 2)
         logits(0, 3)
-        exponential(0, 2)
-        exponential(1, 2)
+        exponential(2, 2)
         exponential(0, 3)
         subtract(0, 2)
         subtract(1, 0, 2)
@@ -378,7 +375,6 @@ def tile_cross_entropy_hidden_gradient_s3_kernel(
         copy_h(scalar, "rest", 3)
         copy_e(scalar, 0, 0)
         logits(1, 3)
-        exponential(2, 2)
         logits(2, 3)
         quantise_h("rest", 3)
         multiply(0, 2, 2)
@@ -427,33 +423,30 @@ def tile_cross_entropy_hidden_gradient_s3_kernel(
         split_copy(scalar, 2, 0)
         copy_e(scalar, 2, 2)
         product(1, 2 * N)
-        subtract(3, 2)
+        subtract(3, 2, 2)
         quantise_e(2, 0, 1)
         quantise_e(2, 1, 1)
-        multiply(3, 0, 2)
+        multiply(3, 0)
         quantise_e(2, 2, 2)
-        subtract(3, 3)
-        multiply(3, 2)
-        multiply(3, 3)
+        multiply(3, 1)
+        multiply(3, 2, 2)
         store(scalar, 1, N)
         store(scalar, 1, 2 * N)
-        for g in range(2):
-            for d in range(D_GROUPS):
-                product(2, d * N, groups=range(g, g + 1))
-        transpose_e(3, 0)
-        copy_e(scalar, 3, 0)
-        quantise_e(3, 0, 2)
-        product(2, 0, groups=range(2, 4))
-        product(2, N, groups=range(2, 4))
+        for groups in (range(1), range(1, 2), range(2, 4)):
+            product(2, 0, groups=groups)
+            product(2, N, groups=groups)
         store(scalar, 2, 0)
+        transpose_e(3, 0)
         transpose_e(3, 2)
-        split_copy(vector, 3, 2)
-        quantise_e(3, 2, 1)
-        quantise_e(3, 3, 1)
-        product(2, 2 * N, groups=range(2, 4))
+        split_copy(vector, 3, 0)
+        copy_e(scalar, 3, 2)
+        product(2, 2 * N)
+        quantise_e(3, 0, 1)
+        quantise_e(3, 1, 1)
+        quantise_e(3, 2, 2)
         store(scalar, 2, N)
-        store(scalar, 2, 2 * N)
-        for groups in (range(2), range(2, 4)):
+        store(vector, 2, 2 * N)
+        for groups in (range(1), range(1, 2), range(2, 4)):
             product(3, 0, groups=groups)
             product(3, N, groups=groups)
         store(scalar, 3, 0)

@@ -25,6 +25,7 @@ M_TILES = TOKENS // P
 V_GROUPS = VOCAB // N
 D_GROUPS = HIDDEN // N
 VS_ROWS = VOCAB // P
+WR_LOADS = {0: 1, 1: 1, 2: 2}
 
 
 def tile_cross_entropy_hidden_gradient_s3_kernel(
@@ -66,7 +67,7 @@ def tile_cross_entropy_hidden_gradient_s3_kernel(
         w_first = [kept([P, VOCAB], U8, "w_first%d" % t) for t in range(2)]
         w_second = kept([P, 2, VOCAB], U8, "w_second")
         w_plane = [w_first[0][:], w_first[1][:], w_second[:, 0, :], w_second[:, 1, :]]
-        wr = [kept([P, 2, 2 * N], U8, "wr%d" % g) for g in range(V_GROUPS)]
+        wr = {g: kept([P, 2, 2 * N * count], U8, "wr%d" % g) for g, count in WR_LOADS.items()}
         h_first = keep.tile([P, 3 * REST_CH], BF16, name="h_first", tag="shared", align_bytes=256)
         rest = [h_first[:, 0:REST_CH], h_first[:, REST_CH:2 * REST_CH]]
         rest = rest + [kept([P, REST_CH], BF16, "rest%d" % m)[:] for m in range(2, M_TILES)]
@@ -89,7 +90,7 @@ def tile_cross_entropy_hidden_gradient_s3_kernel(
                 load(plane[r:P:32].bitcast(I32), source[:, r:16:4, :].bitcast(I32).rearrange("g q n -> q g n"))
 
         def load_wr(g):
-            load(wr[g][:], wr_view[:, :, cols(2 * g, 2)])
+            load(wr[g][:], wr_view[:, :, cols(2 * g, 2 * WR_LOADS[g])])
 
         def load_wr_scales(i):
             load_scales(wr_scale[i], w_rest_scales[:, :, cols(2 * i, 2)])
@@ -123,7 +124,6 @@ def tile_cross_entropy_hidden_gradient_s3_kernel(
         load_target(0, 0, 2)
         load_wr_scales(1)
         load_wr(2)
-        load_wr(3)
         load_target(0, 2, 2)
         load_target(1)
         load_rest(3)
@@ -159,7 +159,8 @@ def tile_cross_entropy_hidden_gradient_s3_kernel(
             h_source["outlier", i] = outlier[i]
         h_grouped, h_codes, h_scale, h_bank = {}, {}, {}, {}
         for kind, i in h_source:
-            h_grouped[kind, i] = kept([P, 2, P, 4], BF16, "h_grouped_%s%d" % (kind, i))
+            h_grouped[kind, i] = keep.tile([P, 2, P, 4], BF16, name="h_grouped_%s%d" % (kind, i), tag="grouped_%s%d" % (kind, i),
+                                           align_bytes=256)
             h_codes[kind, i] = kept([P, 2, P], U32, "h_codes_%s%d" % (kind, i))
             h_scale[kind, i] = kept([P, 2, P], U8, "h_scale_%s%d" % (kind, i))
 
@@ -205,7 +206,7 @@ def tile_cross_entropy_hidden_gradient_s3_kernel(
             nc.tensor.matmul(warm_bank[:].rearrange("p (a c) -> p a c", a=4), lhsT=ident_bf[:],
                              rhs=ident_bf[:].unsqueeze(1).to_broadcast([P, 4, P]), start=True, stop=True)
 
-        z_bank, grad = {}, {}
+        z_bank, grad, side = {}, {}, {}
         e_tile = [kept([P, VOCAB], F32, "e%d" % m) for m in range(M_TILES)]
 
         def logits(m, g, passes=("rest0", "rest1", "outlier"), opens=True, closes=True):
@@ -217,7 +218,9 @@ def tile_cross_entropy_hidden_gradient_s3_kernel(
                     moving, moving_scale = w_codes[g][:].bitcast(E4M3_X4), w_codes_scale[g][:]
                 else:
                     pair, j = ("rest", m), int(name[-1])
-                    moving, moving_scale = wr[g][:, j, :].bitcast(E2M1_X4), wr_scale[g // 2][:, j, cols(g % 2)]
+                    first = max(f for f in WR_LOADS if f <= g)
+                    moving = wr[first][:, j, cols(2 * (g - first), 2)].bitcast(E2M1_X4)
+                    moving_scale = wr_scale[g // 2][:, j, cols(g % 2)]
                 nc.tensor.matmul_mx(
                     out=z_bank[m, g][:], lhsT=h_codes[pair][:, j, :].bitcast(E4M3_X4), lhsT_scale=h_scale[pair][:, j, :],
                     rhs=moving, rhs_scale=moving_scale,
@@ -231,10 +234,15 @@ def tile_cross_entropy_hidden_gradient_s3_kernel(
             e = stored(e_tile[m], g, count)
             nc.vector.tensor_tensor(out=e, in0=e, in1=word_order(target[m][:, cols(g, count)]), op=SUBTRACT)
 
+        def subtract_gpsimd(m, g, tag):
+            side[m, g] = keep.tile([P, 2, P, 2], F32, name="side", tag=tag, align_bytes=256)
+            nc.gpsimd.tensor_tensor(out=side[m, g][:], in0=stored(e_tile[m], g, 1), in1=word_order(target[m][:, cols(g)]),
+                                    op=SUBTRACT)
+
         def multiply(m, g, count=1):
             if m not in grad:
                 grad[m] = grad_pool.tile([P, VOCAB], BF16, name="grad", align_bytes=256)
-            nc.vector.tensor_tensor(out=stored(grad[m], g, count), in0=stored(e_tile[m], g, count),
+            nc.vector.tensor_tensor(out=stored(grad[m], g, count), in0=side[m, g][:] if (m, g) in side else stored(e_tile[m], g, count),
                                     in1=stored(vs_bank[g // 2], g % 2, count), op=MULT)
 
         g_grouped = {}
@@ -251,23 +259,24 @@ def tile_cross_entropy_hidden_gradient_s3_kernel(
                     run = (g + j) // 2 * 4 + 2 * u + (g + j) % 2
                     nc.tensor.transpose(bank[:, 2 * j + u, :], words[:, rows(run)], ident[:])
 
-        def copy_e(copy, m, g, count=2):
-            if m not in g_grouped:
-                g_grouped[m] = grad_pool.tile([P, V_GROUPS, P, 4], BF16, name="g_grouped", align_bytes=256)
-            copy(out=g_grouped[m][:, g:g + count].bitcast(F32),
-                 in_=g_bank[m, g][:, 0:2 * count, :].rearrange("p (g u) r -> p g r u", u=2))
+        def grouped(m, g):
+            if (m, g // 2) not in g_grouped:
+                g_grouped[m, g // 2] = keep.tile([P, 2, P, 4], BF16, name="g_grouped", tag="grouped_%d%d" % (m % 2, g // 2),
+                                                 align_bytes=256)
+            return g_grouped[m, g // 2]
+
+        def copy_e(copy, m, g):
+            copy(out=grouped(m, g)[:].bitcast(F32), in_=g_bank[m, g][:].rearrange("p (g u) r -> p g r u", u=2))
 
         def split_copy(copy, m, g):
-            if m not in g_grouped:
-                g_grouped[m] = grad_pool.tile([P, V_GROUPS, P, 4], BF16, name="g_grouped", align_bytes=256)
             for j in range(2):
-                copy(out=g_grouped[m][:, g + j].bitcast(F32), in_=g_bank[m, g][:, 2 * j:2 * j + 2, :].rearrange("p u r -> p r u"))
+                copy(out=grouped(m, g)[:, j].bitcast(F32), in_=g_bank[m, g][:, 2 * j:2 * j + 2, :].rearrange("p u r -> p r u"))
 
         def quantise_e(m, g, count):
             groups = slice(g, g + count)
             nc.vector.quantize_mx(out=g_codes[m][:, groups].rearrange("p g r -> p (g r)").bitcast(E4M3_X4),
                                   scales=g_scale[m][:, groups].rearrange("p g r -> p (g r)"),
-                                  in_=g_grouped[m][:, groups].rearrange("p g r t -> p (g r t)"))
+                                  in_=grouped(m, g)[:, g % 2:g % 2 + count].rearrange("p g r t -> p (g r t)"))
 
         o_bank = {}
 
@@ -325,8 +334,9 @@ def tile_cross_entropy_hidden_gradient_s3_kernel(
         wt_scale = keep.tile([P, V_GROUPS, HIDDEN], U8, name="wt_scale", tag="shared", align_bytes=256)
         load_scales(wt_scale, wt_scales)
         load_wt(0)
+        load_target(2, 0, 2)
         load_wt(1)
-        load_target(2)
+        load_target(2, 2, 2)
         load_target(3)
         quantise_h("rest", 1)
         interleave(1)
@@ -368,7 +378,7 @@ def tile_cross_entropy_hidden_gradient_s3_kernel(
         exponential(2, 2)
         exponential(0, 3)
         subtract(0, 2)
-        subtract(1, 0, 2)
+        subtract(1, 0)
         subtract(0, 3)
         transpose_h("rest", 3)
         transpose_e(0, 0)
@@ -380,6 +390,7 @@ def tile_cross_entropy_hidden_gradient_s3_kernel(
         multiply(0, 2, 2)
         exponential(1, 3)
         exponential(2, 3)
+        subtract(1, 1)
         quantise_e(0, 0, 2)
         subtract(1, 2, 2)
         logits(3, 0)
@@ -388,8 +399,9 @@ def tile_cross_entropy_hidden_gradient_s3_kernel(
         exponential(3, 0)
         copy_e(scalar, 0, 2)
         exponential(3, 1)
-        multiply(1, 0, 2)
         quantise_e(0, 2, 2)
+        subtract_gpsimd(2, 0, "grouped_01")
+        multiply(1, 0, 2)
         for d in range(D_GROUPS):
             product(0, d * N, groups=range(2))
         multiply(1, 2, 2)
@@ -399,24 +411,25 @@ def tile_cross_entropy_hidden_gradient_s3_kernel(
         store(scalar, 0, N)
         transpose_e(1, 0)
         transpose_e(1, 2)
-        subtract(2, 0, 2)
+        subtract(2, 1)
         subtract(2, 2, 2)
-        multiply(2, 0)
+        subtract(3, 1)
         copy_e(scalar, 1, 0)
         copy_e(scalar, 1, 2)
         store(scalar, 0, 2 * N)
         logits(3, 2)
         logits(3, 3)
         quantise_e(1, 0, 2)
-        multiply(2, 1)
         quantise_e(1, 2, 2)
+        subtract_gpsimd(3, 0, "grouped_11")
+        multiply(2, 0)
+        multiply(2, 1)
         multiply(2, 2, 2)
         exponential(3, 2)
         exponential(3, 3)
         for groups in (range(2), range(2, 4)):
             product(1, 0, groups=groups)
             product(1, N, groups=groups)
-        subtract(3, 0, 2)
         store(scalar, 1, 0)
         transpose_e(2, 0)
         transpose_e(2, 2)

@@ -25,7 +25,10 @@ M_TILES = TOKENS // P
 V_GROUPS = VOCAB // N
 D_GROUPS = HIDDEN // N
 VS_ROWS = VOCAB // P
-WR_LOADS = {0: 1, 1: 1, 2: 2}
+HALF = 2 * N
+SPLIT = 64
+W_LOADS = [(0, 2, 0, 2), (0, 2, 2, 2), (2, 1, 0, 4), (3, 1, 0, 4)]
+WORDS = HALF // 4
 
 
 def tile_cross_entropy_hidden_gradient_s3_kernel(
@@ -35,9 +38,9 @@ def tile_cross_entropy_hidden_gradient_s3_kernel(
     nc = tc.nc
     with ExitStack() as ctx:
         keep = ctx.enter_context(tc.tile_pool(name="keep", bufs=1))
-        wide_pool = ctx.enter_context(tc.tile_pool(name="wide_pool", bufs=2))
-        grad_pool = ctx.enter_context(tc.tile_pool(name="grad_pool", bufs=2))
-        store_pool = ctx.enter_context(tc.tile_pool(name="store_pool", bufs=6))
+        wide_pool = ctx.enter_context(tc.tile_pool(name="wide_pool", bufs=3))
+        grad_pool = ctx.enter_context(tc.tile_pool(name="grad_pool", bufs=3))
+        store_pool = ctx.enter_context(tc.tile_pool(name="store_pool", bufs=8))
         sum_psum = ctx.enter_context(tc.psum_pool(name="sum_psum", bufs=4))
         t_psum = ctx.enter_context(tc.psum_pool(name="t_psum", bufs=2))
         vs_psum = ctx.enter_context(tc.psum_pool(name="vs_psum", bufs=1))
@@ -52,7 +55,7 @@ def tile_cross_entropy_hidden_gradient_s3_kernel(
         def cols(g, count=1):
             return slice(g * N, (g + count) * N)
 
-        wr_scale = [kept([P, 2, 2 * N], U8, "wr_scale%d" % i) for i in range(2)]
+        wr_scale = [kept([P, 2, HALF], U8, "wr_scale%d" % i) for i in range(2)]
         vs_rows = kept([P, P], BF16, "vs_rows")
         ident = kept([P, P], F32, "ident")
         ident_bf = kept([P, P], BF16, "ident_bf")
@@ -64,15 +67,18 @@ def tile_cross_entropy_hidden_gradient_s3_kernel(
 
         norm = kept([P, M_TILES], BF16, "norm")
         w_scale = kept([P, 4], F32, "w_scale")
-        w_first = [kept([P, VOCAB], U8, "w_first%d" % t) for t in range(2)]
-        w_second = kept([P, 2, VOCAB], U8, "w_second")
-        w_plane = [w_first[0][:], w_first[1][:], w_second[:, 0, :], w_second[:, 1, :]]
-        wr = {g: kept([P, 2, 2 * N * count], U8, "wr%d" % g) for g, count in WR_LOADS.items()}
+        w_bytes = {load: kept([P, load[3], N * load[1]], U8, "w_bytes%d%d" % (load[0], load[2])) for load in W_LOADS}
+        wr = [kept([P, 2, 2 * N], U8, "wr%d" % g) for g in range(V_GROUPS)]
         h_first = keep.tile([P, 3 * REST_CH], BF16, name="h_first", tag="shared", align_bytes=256)
         rest = [h_first[:, 0:REST_CH], h_first[:, REST_CH:2 * REST_CH]]
         rest = rest + [kept([P, REST_CH], BF16, "rest%d" % m)[:] for m in range(2, M_TILES)]
         outlier = [h_first[:, 2 * REST_CH:3 * REST_CH], kept([P, 2 * OUT_CH], BF16, "outlier1")[:]]
-        target = [kept([P, VOCAB], BF16, "target%d" % m) for m in range(M_TILES)]
+        target = {(m, half): kept([P, HALF], BF16, "target%d%d" % (m, half)) for m in (0, 2) for half in range(2)}
+        for m in (1, 3):
+            whole = kept([P, VOCAB], BF16, "target%d" % m)
+            target["whole", m] = whole
+            for half in range(2):
+                target[m, half] = whole[:, half * HALF:(half + 1) * HALF]
         wt = [kept([P, 2, 2 * HIDDEN], U8, "wt%d" % i) for i in range(2)]
 
         w_view = w_out_bytes.rearrange("(p t) v -> p t v", t=4)
@@ -89,11 +95,15 @@ def tile_cross_entropy_hidden_gradient_s3_kernel(
             for r in range(4):
                 load(plane[r:P:32].bitcast(I32), source[:, r:16:4, :].bitcast(I32).rearrange("g q n -> q g n"))
 
-        def load_wr(g):
-            load(wr[g][:], wr_view[:, :, cols(2 * g, 2 * WR_LOADS[g])])
+        def load_w(i):
+            g, groups, t, planes = W_LOADS[i]
+            load(w_bytes[W_LOADS[i]][:], w_view[:, t:t + planes, cols(g, groups)])
 
-        def load_wr_scales(i):
-            load_scales(wr_scale[i], w_rest_scales[:, :, cols(2 * i, 2)])
+        def load_wr(g):
+            load(wr[g][:], wr_view[:, :, cols(2 * g, 2)])
+
+        def load_wr_scales(half):
+            load_scales(wr_scale[half], w_rest_scales[:, :, cols(2 * half, 2)])
 
         def load_rest(m):
             load(rest[m][:], rest_view[:, m, :])
@@ -101,52 +111,41 @@ def tile_cross_entropy_hidden_gradient_s3_kernel(
         def load_outlier(i):
             load(outlier[i][:], outlier_view[:, i, :])
 
-        def load_target(m, g=0, count=V_GROUPS):
-            load(target[m][:, cols(g, count)], target_view[:, m, cols(g, count)])
+        def load_target_half(m, half):
+            load(target[m, half][:], target_view[:, m, cols(2 * half, 2)])
+
+        def load_target(m):
+            load(target["whole", m][:], target_view[:, m, :])
 
         def load_wt(i):
             load(wt[i][:], wt_words[2 * i:2 * i + 2].rearrange("g p n -> p g n"))
 
-        load(w_first[0][:], w_view[:, 0, :])
-        load(w_scale[:], w_out_scale.rearrange("(p t) o -> p (t o)", t=4))
-        load(w_first[1][:], w_view[:, 1, :])
-        load(vs_rows[0:VS_ROWS, :], vocab_scale.rearrange("(r c) -> r c", c=P))
-        load(w_second[:], w_view[:, 2:4, :])
-        load_rest(0)
-        load_outlier(0)
-        load_rest(1)
-        load_rest(2)
-        load_outlier(1)
-        load_wr_scales(0)
-        load_wr(0)
-        load(norm[:], log_norm.rearrange("(p m) -> p m", m=M_TILES))
-        load_wr(1)
-        load_target(0, 0, 2)
-        load_wr_scales(1)
-        load_wr(2)
-        load_target(0, 2, 2)
-        load_target(1)
-        load_rest(3)
-
-        w_grouped = {}
-        wide = [kept([P, 2, 4, N], BF16, "wide%d" % half) for half in range(2)]
+        wide, w_grouped = {}, {}
         w_codes = [kept([P, N], U32, "w_codes%d" % g) for g in range(V_GROUPS)]
         w_codes_scale = [kept([P, N], U8, "w_codes_scale%d" % g) for g in range(V_GROUPS)]
 
-        def widen_vector(g, t, count=1):
-            nc.vector.tensor_scalar(out=wide[g // 2][:, g % 2:g % 2 + count, t, :],
-                                    in0=w_plane[t][:, cols(g, count)].bitcast(E4M3FN).rearrange("p (j v) -> p j v", j=count),
+        def wide_plane(g, t):
+            if g not in wide:
+                wide[g] = wide_pool.tile([P, 4, N], BF16, name="wide", align_bytes=256)
+            return wide[g][:, t, :]
+
+        def w_plane(g, t):
+            load = [x for x in W_LOADS if x[0] <= g < x[0] + x[1] and x[2] <= t < x[2] + x[3]][0]
+            return w_bytes[load][:, t - load[2], cols(g - load[0])].bitcast(E4M3FN)
+
+        def widen_vector(g, t):
+            nc.vector.tensor_scalar(out=wide_plane(g, t), in0=w_plane(g, t),
                                     scalar1=w_scale[:, t:t + 1], scalar2=None, op0=MULT)
 
         def widen_scalar(g, t):
-            nc.scalar.activation(out=wide[g // 2][:, g % 2, t, :], in_=w_plane[t][:, cols(g)].bitcast(E4M3FN), func=COPY,
+            nc.scalar.activation(out=wide_plane(g, t), in_=w_plane(g, t), func=COPY,
                                  scale=w_scale[:, t:t + 1])
 
         def interleave(g, copy=nc.vector.tensor_copy, first=0, width=N):
             if g not in w_grouped:
                 w_grouped[g] = wide_pool.tile([P, N, 4], BF16, name="w_grouped", align_bytes=256)
             copy(out=w_grouped[g][:, first:first + width].rearrange("p (c i) t -> p c t i", i=4),
-                 in_=wide[g // 2][:, g % 2, :, first:first + width].rearrange("p t (c i) -> p c t i", i=4))
+                 in_=wide[g][:, :, first:first + width].rearrange("p t (c i) -> p c t i", i=4))
 
         def quantise_w(g):
             nc.vector.quantize_mx(out=w_codes[g][:].bitcast(E4M3_X4), scales=w_codes_scale[g][:],
@@ -181,14 +180,13 @@ def tile_cross_entropy_hidden_gradient_s3_kernel(
                                   in_=h_grouped[pair][:].rearrange("p j r t -> p (j r t)"))
 
         minus_norm = kept([P, M_TILES], F32, "minus_norm")
-        vs_bank = [vs_psum.tile([P, 2 * N], BF16, name="vs_bank%d" % half) for half in range(2)]
+        vs_bank = [vs_psum.tile([P, HALF], BF16, name="vs_bank%d" % half) for half in range(2)]
 
         def word_order(natural):
             return natural.rearrange("q (w u e) -> q u w e", u=2, e=2)
 
-        def stored(tile, g, count):
-            runs = tile[:, cols(g // 2 * 2, 2)].rearrange("q (u w e) -> q u w e", u=2, e=2)
-            return runs[:, :, g % 2 * P:(g % 2 + count) * P, :]
+        def stored(half_tile, first, last):
+            return half_tile.rearrange("q (u w e) -> q u w e", u=2, e=2)[:, :, first:last, :]
 
         def negate_norm():
             nc.vector.tensor_scalar(out=minus_norm[:], in0=norm[:], scalar1=-1.0, scalar2=None, op0=MULT)
@@ -206,8 +204,8 @@ def tile_cross_entropy_hidden_gradient_s3_kernel(
             nc.tensor.matmul(warm_bank[:].rearrange("p (a c) -> p a c", a=4), lhsT=ident_bf[:],
                              rhs=ident_bf[:].unsqueeze(1).to_broadcast([P, 4, P]), start=True, stop=True)
 
-        z_bank, grad, side = {}, {}, {}
-        e_tile = [kept([P, VOCAB], F32, "e%d" % m) for m in range(M_TILES)]
+        z_bank, grad, moved = {}, {}, {}
+        soft = {(m, half): kept([P, HALF], F32, "soft%d%d" % (m, half)) for m in range(M_TILES) for half in range(2)}
 
         def logits(m, g, passes=("rest0", "rest1", "outlier"), opens=True, closes=True):
             if opens:
@@ -218,252 +216,252 @@ def tile_cross_entropy_hidden_gradient_s3_kernel(
                     moving, moving_scale = w_codes[g][:].bitcast(E4M3_X4), w_codes_scale[g][:]
                 else:
                     pair, j = ("rest", m), int(name[-1])
-                    first = max(f for f in WR_LOADS if f <= g)
-                    moving = wr[first][:, j, cols(2 * (g - first), 2)].bitcast(E2M1_X4)
-                    moving_scale = wr_scale[g // 2][:, j, cols(g % 2)]
+                    moving, moving_scale = wr[g][:, j, :].bitcast(E2M1_X4), wr_scale[g // 2][:, j, cols(g % 2)]
                 nc.tensor.matmul_mx(
                     out=z_bank[m, g][:], lhsT=h_codes[pair][:, j, :].bitcast(E4M3_X4), lhsT_scale=h_scale[pair][:, j, :],
                     rhs=moving, rhs_scale=moving_scale,
                     start=(opens and name == passes[0]), stop=(closes and name == passes[-1]))
 
+        def open_logits(m, g):
+            logits(m, g, ("rest0", "rest1"), closes=False)
+
+        def close_logits(m, g):
+            logits(m, g, ("outlier",), opens=False)
+
         def exponential(m, g):
-            nc.scalar.activation(out=stored(e_tile[m], g, 1), in_=word_order(z_bank[m, g][:]), func=EXP,
-                                 bias=minus_norm[:, m:m + 1])
+            nc.scalar.activation(out=stored(soft[m, g // 2][:], g % 2 * P, (g % 2 + 1) * P), in_=word_order(z_bank[m, g][:]),
+                                 func=EXP, bias=minus_norm[:, m:m + 1])
 
-        def subtract(m, g, count=1):
-            e = stored(e_tile[m], g, count)
-            nc.vector.tensor_tensor(out=e, in0=e, in1=word_order(target[m][:, cols(g, count)]), op=SUBTRACT)
+        def subtract(m, half, first=0, last=WORDS, engine=nc.vector, into=None):
+            if into is not None:
+                for word in range(first, last, 64):
+                    moved[m, half, word] = into
+            engine.tensor_tensor(out=stored(soft[m, half][:] if into is None else into[:], first, last),
+                                 in0=stored(soft[m, half][:], first, last),
+                                 in1=word_order(target[m, half][:, 4 * first:4 * last]), op=SUBTRACT)
 
-        def subtract_gpsimd(m, g, tag):
-            side[m, g] = keep.tile([P, 2, P, 2], F32, name="side", tag=tag, align_bytes=256)
-            nc.gpsimd.tensor_tensor(out=side[m, g][:], in0=stored(e_tile[m], g, 1), in1=word_order(target[m][:, cols(g)]),
-                                    op=SUBTRACT)
-
-        def multiply(m, g, count=1):
+        def multiply(m, half, first=0, last=WORDS):
             if m not in grad:
                 grad[m] = grad_pool.tile([P, VOCAB], BF16, name="grad", align_bytes=256)
-            nc.vector.tensor_tensor(out=stored(grad[m], g, count), in0=side[m, g][:] if (m, g) in side else stored(e_tile[m], g, count),
-                                    in1=stored(vs_bank[g // 2], g % 2, count), op=MULT)
+            nc.vector.tensor_tensor(out=stored(grad[m][:, cols(2 * half, 2)], first, last),
+                                    in0=stored(moved.get((m, half, first), soft[m, half])[:], first, last),
+                                    in1=stored(vs_bank[half][:], first, last), op=MULT)
 
         g_grouped = {}
         g_codes = [kept([P, V_GROUPS, P], U32, "g_codes%d" % m) for m in range(M_TILES)]
         g_scale = [kept([P, V_GROUPS, P], U8, "g_scale%d" % m) for m in range(M_TILES)]
         g_bank = {}
 
-        def transpose_e(m, g, count=2):
+        def transpose_e(m, half):
             bank = t_psum.tile([P, 4, P], F32, name="t_bank", tag="t")
-            g_bank[m, g] = bank
+            g_bank[m, half] = bank
             words = grad[m][:].bitcast(F32)
-            for j in range(count):
-                for u in range(2):
-                    run = (g + j) // 2 * 4 + 2 * u + (g + j) % 2
-                    nc.tensor.transpose(bank[:, 2 * j + u, :], words[:, rows(run)], ident[:])
-
-        def grouped(m, g):
-            if (m, g // 2) not in g_grouped:
-                g_grouped[m, g // 2] = keep.tile([P, 2, P, 4], BF16, name="g_grouped", tag="grouped_%d%d" % (m % 2, g // 2),
-                                                 align_bytes=256)
-            return g_grouped[m, g // 2]
-
-        def copy_e(copy, m, g):
-            copy(out=grouped(m, g)[:].bitcast(F32), in_=g_bank[m, g][:].rearrange("p (g u) r -> p g r u", u=2))
-
-        def split_copy(copy, m, g):
             for j in range(2):
-                copy(out=grouped(m, g)[:, j].bitcast(F32), in_=g_bank[m, g][:, 2 * j:2 * j + 2, :].rearrange("p u r -> p r u"))
+                for u in range(2):
+                    nc.tensor.transpose(bank[:, 2 * j + u, :], words[:, rows(4 * half + 2 * u + j)], ident[:])
+
+        def grouped(m, half):
+            if (m, half) not in g_grouped:
+                g_grouped[m, half] = keep.tile([P, 2, P, 4], BF16, name="g_grouped", tag="grouped_%d%d" % (m % 2, half),
+                                               align_bytes=256)
+            return g_grouped[m, half]
+
+        def copy_e(copy, m, half):
+            copy(out=grouped(m, half)[:].bitcast(F32), in_=g_bank[m, half][:].rearrange("p (g u) r -> p g r u", u=2))
+
+        def split_copy(copy, m, half):
+            for j in range(2):
+                copy(out=grouped(m, half)[:, j].bitcast(F32), in_=g_bank[m, half][:, 2 * j:2 * j + 2, :].rearrange("p u r -> p r u"))
 
         def quantise_e(m, g, count):
             groups = slice(g, g + count)
             nc.vector.quantize_mx(out=g_codes[m][:, groups].rearrange("p g r -> p (g r)").bitcast(E4M3_X4),
                                   scales=g_scale[m][:, groups].rearrange("p g r -> p (g r)"),
-                                  in_=grouped(m, g)[:, g % 2:g % 2 + count].rearrange("p g r t -> p (g r t)"))
+                                  in_=grouped(m, g // 2)[:, g % 2:g % 2 + count].rearrange("p g r t -> p (g r t)"))
 
         o_bank = {}
 
-        def product(m, first, width=N, step=N, groups=range(V_GROUPS)):
+        def product(m, first, width=N, groups=range(V_GROUPS)):
             if (m, first) not in o_bank:
                 o_bank[m, first] = sum_psum.tile([P, N], F32, name="o_bank", tag="sum")
-            for c in range(0, width, step):
-                d0 = first + c
-                for g in groups:
-                    nc.tensor.matmul_mx(
-                        out=o_bank[m, first][:, c:c + step],
-                        lhsT=g_codes[m][:, g, :].bitcast(E4M3_X4), lhsT_scale=g_scale[m][:, g, :],
-                        rhs=wt[g // 2][:, g % 2, 2 * d0:2 * (d0 + step)].bitcast(E2M1_X4), rhs_scale=wt_scale[:, g, d0:d0 + step],
-                        start=(g == 0), stop=(g == V_GROUPS - 1))
+            for g in groups:
+                nc.tensor.matmul_mx(
+                    out=o_bank[m, first][:, 0:width],
+                    lhsT=g_codes[m][:, g, :].bitcast(E4M3_X4), lhsT_scale=g_scale[m][:, g, :],
+                    rhs=wt[g // 2][:, g % 2, 2 * first:2 * (first + width)].bitcast(E2M1_X4),
+                    rhs_scale=wt_scale[:, g, first:first + width],
+                    start=(g == 0), stop=(g == V_GROUPS - 1))
 
-        def store(copy, m, first, width=N, skip=0):
+        def store(copy, m, first, width=N):
             result = store_pool.tile([P, N], F32, name="result")
-            copy(out=result[:, 0:width], in_=o_bank[m, first][:, skip:skip + width])
-            nc.sync.dma_start(out=out_view[:, m, first + skip:first + skip + width], in_=result[:, 0:width])
+            copy(out=result[:, 0:width], in_=o_bank[m, first][:, 0:width])
+            nc.sync.dma_start(out=out_view[:, m, first:first + width], in_=result[:, 0:width])
 
         scalar, vector = nc.scalar.copy, nc.vector.tensor_copy
 
-        widen_vector(0, 0, 2)
-        widen_scalar(2, 0)
-        widen_scalar(3, 0)
-        widen_vector(0, 1, 2)
-        widen_vector(2, 1, 2)
+        load_w(0)
+        load(w_scale[:], w_out_scale.rearrange("(p t) o -> p (t o)", t=4))
+        load_w(1)
+        load(vs_rows[0:VS_ROWS, :], vocab_scale.rearrange("(r c) -> r c", c=P))
+        load_rest(0)
+        load_outlier(0)
+        load_rest(1)
+        load_wr_scales(0)
+        load_wr(0)
+        load(norm[:], log_norm.rearrange("(p m) -> p m", m=M_TILES))
+        load_w(2)
+        load_rest(2)
+        load_outlier(1)
+        load_wr(1)
+        load_wr_scales(1)
+        load_w(3)
+        load_wr(2)
+        load_target_half(0, 0)
+        load_wr(3)
+        load_rest(3)
+        load_target_half(0, 1)
+        load_target(1)
+
+        widen_vector(0, 0)
+        widen_scalar(1, 0)
+        widen_vector(0, 1)
+        widen_scalar(1, 1)
         widen_vector(0, 2)
-        widen_scalar(0, 3)
+        widen_vector(0, 3)
         widen_scalar(1, 3)
-        widen_scalar(3, 3)
         widen_vector(1, 2)
         warm_up()
         warm_up()
-        for g in range(V_GROUPS):
-            spread_vs(g)
+        warm_up()
+        spread_vs(0)
+        spread_vs(1)
+        spread_vs(2)
         transpose_h("rest", 0)
         transpose_h("outlier", 0)
-        warm_up()
+        transpose_h("rest", 1, pool=sum_psum, tag="sum")
+        spread_vs(3)
+        interleave(0)
+        interleave(1, scalar, 0, P)
+        interleave(1, vector, P, P)
         copy_h(scalar, "rest", 0)
         copy_h(scalar, "outlier", 0)
-        interleave(0)
-        widen_vector(2, 2)
-        quantise_w(0)
-        quantise_h("outlier", 0)
-        quantise_h("rest", 0)
-        transpose_h("rest", 1, pool=sum_psum, tag="sum")
-        warm_up()
-        transpose_h("rest", 2)
         copy_h(scalar, "rest", 1)
-        warm_up()
+        quantise_w(0)
+        quantise_h("rest", 0)
+        quantise_h("outlier", 0)
+        interleave(1, vector, 2 * P, P)
+        interleave(1, scalar, 3 * P, P)
+        quantise_h("rest", 1)
+        logits(0, 0)
+        logits(1, 0, ("outlier", "rest0", "rest1"))
+        transpose_h("rest", 2)
         transpose_h("outlier", 1)
-        copy_h(scalar, "rest", 2)
-        copy_h(scalar, "outlier", 1)
         wt_scale = keep.tile([P, V_GROUPS, HIDDEN], U8, name="wt_scale", tag="shared", align_bytes=256)
         load_scales(wt_scale, wt_scales)
         load_wt(0)
-        load_target(2, 0, 2)
+        load_target_half(2, 0)
         load_wt(1)
-        load_target(2, 2, 2)
+        load_target_half(2, 1)
         load_target(3)
-        quantise_h("rest", 1)
-        interleave(1)
-        quantise_h("rest", 2)
-        quantise_h("outlier", 1)
         negate_norm()
-        quantise_w(1)
         widen_scalar(2, 3)
-        widen_scalar(3, 2)
-        for m in range(2):
-            logits(m, 0, ("outlier",), closes=False)
-        for m in range(2):
-            logits(m, 0, ("rest0", "rest1"), opens=False)
-        logits(2, 0)
+        widen_scalar(2, 2)
+        widen_vector(2, 0)
+        widen_vector(2, 1)
+        quantise_w(1)
         exponential(0, 0)
         interleave(2)
+        copy_h(scalar, "rest", 2)
+        copy_h(scalar, "outlier", 1)
         exponential(1, 0)
-        subtract(0, 0)
+        quantise_h("rest", 2)
         quantise_w(2)
+        quantise_h("outlier", 1)
         logits(0, 1)
-        interleave(3, scalar, 0 * P, P)
-        exponential(2, 0)
-        exponential(0, 1)
         logits(1, 1)
-        exponential(1, 1)
+        logits(2, 0)
         logits(2, 1)
+        exponential(0, 1)
+        widen_scalar(3, 3)
+        exponential(1, 1)
+        for t in range(3):
+            widen_vector(3, t)
+        exponential(2, 0)
         exponential(2, 1)
-        interleave(3, vector, 1 * P, 3 * P)
-        subtract(0, 1)
-        quantise_w(3)
-        multiply(0, 0, 2)
-
         logits(0, 2)
-        exponential(0, 2)
         logits(1, 2)
-        exponential(1, 2)
         logits(2, 2)
+        subtract(0, 0, 0, P)
+        interleave(3)
+        subtract(0, 0, P, WORDS)
+        exponential(0, 2)
+        exponential(1, 2)
+        quantise_w(3)
         logits(0, 3)
+        transpose_h("rest", 3)
         exponential(2, 2)
         exponential(0, 3)
-        subtract(0, 2)
-        subtract(1, 0)
-        subtract(0, 3)
-        transpose_h("rest", 3)
-        transpose_e(0, 0)
         copy_h(scalar, "rest", 3)
-        copy_e(scalar, 0, 0)
         logits(1, 3)
         logits(2, 3)
-        quantise_h("rest", 3)
-        multiply(0, 2, 2)
+        side = {}
+
+
+        def subtract_aside(m, tag):
+            side[m] = keep.tile([P, HALF], F32, name="side", tag=tag, align_bytes=256)
+            subtract(m, 1, 0, SPLIT, into=side[m])
+            subtract(m, 1, SPLIT, WORDS, engine=nc.gpsimd, into=side[m])
+
+
+        multiply(0, 0)
+        subtract(0, 1, 0, P)
+        subtract(1, 0, 0, P)
+        subtract(0, 1, P, WORDS)
         exponential(1, 3)
         exponential(2, 3)
-        subtract(1, 1)
-        quantise_e(0, 0, 2)
-        subtract(1, 2, 2)
+        quantise_h("rest", 3)
+        subtract_aside(1, "grouped_rest3")
+        subtract(1, 0, P, WORDS)
+        multiply(0, 1)
+        multiply(1, 0)
         logits(3, 0)
-        transpose_e(0, 2)
         logits(3, 1)
         exponential(3, 0)
-        copy_e(scalar, 0, 2)
         exponential(3, 1)
-        quantise_e(0, 2, 2)
-        subtract_gpsimd(2, 0, "grouped_01")
-        multiply(1, 0, 2)
-        for d in range(D_GROUPS):
-            product(0, d * N, groups=range(2))
-        multiply(1, 2, 2)
-        for d in range(D_GROUPS):
-            product(0, d * N, groups=range(2, 4))
-        store(scalar, 0, 0)
-        store(scalar, 0, N)
-        transpose_e(1, 0)
-        transpose_e(1, 2)
-        subtract(2, 1)
-        subtract(2, 2, 2)
-        subtract(3, 1)
-        copy_e(scalar, 1, 0)
-        copy_e(scalar, 1, 2)
-        store(scalar, 0, 2 * N)
-        logits(3, 2)
-        logits(3, 3)
-        quantise_e(1, 0, 2)
-        quantise_e(1, 2, 2)
-        subtract_gpsimd(3, 0, "grouped_11")
-        multiply(2, 0)
-        multiply(2, 1)
-        multiply(2, 2, 2)
-        exponential(3, 2)
-        exponential(3, 3)
-        for groups in (range(2), range(2, 4)):
-            product(1, 0, groups=groups)
-            product(1, N, groups=groups)
-        store(scalar, 1, 0)
-        transpose_e(2, 0)
-        transpose_e(2, 2)
-        split_copy(scalar, 2, 0)
-        copy_e(scalar, 2, 2)
-        product(1, 2 * N)
-        subtract(3, 2, 2)
-        quantise_e(2, 0, 1)
-        quantise_e(2, 1, 1)
-        multiply(3, 0)
-        quantise_e(2, 2, 2)
-        multiply(3, 1)
-        multiply(3, 2, 2)
-        store(scalar, 1, N)
-        store(scalar, 1, 2 * N)
-        for groups in (range(1), range(1, 2), range(2, 4)):
-            product(2, 0, groups=groups)
-            product(2, N, groups=groups)
-        store(scalar, 2, 0)
-        transpose_e(3, 0)
-        transpose_e(3, 2)
-        split_copy(vector, 3, 0)
-        copy_e(scalar, 3, 2)
-        product(2, 2 * N)
-        quantise_e(3, 0, 1)
-        quantise_e(3, 1, 1)
-        quantise_e(3, 2, 2)
-        store(scalar, 2, N)
-        store(vector, 2, 2 * N)
-        for groups in (range(1), range(1, 2), range(2, 4)):
-            product(3, 0, groups=groups)
-            product(3, N, groups=groups)
+        for m in range(M_TILES):
+            transpose_e(m, 0)
+            transpose_e(m, 1)
+            copy_e(scalar, m, 0)
+            copy_e(scalar, m, 1)
+            if m == 0:
+                logits(3, 2)
+                logits(3, 3)
+                exponential(3, 2)
+                exponential(3, 3)
+            else:
+                store(scalar if m < 3 else vector, m - 1, 0)
+                product(m - 1, N, groups=range(2, 4))
+                store(scalar, m - 1, N)
+                product(m - 1, 2 * N)
+                store(scalar, m - 1, 2 * N)
+            if m < 2:
+                subtract(m + 2, 0, 0, P)
+            quantise_e(m, 0, 2)
+            if m < 2:
+                subtract(m + 2, 0, P, WORDS)
+            quantise_e(m, 2, 2)
+            if m == 3:
+                break
+            if m < 2:
+                subtract_aside(m + 2, "grouped_%d1" % (m % 2))
+            multiply(m + 1, 1)
+            if m < 2:
+                multiply(m + 2, 0)
+            product(m, 0, groups=range(2))
+            product(m, N, groups=range(2))
+            product(m, 0, groups=range(2, 4))
+        product(3, 0)
         store(scalar, 3, 0)
-        store(vector, 3, N)
-        product(3, 2 * N)
-        store(scalar, 3, 2 * N, 2 * P)
-        store(scalar, 3, 2 * N, 2 * P, 2 * P)
+        for i in range(4):
+            product(3, N + i * 2 * P, 2 * P)
+            store(vector if i % 2 == 0 else scalar, 3, N + i * 2 * P, 2 * P)

@@ -28,6 +28,7 @@ VS_ROWS = VOCAB // P
 HALF = 2 * N
 SPLIT = 64
 W_LOADS = [(0, 2, 0, 2), (0, 2, 2, 2), (2, 1, 0, 4), (3, 1, 0, 4)]
+WR_LOADS = {0: 1, 1: 1, 2: 1, 3: 1}
 WORDS = HALF // 4
 
 
@@ -38,7 +39,7 @@ def tile_cross_entropy_hidden_gradient_s3_kernel(
     nc = tc.nc
     with ExitStack() as ctx:
         keep = ctx.enter_context(tc.tile_pool(name="keep", bufs=1))
-        wide_pool = ctx.enter_context(tc.tile_pool(name="wide_pool", bufs=3))
+        wide_pool = ctx.enter_context(tc.tile_pool(name="wide_pool", bufs=2))
         grad_pool = ctx.enter_context(tc.tile_pool(name="grad_pool", bufs=3))
         store_pool = ctx.enter_context(tc.tile_pool(name="store_pool", bufs=8))
         sum_psum = ctx.enter_context(tc.psum_pool(name="sum_psum", bufs=4))
@@ -68,7 +69,7 @@ def tile_cross_entropy_hidden_gradient_s3_kernel(
         norm = kept([P, M_TILES], BF16, "norm")
         w_scale = kept([P, 4], F32, "w_scale")
         w_bytes = {load: kept([P, load[3], N * load[1]], U8, "w_bytes%d%d" % (load[0], load[2])) for load in W_LOADS}
-        wr = [kept([P, 2, 2 * N], U8, "wr%d" % g) for g in range(V_GROUPS)]
+        wr = {g: kept([P, 2, 2 * N * count], U8, "wr%d" % g) for g, count in WR_LOADS.items()}
         h_first = keep.tile([P, 3 * REST_CH], BF16, name="h_first", tag="shared", align_bytes=256)
         rest = [h_first[:, 0:REST_CH], h_first[:, REST_CH:2 * REST_CH]]
         rest = rest + [kept([P, REST_CH], BF16, "rest%d" % m)[:] for m in range(2, M_TILES)]
@@ -100,7 +101,7 @@ def tile_cross_entropy_hidden_gradient_s3_kernel(
             load(w_bytes[W_LOADS[i]][:], w_view[:, t:t + planes, cols(g, groups)])
 
         def load_wr(g):
-            load(wr[g][:], wr_view[:, :, cols(2 * g, 2)])
+            load(wr[g][:], wr_view[:, :, cols(2 * g, 2 * WR_LOADS[g])])
 
         def load_wr_scales(half):
             load_scales(wr_scale[half], w_rest_scales[:, :, cols(2 * half, 2)])
@@ -120,32 +121,30 @@ def tile_cross_entropy_hidden_gradient_s3_kernel(
         def load_wt(i):
             load(wt[i][:], wt_words[2 * i:2 * i + 2].rearrange("g p n -> p g n"))
 
-        wide, w_grouped = {}, {}
+        w_grouped = {}
         w_codes = [kept([P, N], U32, "w_codes%d" % g) for g in range(V_GROUPS)]
         w_codes_scale = [kept([P, N], U8, "w_codes_scale%d" % g) for g in range(V_GROUPS)]
 
-        def wide_plane(g, t):
-            if g not in wide:
-                wide[g] = wide_pool.tile([P, 4, N], BF16, name="wide", align_bytes=256)
-            return wide[g][:, t, :]
+        wide = [kept([P, 2, 4, N], BF16, "wide%d" % half) for half in range(2)]
 
-        def w_plane(g, t):
+        def w_plane(g, t, count=1):
             load = [x for x in W_LOADS if x[0] <= g < x[0] + x[1] and x[2] <= t < x[2] + x[3]][0]
-            return w_bytes[load][:, t - load[2], cols(g - load[0])].bitcast(E4M3FN)
+            return w_bytes[load][:, t - load[2], cols(g - load[0], count)].bitcast(E4M3FN)
 
-        def widen_vector(g, t):
-            nc.vector.tensor_scalar(out=wide_plane(g, t), in0=w_plane(g, t),
+        def widen_vector(g, t, count=1):
+            nc.vector.tensor_scalar(out=wide[g // 2][:, g % 2:g % 2 + count, t, :],
+                                    in0=w_plane(g, t, count).rearrange("p (j v) -> p j v", j=count),
                                     scalar1=w_scale[:, t:t + 1], scalar2=None, op0=MULT)
 
         def widen_scalar(g, t):
-            nc.scalar.activation(out=wide_plane(g, t), in_=w_plane(g, t), func=COPY,
+            nc.scalar.activation(out=wide[g // 2][:, g % 2, t, :], in_=w_plane(g, t), func=COPY,
                                  scale=w_scale[:, t:t + 1])
 
         def interleave(g, copy=nc.vector.tensor_copy, first=0, width=N):
             if g not in w_grouped:
                 w_grouped[g] = wide_pool.tile([P, N, 4], BF16, name="w_grouped", align_bytes=256)
             copy(out=w_grouped[g][:, first:first + width].rearrange("p (c i) t -> p c t i", i=4),
-                 in_=wide[g][:, :, first:first + width].rearrange("p t (c i) -> p c t i", i=4))
+                 in_=wide[g // 2][:, g % 2, :, first:first + width].rearrange("p t (c i) -> p c t i", i=4))
 
         def quantise_w(g):
             nc.vector.quantize_mx(out=w_codes[g][:].bitcast(E4M3_X4), scales=w_codes_scale[g][:],
@@ -216,7 +215,9 @@ def tile_cross_entropy_hidden_gradient_s3_kernel(
                     moving, moving_scale = w_codes[g][:].bitcast(E4M3_X4), w_codes_scale[g][:]
                 else:
                     pair, j = ("rest", m), int(name[-1])
-                    moving, moving_scale = wr[g][:, j, :].bitcast(E2M1_X4), wr_scale[g // 2][:, j, cols(g % 2)]
+                    first = max(f for f in WR_LOADS if f <= g)
+                    moving = wr[first][:, j, cols(2 * (g - first), 2)].bitcast(E2M1_X4)
+                    moving_scale = wr_scale[g // 2][:, j, cols(g % 2)]
                 nc.tensor.matmul_mx(
                     out=z_bank[m, g][:], lhsT=h_codes[pair][:, j, :].bitcast(E4M3_X4), lhsT_scale=h_scale[pair][:, j, :],
                     rhs=moving, rhs_scale=moving_scale,
@@ -407,21 +408,30 @@ def tile_cross_entropy_hidden_gradient_s3_kernel(
         side = {}
 
 
-        def subtract_aside(m, tag):
-            side[m] = keep.tile([P, HALF], F32, name="side", tag=tag, align_bytes=256)
-            subtract(m, 1, 0, SPLIT, into=side[m])
-            subtract(m, 1, SPLIT, WORDS, engine=nc.gpsimd, into=side[m])
+        target_words = {m: kept([P, 2, WORDS - SPLIT], F32, "target_words%d" % m) for m in range(1, M_TILES)}
+
+
+        def order_target(m):
+            nc.scalar.copy(out=target_words[m][:], in_=target[m, 1][:, 4 * SPLIT:].bitcast(F32).rearrange("q (w u) -> q u w", u=2))
+
+
+        def subtract_aside(m, buffer):
+            side[m] = buffer
+            runs = [tile[:].rearrange("q (u c) -> q u c", u=2)[:, :, 2 * SPLIT:] for tile in (buffer, soft[m, 1])]
+            nc.gpsimd.tensor_tensor(out=runs[0], in0=runs[1], in1=target_words[m][:].bitcast(BF16), op=SUBTRACT)
 
 
         multiply(0, 0)
         subtract(0, 1, 0, P)
-        subtract(1, 0, 0, P)
+        spare = kept([P, HALF], F32, "spare")
+        subtract(1, 0, 0, P, into=spare)
         subtract(0, 1, P, WORDS)
+        order_target(1)
         exponential(1, 3)
         exponential(2, 3)
         quantise_h("rest", 3)
-        subtract_aside(1, "grouped_rest3")
-        subtract(1, 0, P, WORDS)
+        subtract(1, 0, P, WORDS, into=spare)
+        subtract_aside(1, soft[1, 0])
         multiply(0, 1)
         multiply(1, 0)
         logits(3, 0)
@@ -437,13 +447,17 @@ def tile_cross_entropy_hidden_gradient_s3_kernel(
                 logits(3, 2)
                 logits(3, 3)
                 exponential(3, 2)
+                order_target(2)
                 exponential(3, 3)
+                order_target(3)
             else:
                 store(scalar if m < 3 else vector, m - 1, 0)
                 product(m - 1, N, groups=range(2, 4))
                 store(scalar, m - 1, N)
                 product(m - 1, 2 * N)
                 store(scalar, m - 1, 2 * N)
+            if m < 3:
+                subtract(m + 1, 1, 0, SPLIT, into=side[m + 1])
             if m < 2:
                 subtract(m + 2, 0, 0, P)
             quantise_e(m, 0, 2)
@@ -453,7 +467,7 @@ def tile_cross_entropy_hidden_gradient_s3_kernel(
             if m == 3:
                 break
             if m < 2:
-                subtract_aside(m + 2, "grouped_%d1" % (m % 2))
+                subtract_aside(m + 2, keep.tile([P, HALF], F32, name="side", tag="grouped_%d1" % (m % 2), align_bytes=256))
             multiply(m + 1, 1)
             if m < 2:
                 multiply(m + 2, 0)

@@ -188,7 +188,7 @@ def tile_cross_entropy_hidden_gradient_s3_kernel(
             return half_tile.rearrange("q (u w e) -> q u w e", u=2, e=2)[:, :, first:last, :]
 
         def negate_norm():
-            nc.vector.tensor_scalar(out=minus_norm[:], in0=norm[:], scalar1=-1.0, scalar2=None, op0=MULT)
+            nc.scalar.activation(out=minus_norm[:], in_=norm[:], func=COPY, scale=-1.0)
 
         def spread_vs(g):
             for r in range(4):
@@ -235,7 +235,7 @@ def tile_cross_entropy_hidden_gradient_s3_kernel(
 
         def subtract(m, half, first=0, last=WORDS, engine=nc.vector, into=None):
             if into is not None:
-                for word in range(first, last, 64):
+                for word in range(first, last, 32):
                     moved[m, half, word] = into
             engine.tensor_tensor(out=stored(soft[m, half][:] if into is None else into[:], first, last),
                                  in0=stored(soft[m, half][:], first, last),
@@ -300,6 +300,25 @@ def tile_cross_entropy_hidden_gradient_s3_kernel(
 
         scalar, vector = nc.scalar.copy, nc.vector.tensor_copy
 
+        LAST = 32
+        side = {}
+        target_words = {m: kept([P, 2, WORDS], F32, "target_words%d" % m) for m in range(1, M_TILES)}
+
+
+        spare = [kept([P, HALF], F32, "spare%d" % i) for i in range(2)]
+
+
+        def order_target(m, first=0, last=WORDS):
+            nc.scalar.copy(out=target_words[m][:, :, first:last],
+                           in_=target[m, 0][:, 4 * first:4 * last].bitcast(F32).rearrange("q (w u) -> q u w", u=2))
+
+
+        def subtract_aside(m, buffer):
+            moved[m, 0, 0] = buffer
+            runs = [tile[:].rearrange("q (u c) -> q u c", u=2)[:, :, 2 * SPLIT:] for tile in (buffer, soft[m, 0])]
+            nc.gpsimd.tensor_tensor(out=runs[0], in0=runs[1], in1=target_words[m][:, :, SPLIT:].bitcast(BF16), op=SUBTRACT)
+
+
         load_w(0)
         load(w_scale[:], w_out_scale.rearrange("(p t) o -> p (t o)", t=4))
         load_w(1)
@@ -317,9 +336,9 @@ def tile_cross_entropy_hidden_gradient_s3_kernel(
         load_wr_scales(1)
         load_w(3)
         load_wr(2)
+        load_rest(3)
         load_target_half(0, 0)
         load_wr(3)
-        load_rest(3)
         load_target_half(0, 1)
         load_target(1)
 
@@ -329,29 +348,31 @@ def tile_cross_entropy_hidden_gradient_s3_kernel(
         widen_scalar(1, 1)
         widen_vector(0, 2)
         widen_vector(0, 3)
-        widen_scalar(1, 3)
         widen_vector(1, 2)
+        widen_scalar(1, 3)
         warm_up()
         warm_up()
         warm_up()
         spread_vs(0)
         spread_vs(1)
-        spread_vs(2)
         transpose_h("rest", 0)
+        spread_vs(2)
         transpose_h("outlier", 0)
-        transpose_h("rest", 1, pool=sum_psum, tag="sum")
         spread_vs(3)
-        interleave(0)
-        interleave(1, scalar, 0, P)
+        transpose_h("rest", 1, pool=sum_psum, tag="sum")
+        warm_up()
+        warm_up()
+        interleave(0, scalar, 0, P)
+        interleave(0, vector, P, 3 * P)
         interleave(1, vector, P, P)
         copy_h(scalar, "rest", 0)
         copy_h(scalar, "outlier", 0)
         copy_h(scalar, "rest", 1)
+        negate_norm()
         quantise_w(0)
         quantise_h("rest", 0)
         quantise_h("outlier", 0)
         interleave(1, vector, 2 * P, P)
-        interleave(1, scalar, 3 * P, P)
         quantise_h("rest", 1)
         logits(0, 0)
         logits(1, 0, ("outlier", "rest0", "rest1"))
@@ -364,118 +385,115 @@ def tile_cross_entropy_hidden_gradient_s3_kernel(
         load_wt(1)
         load_target_half(2, 1)
         load_target(3)
-        negate_norm()
+        interleave(1, scalar, 0, P)
+        interleave(1, vector, 3 * P, P)
         widen_scalar(2, 3)
         widen_scalar(2, 2)
         widen_vector(2, 0)
         widen_vector(2, 1)
         quantise_w(1)
         exponential(0, 0)
-        interleave(2)
         copy_h(scalar, "rest", 2)
         copy_h(scalar, "outlier", 1)
         exponential(1, 0)
+        interleave(2, vector, 0, 2 * P)
         quantise_h("rest", 2)
-        quantise_w(2)
+        interleave(2, vector, 2 * P, 2 * P)
         quantise_h("outlier", 1)
-        logits(0, 1)
-        logits(1, 1)
+        open_logits(0, 1)
+        open_logits(1, 1)
+        close_logits(0, 1)
+        close_logits(1, 1)
         logits(2, 0)
         logits(2, 1)
         exponential(0, 1)
         widen_scalar(3, 3)
         exponential(1, 1)
-        for t in range(3):
-            widen_vector(3, t)
+        widen_vector(3, 0)
+        widen_vector(3, 1)
+        widen_vector(3, 2)
+        quantise_w(2)
         exponential(2, 0)
         exponential(2, 1)
-        logits(0, 2)
+        open_logits(0, 2)
+        transpose_h("rest", 3)
+        close_logits(0, 2)
         logits(1, 2)
-        logits(2, 2)
-        subtract(0, 0, 0, P)
-        interleave(3)
-        subtract(0, 0, P, WORDS)
+        copy_h(scalar, "rest", 3)
         exponential(0, 2)
+        interleave(3)
         exponential(1, 2)
         quantise_w(3)
+        quantise_h("rest", 3)
+        subtract(0, 1, 0, P)
+        subtract(0, 0, into=spare[1])
         logits(0, 3)
-        transpose_h("rest", 3)
-        exponential(2, 2)
+        logits(2, 2)
         exponential(0, 3)
-        copy_h(scalar, "rest", 3)
+        order_target(1, SPLIT, WORDS)
+        exponential(2, 2)
         logits(1, 3)
         logits(2, 3)
-        side = {}
-
-
-        target_words = {m: kept([P, 2, WORDS - SPLIT], F32, "target_words%d" % m) for m in range(1, M_TILES)}
-
-
-        def order_target(m):
-            nc.scalar.copy(out=target_words[m][:], in_=target[m, 1][:, 4 * SPLIT:].bitcast(F32).rearrange("q (w u) -> q u w", u=2))
-
-
-        def subtract_aside(m, buffer):
-            side[m] = buffer
-            runs = [tile[:].rearrange("q (u c) -> q u c", u=2)[:, :, 2 * SPLIT:] for tile in (buffer, soft[m, 1])]
-            nc.gpsimd.tensor_tensor(out=runs[0], in0=runs[1], in1=target_words[m][:].bitcast(BF16), op=SUBTRACT)
-
-
-        multiply(0, 0)
-        subtract(0, 1, 0, P)
-        spare = kept([P, HALF], F32, "spare")
-        subtract(1, 0, 0, P, into=spare)
-        subtract(0, 1, P, WORDS)
-        order_target(1)
         exponential(1, 3)
         exponential(2, 3)
-        quantise_h("rest", 3)
-        subtract(1, 0, P, WORDS, into=spare)
-        subtract_aside(1, soft[1, 0])
+        order_target(2, SPLIT, WORDS - LAST)
+        subtract(0, 1, P, WORDS)
+        subtract_aside(1, soft[0, 0])
+        multiply(0, 0)
         multiply(0, 1)
-        multiply(1, 0)
         logits(3, 0)
         logits(3, 1)
         exponential(3, 0)
-        exponential(3, 1)
         for m in range(M_TILES):
             transpose_e(m, 0)
             transpose_e(m, 1)
-            copy_e(scalar, m, 0)
+            (split_copy if m == 3 else copy_e)(scalar, m, 0)
+            if m < 2:
+                order_target(m + 2, WORDS - LAST, WORDS)
             copy_e(scalar, m, 1)
             if m == 0:
+                exponential(3, 1)
                 logits(3, 2)
                 logits(3, 3)
                 exponential(3, 2)
-                order_target(2)
                 exponential(3, 3)
-                order_target(3)
+                order_target(3, SPLIT, WORDS - LAST)
+            elif m < 3:
+                quantise_e(m - 1, 2, 2)
+                for d in range(D_GROUPS):
+                    product(m - 1, d * N, groups=range(2, 4))
+                    store(scalar, m - 1, d * N)
             else:
-                store(scalar if m < 3 else vector, m - 1, 0)
-                product(m - 1, N, groups=range(2, 4))
-                store(scalar, m - 1, N)
-                product(m - 1, 2 * N)
-                store(scalar, m - 1, 2 * N)
+                store(vector, 2, 0)
+                for d in range(1, D_GROUPS):
+                    product(2, d * N, groups=range(2, 4))
+                    store(scalar, 2, d * N)
             if m < 3:
-                subtract(m + 1, 1, 0, SPLIT, into=side[m + 1])
-            if m < 2:
-                subtract(m + 2, 0, 0, P)
-            quantise_e(m, 0, 2)
-            if m < 2:
-                subtract(m + 2, 0, P, WORDS)
-            quantise_e(m, 2, 2)
+                if SPLIT:
+                    subtract(m + 1, 0, 0, SPLIT, into=moved[m + 1, 0, 0])
+                subtract(m + 1, 1, into=spare[(m + 1) % 2])
             if m == 3:
                 break
+            quantise_e(m, 0, 2)
             if m < 2:
-                subtract_aside(m + 2, keep.tile([P, HALF], F32, name="side", tag="grouped_%d1" % (m % 2), align_bytes=256))
+                subtract_aside(m + 2, soft[m + 1, 1])
+            multiply(m + 1, 0)
+            if m == 2:
+                quantise_e(2, 2, 2)
             multiply(m + 1, 1)
-            if m < 2:
-                multiply(m + 2, 0)
-            product(m, 0, groups=range(2))
-            product(m, N, groups=range(2))
-            product(m, 0, groups=range(2, 4))
-        product(3, 0)
-        store(scalar, 3, 0)
-        for i in range(4):
+            for d in range(D_GROUPS):
+                product(m, d * N, groups=range(2))
+            if m == 2:
+                product(2, 0, groups=range(2, 4))
+        quantise_e(3, 0, 1)
+        quantise_e(3, 1, 1)
+        quantise_e(3, 2, 2)
+        product(3, 0, groups=range(2))
+        product(3, N, 2 * P, groups=range(2))
+        product(3, 0, groups=range(2, 4))
+        store(vector, 3, 0)
+        product(3, N, 2 * P, groups=range(2, 4))
+        store(scalar, 3, N, 2 * P)
+        for i in range(1, 4):
             product(3, N + i * 2 * P, 2 * P)
             store(vector if i % 2 == 0 else scalar, 3, N + i * 2 * P, 2 * P)

@@ -60,6 +60,8 @@ def tile_cross_entropy_hidden_gradient_s3_kernel(
         vs_rows = kept([P, P], BF16, "vs_rows")
         ident = kept([P, P], F32, "ident")
         ident_bf = kept([P, P], BF16, "ident_bf")
+        zeros = kept([P, P], F32, "zeros")
+        nc.vector.memset(zeros[:], 0.0)
         make_identity(nc, ident[:])
         nc.vector.memset(vs_rows[:], 0.0)
         nc.scalar.copy(out=ident_bf[:], in_=ident[:])
@@ -199,9 +201,9 @@ def tile_cross_entropy_hidden_gradient_s3_kernel(
 
         warm_bank = sum_psum.tile([P, N], F32, name="warm_bank", tag="sum")
 
-        def warm_up():
-            nc.tensor.matmul(warm_bank[:].rearrange("p (a c) -> p a c", a=4), lhsT=ident_bf[:],
-                             rhs=ident_bf[:].unsqueeze(1).to_broadcast([P, 4, P]), start=True, stop=True)
+        def warm_up(operand=ident_bf):
+            nc.tensor.matmul(warm_bank[:].rearrange("p (a c) -> p a c", a=4), lhsT=operand[:],
+                             rhs=operand[:].unsqueeze(1).to_broadcast([P, 4, P]), start=True, stop=True)
 
         z_bank, grad, moved = {}, {}, {}
         soft = {(m, half): kept([P, HALF], F32, "soft%d%d" % (m, half)) for m in range(M_TILES) for half in range(2)}
@@ -333,11 +335,11 @@ def tile_cross_entropy_hidden_gradient_s3_kernel(
         load_rest(2)
         load_outlier(1)
         load_wr(1)
-        load_wr_scales(1)
         load_w(3)
+        load_wr_scales(1)
         load_wr(2)
-        load_rest(3)
         load_target_half(0, 0)
+        load_rest(3)
         load_wr(3)
         load_target_half(0, 1)
         load_target(1)
@@ -350,7 +352,7 @@ def tile_cross_entropy_hidden_gradient_s3_kernel(
         widen_vector(0, 3)
         widen_vector(1, 2)
         widen_scalar(1, 3)
-        warm_up()
+        warm_up(zeros)
         warm_up()
         warm_up()
         spread_vs(0)
@@ -380,10 +382,10 @@ def tile_cross_entropy_hidden_gradient_s3_kernel(
         transpose_h("outlier", 1)
         wt_scale = keep.tile([P, V_GROUPS, HIDDEN], U8, name="wt_scale", tag="shared", align_bytes=256)
         load_scales(wt_scale, wt_scales)
-        load_wt(0)
         load_target_half(2, 0)
-        load_wt(1)
+        load_wt(0)
         load_target_half(2, 1)
+        load_wt(1)
         load_target(3)
         interleave(1, scalar, 0, P)
         interleave(1, vector, 3 * P, P)
@@ -396,9 +398,9 @@ def tile_cross_entropy_hidden_gradient_s3_kernel(
         copy_h(scalar, "rest", 2)
         copy_h(scalar, "outlier", 1)
         exponential(1, 0)
-        interleave(2, vector, 0, 2 * P)
+        interleave(2)
         quantise_h("rest", 2)
-        interleave(2, vector, 2 * P, 2 * P)
+        widen_vector(3, 0)
         quantise_h("outlier", 1)
         open_logits(0, 1)
         open_logits(1, 1)
@@ -409,10 +411,10 @@ def tile_cross_entropy_hidden_gradient_s3_kernel(
         exponential(0, 1)
         widen_scalar(3, 3)
         exponential(1, 1)
-        widen_vector(3, 0)
         widen_vector(3, 1)
-        widen_vector(3, 2)
         quantise_w(2)
+        widen_vector(3, 2)
+        subtract(0, 0, 0, P)
         exponential(2, 0)
         exponential(2, 1)
         open_logits(0, 2)
@@ -422,11 +424,12 @@ def tile_cross_entropy_hidden_gradient_s3_kernel(
         copy_h(scalar, "rest", 3)
         exponential(0, 2)
         interleave(3)
+        subtract(0, 0, P, WORDS)
         exponential(1, 2)
         quantise_w(3)
         quantise_h("rest", 3)
-        subtract(0, 1, 0, P)
-        subtract(0, 0, into=spare[1])
+        subtract(0, 1, 0, P, into=spare[0])
+        subtract(1, 0, 0, SPLIT, into=soft[0, 1])
         logits(0, 3)
         logits(2, 2)
         exponential(0, 3)
@@ -437,8 +440,8 @@ def tile_cross_entropy_hidden_gradient_s3_kernel(
         exponential(1, 3)
         exponential(2, 3)
         order_target(2, SPLIT, WORDS - LAST)
-        subtract(0, 1, P, WORDS)
-        subtract_aside(1, soft[0, 0])
+        subtract(0, 1, P, WORDS, into=spare[0])
+        subtract_aside(1, soft[0, 1])
         multiply(0, 0)
         multiply(0, 1)
         logits(3, 0)
@@ -468,9 +471,13 @@ def tile_cross_entropy_hidden_gradient_s3_kernel(
                 for d in range(1, D_GROUPS):
                     product(2, d * N, groups=range(2, 4))
                     store(scalar, 2, d * N)
-            if m < 3:
-                if SPLIT:
-                    subtract(m + 1, 0, 0, SPLIT, into=moved[m + 1, 0, 0])
+            if m == 0:
+                subtract(1, 1, 0, P, into=spare[1])
+                subtract(2, 0, 0, SPLIT, into=soft[1, 1])
+                subtract(1, 1, P, WORDS, into=spare[1])
+            if m == 2:
+                subtract(3, 0, 0, SPLIT, into=soft[2, 1])
+            if m in (1, 2):
                 subtract(m + 1, 1, into=spare[(m + 1) % 2])
             if m == 3:
                 break

@@ -148,6 +148,20 @@ def tile_cross_entropy_hidden_gradient_s3_kernel(
             copy(out=w_grouped[g][:, first:first + width].rearrange("p (c i) t -> p c t i", i=4),
                  in_=wide[g // 2][:, g % 2, :, first:first + width].rearrange("p t (c i) -> p c t i", i=4))
 
+        w_bank = {}
+
+        def interleave_tensor(g, b):
+            w_bank[g, b] = sum_psum.tile([P, 2 * P, 4], BF16, name="w_bank", tag="sum")
+            for j in range(2):
+                nc.tensor.matmul(w_bank[g, b][:, rows(j), :], lhsT=ident_bf[:],
+                                 rhs=wide[g // 2][:, g % 2, :, rows(2 * b + j)].rearrange("p t v -> p v t"), start=True, stop=True)
+
+        def copy_w(g, b):
+            if g not in w_grouped:
+                w_grouped[g] = wide_pool.tile([P, N, 4], BF16, name="w_grouped", align_bytes=256)
+            nc.scalar.copy(out=w_grouped[g][:, 2 * P * b:2 * P * (b + 1), :].rearrange("p v t -> p (v t)"),
+                           in_=w_bank[g, b][:].rearrange("p v t -> p (v t)"))
+
         def quantise_w(g):
             nc.vector.quantize_mx(out=w_codes[g][:].bitcast(E4M3_X4), scales=w_codes_scale[g][:],
                                   in_=w_grouped[g][:].rearrange("p v t -> p (v t)"))
@@ -230,6 +244,12 @@ def tile_cross_entropy_hidden_gradient_s3_kernel(
 
         def close_logits(m, g):
             logits(m, g, ("outlier",), opens=False)
+
+        def open_outlier(m, g):
+            logits(m, g, ("outlier",), closes=False)
+
+        def close_rest(m, g):
+            logits(m, g, ("rest0", "rest1"), opens=False)
 
         def exponential(m, g):
             nc.scalar.activation(out=stored(soft[m, g // 2][:], g % 2 * P, (g % 2 + 1) * P), in_=word_order(z_bank[m, g][:]),
@@ -323,63 +343,39 @@ def tile_cross_entropy_hidden_gradient_s3_kernel(
 
         load_w(0)
         load(w_scale[:], w_out_scale.rearrange("(p t) o -> p (t o)", t=4))
-        load_w(1)
         load(vs_rows[0:VS_ROWS, :], vocab_scale.rearrange("(r c) -> r c", c=P))
-        load_rest(0)
+        load_w(1)
         load_outlier(0)
+        load_rest(0)
         load_rest(1)
+        load_outlier(1)
+        load_rest(2)
         load_wr_scales(0)
         load_wr(0)
         load(norm[:], log_norm.rearrange("(p m) -> p m", m=M_TILES))
         load_w(2)
-        load_rest(2)
-        load_outlier(1)
         load_wr(1)
         load_w(3)
+        load_rest(3)
         load_wr_scales(1)
         load_wr(2)
-        load_target_half(0, 0)
-        load_rest(3)
         load_wr(3)
+        load_target_half(0, 0)
         load_target_half(0, 1)
         load_target(1)
-
-        widen_vector(0, 0)
-        widen_scalar(1, 0)
-        widen_vector(0, 1)
-        widen_scalar(1, 1)
-        widen_vector(0, 2)
-        widen_vector(0, 3)
-        widen_vector(1, 2)
-        widen_scalar(1, 3)
         warm_up(zeros)
-        warm_up()
-        warm_up()
         spread_vs(0)
         spread_vs(1)
-        transpose_h("rest", 0)
-        spread_vs(2)
+        warm_up()
+        warm_up()
         transpose_h("outlier", 0)
-        spread_vs(3)
+        widen_scalar(1, 0)
+        widen_vector(0, 0)
+        transpose_h("rest", 0)
+        widen_scalar(1, 1)
+        widen_vector(0, 1)
+        spread_vs(2)
         transpose_h("rest", 1, pool=sum_psum, tag="sum")
-        warm_up()
-        warm_up()
-        interleave(0, scalar, 0, P)
-        interleave(0, vector, P, 3 * P)
-        interleave(1, vector, P, P)
-        copy_h(scalar, "rest", 0)
-        copy_h(scalar, "outlier", 0)
-        copy_h(scalar, "rest", 1)
-        negate_norm()
-        quantise_w(0)
-        quantise_h("rest", 0)
-        quantise_h("outlier", 0)
-        interleave(1, vector, 2 * P, P)
-        quantise_h("rest", 1)
-        logits(0, 0)
-        logits(1, 0, ("outlier", "rest0", "rest1"))
-        transpose_h("rest", 2)
-        transpose_h("outlier", 1)
         wt_scale = keep.tile([P, V_GROUPS, HIDDEN], U8, name="wt_scale", tag="shared", align_bytes=256)
         load_scales(wt_scale, wt_scales)
         load_target_half(2, 0)
@@ -387,120 +383,170 @@ def tile_cross_entropy_hidden_gradient_s3_kernel(
         load_target_half(2, 1)
         load_wt(1)
         load_target(3)
-        interleave(1, scalar, 0, P)
-        interleave(1, vector, 3 * P, P)
-        widen_scalar(2, 3)
-        widen_scalar(2, 2)
-        widen_vector(2, 0)
-        widen_vector(2, 1)
-        quantise_w(1)
-        exponential(0, 0)
-        copy_h(scalar, "rest", 2)
+        widen_scalar(1, 3)
+        widen_vector(0, 2)
+        transpose_h("outlier", 1, pool=sum_psum, tag="sum")
+        widen_vector(0, 3)
+        spread_vs(3)
+        interleave(0, scalar, 0, P)
+        widen_vector(1, 2)
+        copy_h(scalar, "outlier", 0)
+        interleave(0, vector, P, 3 * P)
+        transpose_h("rest", 2)
+        copy_h(scalar, "rest", 0)
+        interleave(1, vector, 0, P)
+        copy_h(scalar, "rest", 1)
+        quantise_w(0)
         copy_h(scalar, "outlier", 1)
-        exponential(1, 0)
-        interleave(2)
-        quantise_h("rest", 2)
-        widen_vector(3, 0)
+        quantise_h("outlier", 0)
+        open_outlier(0, 0)
+        copy_h(scalar, "rest", 2)
+        quantise_h("rest", 0)
+        open_outlier(1, 0)
+        negate_norm()
+        interleave(1, vector, P, P)
+        close_rest(0, 0)
+        interleave(1, scalar, 3 * P, P)
+        quantise_h("rest", 1)
+        close_rest(1, 0)
+        widen_scalar(2, 3)
+        interleave(1, vector, 2 * P, P)
+        exponential(0, 0)
         quantise_h("outlier", 1)
-        open_logits(0, 1)
-        open_logits(1, 1)
-        close_logits(0, 1)
-        close_logits(1, 1)
-        logits(2, 0)
-        logits(2, 1)
-        exponential(0, 1)
+        exponential(1, 0)
+        quantise_h("rest", 2)
+        logits(2, 0, ("outlier", "rest0", "rest1"))
         widen_scalar(3, 3)
+        widen_vector(2, 0)
+        exponential(2, 0)
+        quantise_w(1)
+        logits(0, 1)
+        widen_scalar(3, 2)
+        widen_vector(2, 1)
+        logits(1, 1)
+        exponential(0, 1)
+        widen_vector(2, 2)
+        logits(2, 1)
         exponential(1, 1)
+        widen_vector(3, 0)
+        transpose_h("rest", 3)
+        exponential(2, 1)
+        interleave(2, vector)
+        copy_h(scalar, "rest", 3)
         widen_vector(3, 1)
         quantise_w(2)
-        widen_vector(3, 2)
-        subtract(0, 0, 0, P)
-        exponential(2, 0)
-        exponential(2, 1)
-        open_logits(0, 2)
-        transpose_h("rest", 3)
-        close_logits(0, 2)
-        logits(1, 2)
-        copy_h(scalar, "rest", 3)
+        logits(0, 2)
         exponential(0, 2)
-        interleave(3)
-        subtract(0, 0, P, WORDS)
+        interleave(3, vector)
+        logits(1, 2)
         exponential(1, 2)
-        quantise_w(3)
-        quantise_h("rest", 3)
-        subtract(0, 1, 0, P, into=spare[0])
-        subtract(1, 0, 0, SPLIT, into=soft[0, 1])
-        logits(0, 3)
+        subtract(0, 0, 0, P)
         logits(2, 2)
-        exponential(0, 3)
-        order_target(1, SPLIT, WORDS)
         exponential(2, 2)
+        quantise_w(3)
+        logits(0, 3)
+        exponential(0, 3)
+        subtract(0, 1, 0, P, into=spare[0])
         logits(1, 3)
+        order_target(1, SPLIT, WORDS)
+        quantise_h("rest", 3)
         logits(2, 3)
         exponential(1, 3)
+        subtract(0, 0, P, WORDS)
+        logits(3, 0)
         exponential(2, 3)
-        order_target(2, SPLIT, WORDS - LAST)
+        subtract(1, 0, 0, SPLIT, into=soft[0, 1])
+        logits(3, 1)
+        order_target(2, SPLIT, WORDS)
+        subtract(1, 1, 0, SPLIT, into=spare[1])
+        exponential(3, 0)
         subtract(0, 1, P, WORDS, into=spare[0])
         subtract_aside(1, soft[0, 1])
         multiply(0, 0)
+        transpose_e(0, 0)
+        copy_e(scalar, 0, 0)
         multiply(0, 1)
-        logits(3, 0)
-        logits(3, 1)
-        exponential(3, 0)
-        for m in range(M_TILES):
-            transpose_e(m, 0)
-            transpose_e(m, 1)
-            (split_copy if m == 3 else copy_e)(scalar, m, 0)
-            if m < 2:
-                order_target(m + 2, WORDS - LAST, WORDS)
-            copy_e(scalar, m, 1)
-            if m == 0:
-                exponential(3, 1)
-                logits(3, 2)
-                logits(3, 3)
-                exponential(3, 2)
-                exponential(3, 3)
-                order_target(3, SPLIT, WORDS - LAST)
-            elif m < 3:
-                quantise_e(m - 1, 2, 2)
-                for d in range(D_GROUPS):
-                    product(m - 1, d * N, groups=range(2, 4))
-                    store(scalar, m - 1, d * N)
-            else:
-                store(vector, 2, 0)
-                for d in range(1, D_GROUPS):
-                    product(2, d * N, groups=range(2, 4))
-                    store(scalar, 2, d * N)
-            if m == 0:
-                subtract(1, 1, 0, P, into=spare[1])
-                subtract(2, 0, 0, SPLIT, into=soft[1, 1])
-                subtract(1, 1, P, WORDS, into=spare[1])
-            if m == 2:
-                subtract(3, 0, 0, SPLIT, into=soft[2, 1])
-            if m in (1, 2):
-                subtract(m + 1, 1, into=spare[(m + 1) % 2])
-            if m == 3:
-                break
-            quantise_e(m, 0, 2)
-            if m < 2:
-                subtract_aside(m + 2, soft[m + 1, 1])
-            multiply(m + 1, 0)
-            if m == 2:
-                quantise_e(2, 2, 2)
-            multiply(m + 1, 1)
-            for d in range(D_GROUPS):
-                product(m, d * N, groups=range(2))
-            if m == 2:
-                product(2, 0, groups=range(2, 4))
+        logits(3, 2)
+        exponential(3, 1)
+        subtract(1, 1, SPLIT, 160, into=spare[1])
+        transpose_e(0, 1)
+        copy_e(scalar, 0, 1)
+        subtract(2, 0, 0, SPLIT, into=soft[1, 1])
+        logits(3, 3)
+        exponential(3, 2)
+        quantise_e(0, 0, 2)
+        product(0, 0 * N, groups=range(2))
+        exponential(3, 3)
+        subtract(1, 1, 160, WORDS, into=spare[1])
+        subtract_aside(2, soft[1, 1])
+        product(0, 1 * N, groups=range(2))
+        order_target(3, SPLIT, WORDS - LAST)
+        multiply(1, 0)
+        product(0, 2 * N, groups=range(2))
+        multiply(1, 1)
+        transpose_e(1, 0)
+        copy_e(scalar, 1, 0)
+        quantise_e(0, 2, 2)
+        transpose_e(1, 1)
+        order_target(3, WORDS - LAST, WORDS)
+        subtract(2, 1, into=spare[0])
+        subtract_aside(3, soft[2, 1])
+        product(0, 0 * N, groups=range(2, 4))
+        copy_e(scalar, 1, 1)
+        quantise_e(1, 0, 2)
+        product(0, 1 * N, groups=range(2, 4))
+        store(scalar, 0, 0 * N)
+        multiply(2, 0)
+        product(0, 2 * N, groups=range(2, 4))
+        store(scalar, 0, 1 * N)
+        multiply(2, 1)
+        product(1, 0 * N, groups=range(2))
+        store(scalar, 0, 2 * N)
+        quantise_e(1, 2, 2)
+        product(1, 1 * N, groups=range(2))
+        subtract(3, 0, 0, SPLIT, into=soft[2, 1])
+        product(1, 2 * N, groups=range(2))
+        subtract(3, 1, into=spare[1])
+        transpose_e(2, 0)
+        copy_e(scalar, 2, 0)
+        quantise_e(2, 0, 2)
+        transpose_e(2, 1)
+        copy_e(scalar, 2, 1)
+        multiply(3, 0)
+        product(1, 0 * N, groups=range(2, 4))
+        store(scalar, 1, 0 * N)
+        quantise_e(2, 2, 2)
+        product(1, 1 * N, groups=range(2, 4))
+        store(scalar, 1, 1 * N)
+        multiply(3, 1)
+        product(1, 2 * N, groups=range(2, 4))
+        store(scalar, 1, 2 * N)
+        product(2, 0 * N, groups=range(2))
+        product(2, 1 * N, groups=range(2))
+        product(2, 2 * N, groups=range(2))
+        product(2, 0 * N, groups=range(2, 4))
+        store(vector, 2, 0 * N)
+        transpose_e(3, 0)
+        split_copy(scalar, 3, 0)
         quantise_e(3, 0, 1)
+        transpose_e(3, 1)
+        split_copy(scalar, 3, 1)
         quantise_e(3, 1, 1)
-        quantise_e(3, 2, 2)
-        product(3, 0, groups=range(2))
+        product(2, 1 * N, groups=range(2, 4))
+        store(scalar, 2, 1 * N)
+        quantise_e(3, 2, 1)
+        product(2, 2 * N, groups=range(2, 4))
+        store(scalar, 2, 2 * N)
+        quantise_e(3, 3, 1)
+        product(3, 0 * N, groups=range(2))
         product(3, N, 2 * P, groups=range(2))
-        product(3, 0, groups=range(2, 4))
-        store(vector, 3, 0)
+        product(3, 0 * N, groups=range(2, 4))
+        store(vector, 3, 0 * N)
         product(3, N, 2 * P, groups=range(2, 4))
         store(scalar, 3, N, 2 * P)
-        for i in range(1, 4):
-            product(3, N + i * 2 * P, 2 * P)
-            store(vector if i % 2 == 0 else scalar, 3, N + i * 2 * P, 2 * P)
+        product(3, N + 2 * P, 2 * P)
+        store(scalar, 3, N + 2 * P, 2 * P)
+        product(3, 2 * N, 2 * P)
+        store(vector, 3, 2 * N, 2 * P)
+        product(3, 2 * N + 2 * P, 2 * P)
+        store(scalar, 3, 2 * N + 2 * P, 2 * P)

@@ -423,7 +423,7 @@ def tile_cross_entropy_hidden_gradient_s3_kernel(
         logits(0, 1)
         widen_scalar(3, 2)
         widen_vector(2, 1)
-        logits(1, 1)
+        logits(1, 1, ("outlier", "rest0", "rest1"))
         exponential(0, 1)
         widen_vector(2, 2)
         logits(2, 1)
@@ -438,7 +438,7 @@ def tile_cross_entropy_hidden_gradient_s3_kernel(
         logits(0, 2)
         exponential(0, 2)
         interleave(3, vector)
-        logits(1, 2)
+        logits(1, 2, ("outlier", "rest0", "rest1"))
         exponential(1, 2)
         subtract(0, 0, 0, P)
         logits(2, 2)
@@ -447,13 +447,13 @@ def tile_cross_entropy_hidden_gradient_s3_kernel(
         logits(0, 3)
         exponential(0, 3)
         subtract(0, 1, 0, P, into=spare[0])
-        logits(1, 3)
+        logits(1, 3, ("outlier", "rest0", "rest1"))
         order_target(1, SPLIT, WORDS)
         quantise_h("rest", 3)
         logits(2, 3)
         exponential(1, 3)
         subtract(0, 0, P, WORDS)
-        logits(3, 0)
+        logits(3, 0, ("outlier", "rest0", "rest1"))
         exponential(2, 3)
         subtract(1, 0, 0, SPLIT, into=soft[0, 1])
         logits(3, 1)

from contextlib import ExitStack

import concourse.mybir as mybir
from concourse.masks import make_identity

TOKENS, OUT_CH, REST_CH, HIDDEN, VOCAB = 512, 512, 1024, 1536, 2048
FLOPS = 2 * TOKENS * (OUT_CH + REST_CH) * VOCAB + 2 * TOKENS * VOCAB * HIDDEN

F32 = mybir.dt.float32
BF16 = mybir.dt.bfloat16
I32 = mybir.dt.int32
U32 = mybir.dt.uint32
U8 = mybir.dt.uint8
E4M3FN = mybir.dt.float8_e4m3fn
E4M3_X4 = mybir.dt.float8_e4m3fn_x4
E2M1_X4 = mybir.dt.float4_e2m1fn_x4
MULT = mybir.AluOpType.mult
SUBTRACT = mybir.AluOpType.subtract
EXP = mybir.ActivationFunctionType.Exp
COPY = mybir.ActivationFunctionType.Copy

P = 128
N = 512
M_TILES = TOKENS // P
V_GROUPS = VOCAB // N
D_GROUPS = HIDDEN // N
VS_ROWS = VOCAB // P
HALF = 2 * N
SPLIT = 64
W_LOADS = [(0, 2, 0, 2), (0, 2, 2, 2), (2, 1, 0, 4), (3, 1, 0, 4)]
WR_LOADS = {0: 1, 1: 1, 2: 1, 3: 1}
WORDS = HALF // 4


def tile_cross_entropy_hidden_gradient_s3_kernel(
    tc, h_out, h_rest, w_out_bytes, w_out_scale, w_rest_words, w_rest_scales,
    log_norm, targets, vocab_scale, wt_words, wt_scales, out
):
    nc = tc.nc
    with ExitStack() as ctx:
        keep = ctx.enter_context(tc.tile_pool(name="keep", bufs=1))
        wide_pool = ctx.enter_context(tc.tile_pool(name="wide_pool", bufs=2))
        grad_pool = ctx.enter_context(tc.tile_pool(name="grad_pool", bufs=3))
        store_pool = ctx.enter_context(tc.tile_pool(name="store_pool", bufs=8))
        sum_psum = ctx.enter_context(tc.psum_pool(name="sum_psum", bufs=4))
        t_psum = ctx.enter_context(tc.psum_pool(name="t_psum", bufs=2))
        vs_psum = ctx.enter_context(tc.psum_pool(name="vs_psum", bufs=1))
        ctx.enter_context(tc.manual_schedule())

        def kept(shape, dtype, name):
            return keep.tile(shape, dtype, name=name, align_bytes=256)

        def rows(m):
            return slice(m * P, (m + 1) * P)

        def cols(g, count=1):
            return slice(g * N, (g + count) * N)

        wr_scale = [kept([P, 2, HALF], U8, "wr_scale%d" % i) for i in range(2)]
        vs_rows = kept([P, P], BF16, "vs_rows")
        ident = kept([P, P], F32, "ident")
        ident_bf = kept([P, P], BF16, "ident_bf")
        zeros = kept([P, P], F32, "zeros")
        nc.vector.memset(zeros[:], 0.0)
        make_identity(nc, ident[:])
        nc.vector.memset(vs_rows[:], 0.0)
        nc.scalar.copy(out=ident_bf[:], in_=ident[:])
        for plane in wr_scale:
            nc.vector.memset(plane[:].bitcast(I32), 0)

        norm = kept([P, M_TILES], BF16, "norm")
        w_scale = kept([P, 4], F32, "w_scale")
        w_bytes = {load: kept([P, load[3], N * load[1]], U8, "w_bytes%d%d" % (load[0], load[2])) for load in W_LOADS}
        wr = {g: kept([P, 2, 2 * N * count], U8, "wr%d" % g) for g, count in WR_LOADS.items()}
        h_first = keep.tile([P, 3 * REST_CH], BF16, name="h_first", tag="shared", align_bytes=256)
        rest = [h_first[:, 0:REST_CH], h_first[:, REST_CH:2 * REST_CH]]
        rest = rest + [kept([P, REST_CH], BF16, "rest%d" % m)[:] for m in range(2, M_TILES)]
        outlier = [h_first[:, 2 * REST_CH:3 * REST_CH], kept([P, 2 * OUT_CH], BF16, "outlier1")[:]]
        target = {(m, half): kept([P, HALF], BF16, "target%d%d" % (m, half)) for m in (0, 2) for half in range(2)}
        for m in (1, 3):
            whole = kept([P, VOCAB], BF16, "target%d" % m)
            target["whole", m] = whole
            for half in range(2):
                target[m, half] = whole[:, half * HALF:(half + 1) * HALF]
        wt = [kept([P, 2, 2 * HIDDEN], U8, "wt%d" % i) for i in range(2)]

        w_view = w_out_bytes.rearrange("(p t) v -> p t v", t=4)
        wr_view = w_rest_words.rearrange("g p n -> p g n")
        rest_view = h_rest.rearrange("(p m) k -> p m k", m=M_TILES)
        outlier_view = h_out.rearrange("(p i m) k -> p i (m k)", i=2, m=2)
        target_view = targets.rearrange("(p m) v -> p m v", m=M_TILES)
        out_view = out.rearrange("(p m) d -> p m d", m=M_TILES)

        def load(tile, source):
            nc.sync.dma_start(out=tile, in_=source)

        def load_scales(plane, source):
            for r in range(4):
                load(plane[r:P:32].bitcast(I32), source[:, r:16:4, :].bitcast(I32).rearrange("g q n -> q g n"))

        def load_w(i):
            g, groups, t, planes = W_LOADS[i]
            load(w_bytes[W_LOADS[i]][:], w_view[:, t:t + planes, cols(g, groups)])

        def load_wr(g):
            load(wr[g][:], wr_view[:, :, cols(2 * g, 2 * WR_LOADS[g])])

        def load_wr_scales(half):
            load_scales(wr_scale[half], w_rest_scales[:, :, cols(2 * half, 2)])

        def load_rest(m):
            load(rest[m][:], rest_view[:, m, :])

        def load_outlier(i):
            load(outlier[i][:], outlier_view[:, i, :])

        def load_target_half(m, half):
            load(target[m, half][:], target_view[:, m, cols(2 * half, 2)])

        def load_target(m):
            load(target["whole", m][:], target_view[:, m, :])

        def load_wt(i):
            load(wt[i][:], wt_words[2 * i:2 * i + 2].rearrange("g p n -> p g n"))

        w_grouped = {}
        w_codes = [kept([P, N], U32, "w_codes%d" % g) for g in range(V_GROUPS)]
        w_codes_scale = [kept([P, N], U8, "w_codes_scale%d" % g) for g in range(V_GROUPS)]

        wide = [kept([P, 2, 4, N], BF16, "wide%d" % half) for half in range(2)]

        def w_plane(g, t, count=1):
            load = [x for x in W_LOADS if x[0] <= g < x[0] + x[1] and x[2] <= t < x[2] + x[3]][0]
            return w_bytes[load][:, t - load[2], cols(g - load[0], count)].bitcast(E4M3FN)

        def widen_vector(g, t, count=1):
            nc.vector.tensor_scalar(out=wide[g // 2][:, g % 2:g % 2 + count, t, :],
                                    in0=w_plane(g, t, count).rearrange("p (j v) -> p j v", j=count),
                                    scalar1=w_scale[:, t:t + 1], scalar2=None, op0=MULT)

        def widen_scalar(g, t):
            nc.scalar.activation(out=wide[g // 2][:, g % 2, t, :], in_=w_plane(g, t), func=COPY,
                                 scale=w_scale[:, t:t + 1])

        def interleave(g, copy=nc.vector.tensor_copy, first=0, width=N):
            if g not in w_grouped:
                w_grouped[g] = wide_pool.tile([P, N, 4], BF16, name="w_grouped", align_bytes=256)
            copy(out=w_grouped[g][:, first:first + width].rearrange("p (c i) t -> p c t i", i=4),
                 in_=wide[g // 2][:, g % 2, :, first:first + width].rearrange("p t (c i) -> p c t i", i=4))

        w_bank = {}

        def interleave_tensor(g, b):
            w_bank[g, b] = sum_psum.tile([P, 2 * P, 4], BF16, name="w_bank", tag="sum")
            for j in range(2):
                nc.tensor.matmul(w_bank[g, b][:, rows(j), :], lhsT=ident_bf[:],
                                 rhs=wide[g // 2][:, g % 2, :, rows(2 * b + j)].rearrange("p t v -> p v t"), start=True, stop=True)

        def copy_w(g, b):
            if g not in w_grouped:
                w_grouped[g] = wide_pool.tile([P, N, 4], BF16, name="w_grouped", align_bytes=256)
            nc.scalar.copy(out=w_grouped[g][:, 2 * P * b:2 * P * (b + 1), :].rearrange("p v t -> p (v t)"),
                           in_=w_bank[g, b][:].rearrange("p v t -> p (v t)"))

        def quantise_w(g):
            nc.vector.quantize_mx(out=w_codes[g][:].bitcast(E4M3_X4), scales=w_codes_scale[g][:],
                                  in_=w_grouped[g][:].rearrange("p v t -> p (v t)"))

        h_source = {}
        for m in range(M_TILES):
            h_source["rest", m] = rest[m]
        for i in range(2):
            h_source["outlier", i] = outlier[i]
        h_grouped, h_codes, h_scale, h_bank = {}, {}, {}, {}
        for kind, i in h_source:
            h_grouped[kind, i] = keep.tile([P, 2, P, 4], BF16, name="h_grouped_%s%d" % (kind, i), tag="grouped_%s%d" % (kind, i),
                                           align_bytes=256)
            h_codes[kind, i] = kept([P, 2, P], U32, "h_codes_%s%d" % (kind, i))
            h_scale[kind, i] = kept([P, 2, P], U8, "h_scale_%s%d" % (kind, i))

        def transpose_h(*pair, pool=t_psum, tag="t"):
            bank = pool.tile([P, 4, P], F32, name="t_bank", tag=tag)
            h_bank[pair] = bank
            words = h_source[pair][:].bitcast(F32)
            for j in range(2):
                for u in range(2):
                    nc.tensor.transpose(bank[:, 2 * j + u, :], words[:, 2 * P * j + u:2 * P * (j + 1):2], ident[:])

        def copy_h(copy, *pair):
            copy(out=h_grouped[pair][:].bitcast(F32), in_=h_bank[pair][:].rearrange("p (j u) r -> p j r u", u=2))

        def quantise_h(*pair):
            nc.vector.quantize_mx(out=h_codes[pair][:].rearrange("p j r -> p (j r)").bitcast(E4M3_X4),
                                  scales=h_scale[pair][:].rearrange("p j r -> p (j r)"),
                                  in_=h_grouped[pair][:].rearrange("p j r t -> p (j r t)"))

        minus_norm = kept([P, M_TILES], F32, "minus_norm")
        vs_bank = [vs_psum.tile([P, HALF], BF16, name="vs_bank%d" % half) for half in range(2)]

        def word_order(natural):
            return natural.rearrange("q (w u e) -> q u w e", u=2, e=2)

        def stored(half_tile, first, last):
            return half_tile.rearrange("q (u w e) -> q u w e", u=2, e=2)[:, :, first:last, :]

        def negate_norm():
            nc.scalar.activation(out=minus_norm[:], in_=norm[:], func=COPY, scale=-1.0)

        def spread_vs(g):
            for r in range(4):
                row = 4 * g + r
                runs = vs_bank[g // 2][:].rearrange("q (u r c) -> q u r c", u=2, r=8)
                nc.tensor.matmul(runs[:, :, row % 8, :], lhsT=ident_bf[:, row:row + 1].to_broadcast([P, P]),
                                 rhs=word_order(vs_rows[:]), start=True, stop=True)

        warm_bank = sum_psum.tile([P, N], F32, name="warm_bank", tag="sum")

        def warm_up(operand=ident_bf):
            nc.tensor.matmul(warm_bank[:].rearrange("p (a c) -> p a c", a=4), lhsT=operand[:],
                             rhs=operand[:].unsqueeze(1).to_broadcast([P, 4, P]), start=True, stop=True)

        z_bank, grad, moved = {}, {}, {}
        soft = {(m, half): kept([P, HALF], F32, "soft%d%d" % (m, half)) for m in range(M_TILES) for half in range(2)}

        def logits(m, g, passes=("rest0", "rest1", "outlier"), opens=True, closes=True):
            if opens:
                z_bank[m, g] = sum_psum.tile([P, N], F32, name="z_bank", tag="sum")
            for name in passes:
                if name == "outlier":
                    pair, j = ("outlier", m // 2), m % 2
                    moving, moving_scale = w_codes[g][:].bitcast(E4M3_X4), w_codes_scale[g][:]
                else:
                    pair, j = ("rest", m), int(name[-1])
                    first = max(f for f in WR_LOADS if f <= g)
                    moving = wr[first][:, j, cols(2 * (g - first), 2)].bitcast(E2M1_X4)
                    moving_scale = wr_scale[g // 2][:, j, cols(g % 2)]
                nc.tensor.matmul_mx(
                    out=z_bank[m, g][:], lhsT=h_codes[pair][:, j, :].bitcast(E4M3_X4), lhsT_scale=h_scale[pair][:, j, :],
                    rhs=moving, rhs_scale=moving_scale,
                    start=(opens and name == passes[0]), stop=(closes and name == passes[-1]))

        def open_logits(m, g):
            logits(m, g, ("rest0", "rest1"), closes=False)

        def close_logits(m, g):
            logits(m, g, ("outlier",), opens=False)

        def open_outlier(m, g):
            logits(m, g, ("outlier",), closes=False)

        def close_rest(m, g):
            logits(m, g, ("rest0", "rest1"), opens=False)

        def exponential(m, g):
            nc.scalar.activation(out=stored(soft[m, g // 2][:], g % 2 * P, (g % 2 + 1) * P), in_=word_order(z_bank[m, g][:]),
                                 func=EXP, bias=minus_norm[:, m:m + 1])

        def subtract(m, half, first=0, last=WORDS, engine=nc.vector, into=None):
            if into is not None:
                for word in range(first, last, 32):
                    moved[m, half, word] = into
            engine.tensor_tensor(out=stored(soft[m, half][:] if into is None else into[:], first, last),
                                 in0=stored(soft[m, half][:], first, last),
                                 in1=word_order(target[m, half][:, 4 * first:4 * last]), op=SUBTRACT)

        def multiply(m, half, first=0, last=WORDS):
            if m not in grad:
                grad[m] = grad_pool.tile([P, VOCAB], BF16, name="grad", align_bytes=256)
            nc.vector.tensor_tensor(out=stored(grad[m][:, cols(2 * half, 2)], first, last),
                                    in0=stored(moved.get((m, half, first), soft[m, half])[:], first, last),
                                    in1=stored(vs_bank[half][:], first, last), op=MULT)

        g_grouped = {}
        g_codes = [kept([P, V_GROUPS, P], U32, "g_codes%d" % m) for m in range(M_TILES)]
        g_scale = [kept([P, V_GROUPS, P], U8, "g_scale%d" % m) for m in range(M_TILES)]
        g_bank = {}

        def transpose_e(m, half):
            bank = t_psum.tile([P, 4, P], F32, name="t_bank", tag="t")
            g_bank[m, half] = bank
            words = grad[m][:].bitcast(F32)
            for j in range(2):
                for u in range(2):
                    nc.tensor.transpose(bank[:, 2 * j + u, :], words[:, rows(4 * half + 2 * u + j)], ident[:])

        def grouped(m, half):
            if (m, half) not in g_grouped:
                g_grouped[m, half] = keep.tile([P, 2, P, 4], BF16, name="g_grouped", tag="grouped_%d%d" % (m % 2, half),
                                               align_bytes=256)
            return g_grouped[m, half]

        def copy_e(copy, m, half):
            copy(out=grouped(m, half)[:].bitcast(F32), in_=g_bank[m, half][:].rearrange("p (g u) r -> p g r u", u=2))

        def split_copy(copy, m, half):
            for j in range(2):
                copy(out=grouped(m, half)[:, j].bitcast(F32), in_=g_bank[m, half][:, 2 * j:2 * j + 2, :].rearrange("p u r -> p r u"))

        def quantise_e(m, g, count):
            groups = slice(g, g + count)
            nc.vector.quantize_mx(out=g_codes[m][:, groups].rearrange("p g r -> p (g r)").bitcast(E4M3_X4),
                                  scales=g_scale[m][:, groups].rearrange("p g r -> p (g r)"),
                                  in_=grouped(m, g // 2)[:, g % 2:g % 2 + count].rearrange("p g r t -> p (g r t)"))

        o_bank = {}

        def product(m, first, width=N, groups=range(V_GROUPS)):
            if (m, first) not in o_bank:
                o_bank[m, first] = sum_psum.tile([P, N], F32, name="o_bank", tag="sum")
            for g in groups:
                nc.tensor.matmul_mx(
                    out=o_bank[m, first][:, 0:width],
                    lhsT=g_codes[m][:, g, :].bitcast(E4M3_X4), lhsT_scale=g_scale[m][:, g, :],
                    rhs=wt[g // 2][:, g % 2, 2 * first:2 * (first + width)].bitcast(E2M1_X4),
                    rhs_scale=wt_scale[:, g, first:first + width],
                    start=(g == 0), stop=(g == V_GROUPS - 1))

        def store(copy, m, first, width=N):
            result = store_pool.tile([P, N], F32, name="result")
            copy(out=result[:, 0:width], in_=o_bank[m, first][:, 0:width])
            nc.sync.dma_start(out=out_view[:, m, first:first + width], in_=result[:, 0:width])

        scalar, vector = nc.scalar.copy, nc.vector.tensor_copy

        LAST = 32
        side = {}
        target_words = {m: kept([P, 2, WORDS], F32, "target_words%d" % m) for m in range(1, M_TILES)}


        spare = [kept([P, HALF], F32, "spare%d" % i) for i in range(2)]


        def order_target(m, first=0, last=WORDS):
            nc.scalar.copy(out=target_words[m][:, :, first:last],
                           in_=target[m, 0][:, 4 * first:4 * last].bitcast(F32).rearrange("q (w u) -> q u w", u=2))


        def subtract_aside(m, buffer):
            moved[m, 0, 0] = buffer
            runs = [tile[:].rearrange("q (u c) -> q u c", u=2)[:, :, 2 * SPLIT:] for tile in (buffer, soft[m, 0])]
            nc.gpsimd.tensor_tensor(out=runs[0], in0=runs[1], in1=target_words[m][:, :, SPLIT:].bitcast(BF16), op=SUBTRACT)


        load_w(0)
        load(w_scale[:], w_out_scale.rearrange("(p t) o -> p (t o)", t=4))
        load(vs_rows[0:VS_ROWS, :], vocab_scale.rearrange("(r c) -> r c", c=P))
        load_w(1)
        load_outlier(0)
        load_rest(0)
        load_rest(1)
        load_outlier(1)
        load_rest(2)
        load_wr_scales(0)
        load_wr(0)
        load(norm[:], log_norm.rearrange("(p m) -> p m", m=M_TILES))
        load_w(2)
        load_wr(1)
        load_w(3)
        load_rest(3)
        load_wr_scales(1)
        load_wr(2)
        load_wr(3)
        load_target_half(0, 0)
        load_target_half(0, 1)
        load_target(1)
        warm_up(zeros)
        spread_vs(0)
        spread_vs(1)
        warm_up()
        warm_up()
        transpose_h("outlier", 0)
        widen_scalar(1, 0)
        widen_vector(0, 0)
        transpose_h("rest", 0)
        widen_scalar(1, 1)
        widen_vector(0, 1)
        spread_vs(2)
        transpose_h("rest", 1, pool=sum_psum, tag="sum")
        wt_scale = keep.tile([P, V_GROUPS, HIDDEN], U8, name="wt_scale", tag="shared", align_bytes=256)
        load_scales(wt_scale, wt_scales)
        load_target_half(2, 0)
        load_wt(0)
        load_target_half(2, 1)
        load_wt(1)
        load_target(3)
        widen_scalar(1, 3)
        widen_vector(0, 2)
        transpose_h("outlier", 1, pool=sum_psum, tag="sum")
        widen_vector(0, 3)
        spread_vs(3)
        interleave(0, scalar, 0, P)
        widen_vector(1, 2)
        copy_h(scalar, "outlier", 0)
        interleave(0, vector, P, 3 * P)
        transpose_h("rest", 2)
        copy_h(scalar, "rest", 0)
        interleave(1, vector, 0, P)
        copy_h(scalar, "rest", 1)
        quantise_w(0)
        copy_h(scalar, "outlier", 1)
        quantise_h("outlier", 0)
        open_outlier(0, 0)
        copy_h(scalar, "rest", 2)
        quantise_h("rest", 0)
        open_outlier(1, 0)
        negate_norm()
        interleave(1, vector, P, P)
        close_rest(0, 0)
        interleave(1, scalar, 3 * P, P)
        quantise_h("rest", 1)
        close_rest(1, 0)
        widen_scalar(2, 3)
        interleave(1, vector, 2 * P, P)
        exponential(0, 0)
        quantise_h("outlier", 1)
        exponential(1, 0)
        quantise_h("rest", 2)
        logits(2, 0, ("outlier", "rest0", "rest1"))
        widen_scalar(3, 3)
        widen_vector(2, 0)
        exponential(2, 0)
        quantise_w(1)
        logits(0, 1)
        widen_scalar(3, 2)
        widen_vector(2, 1)
        logits(1, 1, ("outlier", "rest0", "rest1"))
        exponential(0, 1)
        widen_vector(2, 2)
        logits(2, 1)
        exponential(1, 1)
        widen_vector(3, 0)
        transpose_h("rest", 3)
        exponential(2, 1)
        interleave(2, vector)
        copy_h(scalar, "rest", 3)
        widen_vector(3, 1)
        quantise_w(2)
        logits(0, 2)
        exponential(0, 2)
        interleave(3, vector)
        logits(1, 2, ("outlier", "rest0", "rest1"))
        exponential(1, 2)
        subtract(0, 0, 0, P)
        logits(2, 2)
        exponential(2, 2)
        quantise_w(3)
        logits(0, 3)
        exponential(0, 3)
        subtract(0, 1, 0, P, into=spare[0])
        logits(1, 3, ("outlier", "rest0", "rest1"))
        order_target(1, SPLIT, WORDS)
        quantise_h("rest", 3)
        logits(2, 3)
        exponential(1, 3)
        subtract(0, 0, P, WORDS)
        logits(3, 0, ("outlier", "rest0", "rest1"))
        exponential(2, 3)
        subtract(1, 0, 0, SPLIT, into=soft[0, 1])
        logits(3, 1)
        order_target(2, SPLIT, WORDS)
        subtract(1, 1, 0, SPLIT, into=spare[1])
        exponential(3, 0)
        subtract(0, 1, P, WORDS, into=spare[0])
        subtract_aside(1, soft[0, 1])
        multiply(0, 0)
        transpose_e(0, 0)
        copy_e(scalar, 0, 0)
        multiply(0, 1)
        logits(3, 2)
        exponential(3, 1)
        subtract(1, 1, SPLIT, 160, into=spare[1])
        transpose_e(0, 1)
        copy_e(scalar, 0, 1)
        subtract(2, 0, 0, SPLIT, into=soft[1, 1])
        logits(3, 3)
        exponential(3, 2)
        quantise_e(0, 0, 2)
        product(0, 0 * N, groups=range(2))
        exponential(3, 3)
        subtract(1, 1, 160, WORDS, into=spare[1])
        subtract_aside(2, soft[1, 1])
        product(0, 1 * N, groups=range(2))
        order_target(3, SPLIT, WORDS - LAST)
        multiply(1, 0)
        product(0, 2 * N, groups=range(2))
        multiply(1, 1)
        transpose_e(1, 0)
        copy_e(scalar, 1, 0)
        quantise_e(0, 2, 2)
        transpose_e(1, 1)
        order_target(3, WORDS - LAST, WORDS)
        subtract(2, 1, into=spare[0])
        subtract_aside(3, soft[2, 1])
        product(0, 0 * N, groups=range(2, 4))
        copy_e(scalar, 1, 1)
        quantise_e(1, 0, 2)
        product(0, 1 * N, groups=range(2, 4))
        store(scalar, 0, 0 * N)
        multiply(2, 0)
        product(0, 2 * N, groups=range(2, 4))
        store(scalar, 0, 1 * N)
        multiply(2, 1)
        product(1, 0 * N, groups=range(2))
        store(scalar, 0, 2 * N)
        quantise_e(1, 2, 2)
        product(1, 1 * N, groups=range(2))
        subtract(3, 0, 0, SPLIT, into=soft[2, 1])
        product(1, 2 * N, groups=range(2))
        subtract(3, 1, into=spare[1])
        transpose_e(2, 0)
        copy_e(scalar, 2, 0)
        quantise_e(2, 0, 2)
        transpose_e(2, 1)
        copy_e(scalar, 2, 1)
        multiply(3, 0)
        product(1, 0 * N, groups=range(2, 4))
        store(scalar, 1, 0 * N)
        quantise_e(2, 2, 2)
        product(1, 1 * N, groups=range(2, 4))
        store(scalar, 1, 1 * N)
        multiply(3, 1)
        product(1, 2 * N, groups=range(2, 4))
        store(scalar, 1, 2 * N)
        product(2, 0 * N, groups=range(2))
        product(2, 1 * N, groups=range(2))
        product(2, 2 * N, groups=range(2))
        product(2, 0 * N, groups=range(2, 4))
        store(vector, 2, 0 * N)
        transpose_e(3, 0)
        split_copy(scalar, 3, 0)
        quantise_e(3, 0, 1)
        transpose_e(3, 1)
        split_copy(scalar, 3, 1)
        quantise_e(3, 1, 1)
        product(2, 1 * N, groups=range(2, 4))
        store(scalar, 2, 1 * N)
        quantise_e(3, 2, 1)
        product(2, 2 * N, groups=range(2, 4))
        store(scalar, 2, 2 * N)
        quantise_e(3, 3, 1)
        product(3, 0 * N, groups=range(2))
        product(3, N, 2 * P, groups=range(2))
        product(3, 0 * N, groups=range(2, 4))
        store(vector, 3, 0 * N)
        product(3, N, 2 * P, groups=range(2, 4))
        store(scalar, 3, N, 2 * P)
        product(3, N + 2 * P, 2 * P)
        store(scalar, 3, N + 2 * P, 2 * P)
        product(3, 2 * N, 2 * P)
        store(vector, 3, 2 * N, 2 * P)
        product(3, 2 * N + 2 * P, 2 * P)
        store(scalar, 3, 2 * N + 2 * P, 2 * P)
